import numpy as np, ml_dtypes
CORES = [1,14,19,24,37,42,55,60,65,78,83,88,101,106,119,124]
N = 16
T, KB = 2048, 64
CAPP = 256
def entries(a): return a.T.reshape(-1)
def pack(v, P): return np.ascontiguousarray(np.asarray(v, np.int32).reshape(-1, P).T)
def order(K):
    return np.argsort(K, kind="stable")
def most(K):
    o = order(K); return int(np.bincount(o // T * N + np.arange(N * T) // T, minlength=N * N).max())
def lists(rng, how):
    i, G = np.arange(N), T // CAPP
    if how == "uniform":
        for again in range(50):
            K = rng.integers(0, KB, (N, T))
            if most(K.reshape(-1)) <= CAPP: break
        else: K = np.broadcast_to(np.arange(T) % KB, (N, T)).copy()
    else:
        if how == "uneven":
            t = rng.integers(0, CAPP + 1, N)
            if t.sum() < T: t = CAPP - t
            t[0] = CAPP; w = np.diff(np.minimum(np.cumsum(t), T), prepend=0); L = w[(rng.permutation(N)[:, None] - rng.permutation(N)) % N]
        else:
            w = np.zeros(N, int); w[(G * (ord(how[-1]) - 97) + np.arange(G)) % N] = CAPP; L = w[(i[:, None] - i) % N]
        a = N - 1 - np.argmax(L[::-1] > 0, axis=0)
        m = np.minimum(rng.integers(1, CAPP, N - 1), L[a[:-1], i[1:]])
        v = np.nonzero((L[a[:-1], i[:-1]] == CAPP) & (L[a[:-1], i[1:]] == CAPP) & (a[:-1] != np.append(-1, a[:-2])))[0]
        if len(v): m[rng.choice(v)] = CAPP
        C = L.copy(); C[a[:-1], i[:-1]] += m; C[a[:-1], i[1:]] -= m
        kv = np.sort(rng.permutation(KB)[:N]); K = np.stack([rng.permutation(np.repeat(kv, c)) for c in C]); K[::3] = np.sort(K[::3], axis=1)
    return {"key": np.stack([pack(k, 16) for k in K])}
def setup_inputs(rng):
    return dict({"x": rng.standard_normal((N, 128, T), dtype=np.float32).astype(ml_dtypes.bfloat16)}, **lists(rng, "uniform"))
def setup_inputs_fulla(rng):
    d = setup_inputs(rng); d.update(lists(rng, "fulla"))
    for k in ("x",): d[k] = (d[k].astype(np.float32) * 1048576.0).astype(d[k].dtype)
    return d
def setup_inputs_fullb(rng):
    d = setup_inputs(rng); d.update(lists(rng, "fullb"))
    for k in ("x",): d[k] = (d[k].astype(np.float32) * (1 / 1024.0)).astype(d[k].dtype)
    return d
def setup_inputs_uneven(rng):
    d = setup_inputs(rng); d.update(lists(rng, "uneven"))
    return d
def check_inputs(x):
    bad = []
    if x["key"].min() < 0 or x["key"].max() >= KB: bad.append("key out of range")
    if most(np.concatenate([entries(a) for a in x["key"]])) > CAPP: bad.append("more than CAPP columns go from one rank to one rank")
    return bad
def reference(x, key):
    X = np.concatenate(list(x), axis=1); K = np.concatenate([entries(a) for a in key])
    Y = X[:, order(K)]
    return {"y": np.stack([Y[:, T * r:T * r + T] for r in range(N)])}

@@ -1,0 +1,410 @@
+from concourse.bass import DstId, RemoteDMATransfer
+from concourse.mybir import AluOpType as A, AxisListType, ActivationFunctionType as F
+
+N, TC, KB, CAP = 16, 2048, 64, 256
+NMAX = 5
+NCORES = 128
+
+F32, BF, FH, I32, U16 = "float32", "bfloat16", "float16", "int32", "uint16"
+SCRATCH = {"cd": ("dram", [N, 128, 1], F32)}
+for _n, _p, _w, _d in (
+        ("xb", 128, TC, BF), ("xs", 128, TC + CAP, BF), ("msg", 128, NMAX * CAP, BF), ("rcv", 128, N * CAP, BF),
+        ("yb", 128, TC, BF), ("plist", 128, 128, U16), ("off", 128, 16 * NMAX, U16), ("yoff", 128, 128, U16),
+        ("cb", 48, 128, F32), ("cs", 48, 128, F32), ("mx", 16, 4, F32), ("dc", 64, 16 * NMAX, F32),
+        ("cl", 128, 16 * NMAX, F32), ("lq", 128, 128, F32), ("zf", 128, 128, F32), ("onf", 128, 128, F32), ("ngf", 128, 8, F32),
+        ("k1", 128, 16, I32), ("k1f", 128, 16, F32), ("i64", 128, 64, BF), ("oh", 128, 1024, BF), ("onb", 128, 512, BF),
+        ("cst", 2, 64, F32), ("kt", 8, 256, I32), ("ktb", 8, 256, BF), ("sel", 8, 512, BF), ("kcol", 128, 1, F32),
+        ("ot", 128, 1024, FH), ("pr", 128, 1024, FH), ("tot", 128, 1, F32), ("wt", 128, 128, F32), ("hm", 128, 2, F32),
+        ("hmh", 128, 2, FH), ("ls", 128, 2, FH), ("so", 128, 16, U16), ("win", 128, TC, BF), ("jlo", 128, 256, BF),
+        ("jhi", 128, 256, BF), ("jv", 128, 256, BF), ("zb", 128, 144, BF), ("pint", 128, 2, I32), ("pm", 128, 4, F32),
+        ("ee", 48, 24, F32), ("yf", 128, 64, F32), ("ci", 128, 24, I32), ("blk", 128, 128, F32), ("sh", 128, 128, F32),
+        ("s15", 128, 128, F32), ("iq", 128, 128, F32), ("ic", 128, 128, F32), ("ip", 128, 128, F32), ("aa", 128, 1024, F32),
+        ("bb", 128, 1024, F32), ("ds", 128, 128, F32), ("es", 128, 128, F32)):
+    SCRATCH[_n] = ("sbuf", [_p, _w], _d)
+for _n, _w in (("kb", 1024), ("cp", 1024), ("p0", 512), ("p1", 512), ("p2", 512), ("p3", 512)):
+    SCRATCH[_n] = ("psum", [128, _w], F32)
+SEMAPHORES = ["sv", "st", "ss", "sg", "lsnd", "cown", "call", "xarr", "xpart", "parr", "data",
+              "dk1", "dkt0", "dkt1", "dx0", "dx1", "dcs", "dcb0", "dcb1", "dy0", "dy1"]
+
+_PLAN = {}
+
+
+def make_plan(cores, topo):
+    if _PLAN:
+        return _PLAN
+    chip_rank = {topo.chip(c): r for r, c in enumerate(cores)}
+    chips = sorted(chip_rank)
+    owners, active, helpers = {}, {}, {}
+    for ch in chips:
+        far = [c for c in cores if topo.mates(ch, topo.chip(c))][0]
+        here = [c for c in range(NCORES) if topo.chip(c) == ch]
+        R = cores[chip_rank[ch]]
+        own = [c for c in here if topo.may_write(c, far)]
+        owners[ch] = own
+        active[ch] = own if R in own else own + [R]
+        helpers[ch] = [c for c in own if c != R]
+    msgs, cnts = {}, {}
+    for n, ch in enumerate(chips):
+        R = cores[chip_rank[ch]]
+        for c in active[ch]:
+            msgs[c], cnts[c] = [], []
+        cross = [d for d in cores if topo.chip(d) != ch and not topo.same_plane(ch, topo.chip(d))]
+        same = [d for d in cores if topo.same_plane(ch, topo.chip(d))]
+        for i, d in enumerate(cross):
+            msgs[owners[ch][(i + n // 2) % len(owners[ch])]].append(d)
+        same = same[n // 2:] + same[:n // 2]
+        order = [c for c in active[ch] if c != R]
+        order = order[n % len(order):] + order[:n % len(order)] + [R]
+        for d in same:
+            order_min = min(order, key=lambda c: len(msgs[c]))
+            msgs[order_min].append(d)
+        dst = [d for c2 in chips if c2 != ch for d in active[c2]]
+        for d in dst:
+            if not topo.same_plane(ch, topo.chip(d)):
+                cnts[min(owners[ch], key=lambda c: len(cnts[c]))].append(d)
+        for d in dst:
+            if topo.same_plane(ch, topo.chip(d)):
+                cnts[min(active[ch], key=lambda c: len(cnts[c]))].append(d)
+    _PLAN.update(dict(rank=chip_rank, owners=owners, active=active, helpers=helpers, msgs=msgs, cnts=cnts))
+    return _PLAN
+
+
+def engines(mask):
+    return [1 << e for e in range(16) if mask >> e & 1]
+
+
+def calls_of(m, eng):
+    out = []
+    for i in range(0, len(m), 2):
+        part = list(range(i, min(i + 2, len(m))))
+        w = len(eng) // len(part)
+        out.append([(j, sum(eng[k * w:(k + 1) * w]), w) for k, j in enumerate(part)])
+    return out
+
+
+def rank_program(g, core, T, topo):
+    cores = list(T.cores)
+    P = make_plan(cores, topo)
+    ch = topo.chip(core)
+    if ch not in P["rank"] or core not in P["active"][ch]:
+        return
+    rk = P["rank"][ch]
+    R = cores[rk]
+    isR = core == R
+    helpers = P["helpers"][ch]
+    far = [c for c in cores if topo.same_plane(ch, topo.chip(c))][0]
+    eng_off = engines(topo.mask(core, far))
+    near = [c for c in P["active"][ch] if c != core][0]
+    eng_on = engines(topo.mask(core, near))
+    eng_rest = [e for e in eng_on if e not in eng_off]
+    Q = {"v": g.vector, "t": g.tensor, "s": g.scalar, "g": g, "y": g.sync}
+    cnt, seen, last, readers, totals = {}, {}, {}, {}, {}
+
+    def wait(q, tok):
+        if seen.get((q, tok[0]), 0) < tok[1]:
+            Q[q].wait_ge(T.sem[tok[0]], tok[1])
+            seen[(q, tok[0])] = tok[1]
+
+    def deps(q, r, w, acc=False):
+        own = "s" + q
+        for k in r:
+            if k in last:
+                wait(q, last[k])
+        for k in w:
+            if k in last and not (acc and last[k][0] == own):
+                wait(q, last[k])
+            for t in readers.get(k, []):
+                if t[0] != own:
+                    wait(q, t)
+
+    def note(tok, r, w):
+        for k in r:
+            readers.setdefault(k, []).append(tok)
+        for k in w:
+            last[k] = tok
+            readers[k] = []
+
+    def op(q, name, r, w, *args, acc=False, **kw):
+        s = "s" + q
+        if q == "g" and s in cnt:
+            wait(q, (s, cnt[s]))
+        deps(q, r, w, acc)
+        f = {"copy": lambda: Q[q].tensor_copy(*args), "tt": lambda: Q[q].tensor_tensor(*args),
+             "ts": lambda: Q[q].tensor_scalar(*args), "scan": lambda: Q[q].tensor_tensor_scan(*args),
+             "set": lambda: Q[q].memset(*args), "mm": lambda: Q[q].matmul(*args),
+             "act": lambda: Q[q].activation(*args), "iota": lambda: Q[q].iota(*args, **kw),
+             "aff": lambda: Q[q].affine_select(*args)}[name]
+        ins = f()
+        cnt[s] = cnt.get(s, 0) + 1
+        ins.then_inc(T.sem[s], 1)
+        totals[s] = cnt[s]
+        note((s, cnt[s]), r, w)
+
+    def iota(out, w, pat, base, cm, small=True):
+        if small:
+            op("g", "iota", [], [w], out, pat, base, cm, allow_small_or_imprecise_dtypes=True)
+        else:
+            op("g", "iota", [], [w], out, pat, base, cm)
+
+    def aff(out, w, src, rs, pat, cmp, base, cm):
+        op("g", "aff", [rs], [w], out, src, pat, cmp, 0.0, base, cm)
+
+    def dma(q, sem, r, w, out, in_):
+        deps(q, r, w)
+        Q[q].dma_start(out, in_).then_inc(T.sem[sem], 16)
+        totals[sem] = 16
+        note((sem, 16), r, w)
+
+    def arrive(sem, n, w):
+        totals[sem] = n
+        note((sem, n), [], w)
+
+    def dst_id(d):
+        a = topo.addr(d)
+        return DstId(rid=a[0], pnc=a[1])
+
+    nsent = [0]
+
+    def fused(r, trs):
+        deps("g", r, [])
+        g.remote_dma_fused([RemoteDMATransfer(dst_ids=[dst_id(d) for d in ds], dma_engine_mask=m, remote_sem=T.sem[sem],
+                                              srcs=[src], dsts=[dst for d in ds]) for ds, src, dst, m, n, sem in trs],
+                           local_sem=T.sem.lsnd)
+        nsent[0] += sum(t[4] for t in trs)
+        totals["lsnd"] = nsent[0]
+
+    def mm(r, w, out, l, rh, start=True, stop=True):
+        op("t", "mm", r, [w], out, l, rh, start, stop, acc=True)
+
+    mine = P["msgs"][core]
+    dest = [cores.index(d) for d in mine] + ([rk] if isR else [])
+    nd = len(dest)
+    n16 = 16 * nd
+
+    if isR:
+        dma("y", "dk1", [], ["k1"], T.k1[:], T.key[:])
+        dma("s", "dkt0", [], ["kt0"], T.kt[0:4, :], T.key[:, 0:64])
+        dma("y", "dkt1", [], ["kt1"], T.kt[4:8, :], T.key[:, 64:128])
+        dma("s", "dx0", [], ["x0"], T.xb[:, 0:1024], T.x[:, 0:1024])
+        dma("y", "dx1", [], ["x1"], T.xb[:, 1024:2048], T.x[:, 1024:2048])
+
+    op("v", "set", [], ["onf"], T.onf[:], 1.0)
+    if isR:
+        op("v", "set", [], ["onb"], T.onb[:], 1.0)
+        op("v", "set", [], ["win"], T.win[:], 0.0)
+        op("v", "set", [], ["zb"], T.zb[:], 0.0)
+        op("v", "set", [], ["hm"], T.hm[:], 0.0)
+        op("v", "set", [], ["hm"], T.hm[0:64, 0:1], 1.0)
+        op("v", "set", [], ["hm"], T.hm[64:128, 1:2], 1.0)
+        op("v", "copy", ["hm"], ["hmh"], T.hmh[:], T.hm[:])
+    op("v", "set", [], ["ngf"], T.ngf[:], -1.0)
+    op("v", "set", [], ["zf"], T.zf[:], 0.0)
+    op("v", "set", [], ["xpad"], T.xs[:, TC:], 0.0)
+    op("v", "set", [], ["lq"], T.lq[:], 1.0)
+    op("v", "set", [], ["clc"], T.cl[64:128, :], 0.0)
+    op("v", "set", [], ["clc"], T.cl[96:97, :], 1.0)
+    for j, d in enumerate(dest):
+        op("v", "set", [], ["dc"], T.dc[:, 16 * j:16 * j + 16], float(TC * d))
+    op("v", "set", [], ["cb0", "cb1"], T.cb[:], 0.0)
+    op("v", "set", [], ["cs0", "cs1"], T.cs[:], 0.0)
+
+    def offset_constants():
+        iota(T.cl[64:65, 0:n16], "clc", [[0, nd], [16, 16]], 0, 0)
+        iota(T.lq[96:97, :], "lq", [[0, 8], [1, 16]], 0, 0)
+        aff(T.mx[:, 0:1], "mx", T.ngf[0:16, 0:1], "ngf", [[0, 1]], A.is_ge, -rk, 1)
+        aff(T.mx[:, 1:2], "mx", T.onf[0:16, 0:1], "onf", [[0, 1]], A.is_equal, -rk, 1)
+
+    cds = P["cnts"][core]
+    half = (len(cds) + 1) // 2
+    w4 = len(eng_off) // 2
+    cnt_trs = [(ds, T.cd[rk], T.cd[rk], sum(eng_off[i * w4:(i + 1) * w4]), w4, "call")
+               for i, ds in enumerate([cds[:half], cds[half:]]) if ds]
+    call_total = 15 * w4
+    iR_on = 4
+
+    xplan = {}
+    for die in (0, 1):
+        pair = [c for c in P["owners"][ch] if topo.die(c) == die]
+        if R in pair:
+            for c in pair:
+                if c != R:
+                    xplan[c] = ([0, 1], None)
+        else:
+            for i, c in enumerate(pair):
+                xplan[c] = ([i], pair[1 - i])
+    xtr = [(c, h) for c in helpers for h in xplan[c][0]]
+    xw = len(engines(topo.mask(R, helpers[0]))) // len(xtr)
+
+    if isR:
+        iota(T.i64[:], "i64", [[1, 64]], 0, 0)
+        iota(T.pint[:, 0:1], "pint", [[0, 1]], 0, 1, small=False)
+        aff(T.sel[:], "sel", T.onb[0:8, :], "onb", [[-1, 4], [-4, 2], [0, 64]], A.is_equal, 0, 1)
+        iota(T.kcol[0:64, :], "kcol", [[0, 1]], 0, 1)
+        iota(T.kcol[64:128, :], "kcol", [[0, 1]], 0, 1)
+        for (a, b, cmp) in ((0, 0, A.is_gt), (64, 0, A.is_gt), (0, 64, A.is_ge), (64, 64, A.is_gt)):
+            aff(T.wt[a:a + 64, b:b + 64], "wt", T.onf[a:a + 64, 0:64], "onf", [[1, 64]], cmp, 0, -1)
+        op("v", "copy", ["k1"], ["k1f"], T.k1f[:], T.k1[:])
+        for i in range(16):
+            op("v", "ts", ["i64", "k1f"], ["oh%d" % i], T.oh[:, 64 * i:64 * i + 64], T.i64[:], T.k1f[:, i:i + 1], None, A.is_equal)
+            mm(["onb", "oh%d" % i], "p0", T.p0[0:2, 0:64], T.onb[:, 0:2], T.oh[:, 64 * i:64 * i + 64], i == 0, i == 15)
+        op("v", "copy", ["kt0", "kt1"], ["ktb"], T.ktb[:], T.kt[:])
+        op("v", "copy", ["p0"], ["cst"], T.cst[:], T.p0[0:2, 0:64])
+        dma("y", "dcs", ["cst"], ["cdown"], T.cd[rk], T.cst[:])
+        ew = eng_rest[:iR_on]
+        fused(["cdown"], [(helpers, T.cd[rk], T.cd[rk], sum(ew), len(ew), "cown")] + cnt_trs)
+        fused(["x0", "x1"], [([c], T.xb[:, 1024 * h:1024 * h + 1024], T.xb[:, 1024 * h:1024 * h + 1024],
+                              sum(eng_on[xw * i:xw * i + xw]), xw, "xarr") for i, (c, h) in enumerate(xtr)])
+        iota(T.jlo[:], "jlo", [[0, 16], [1, 16]], 0, 1)
+        iota(T.jhi[:], "jhi", [[128, 8], [1024, 2], [0, 16]], 0, 0)
+        offset_constants()
+        for a in range(4):
+            mm(["sel", "ktb"], "kb%d" % (a // 2), T.kb[:, 256 * a:256 * a + 256], T.sel[:, 128 * a:128 * a + 128], T.ktb[:])
+        for q in range(16):
+            op("v", "ts", ["kb%d" % (q // 8), "kcol"], ["ot"], T.ot[:, q::16], T.kb[:, 64 * q:64 * q + 64], T.kcol[:], None, A.is_equal, acc=True)
+        op("v", "scan", ["ot"], ["cp"], T.cp[:], T.ot[:], T.ot[:], 0.0, A.add, A.max)
+        op("v", "copy", ["cp"], ["tot"], T.tot[:], T.cp[:, 1023:1024])
+        mm(["wt", "tot"], "p0", T.p0[:, 64:65], T.wt[:], T.tot[:])
+        for h in (0, 1):
+            op("v", "tt", ["ot", "cp"], ["pr%d" % h], T.pr[:, 512 * h:512 * h + 512], T.ot[:, 512 * h:512 * h + 512], T.cp[:, 512 * h:512 * h + 512], A.mult)
+            if h == 0:
+                op("v", "ts", ["hm", "p0"], ["ls"], T.ls[:], T.hm[:], T.p0[:, 64:65], None, A.mult)
+        for b in range(8):
+            sl = slice(128 * b, 128 * b + 128)
+            mm(["ot", "ls"], "p1", T.p1[:, 2 * b:2 * b + 2], T.ot[:, sl], T.ls[:], True, False)
+            mm(["pr%d" % (b // 4), "hmh"], "p1", T.p1[:, 2 * b:2 * b + 2], T.pr[:, sl], T.hmh[:], False, True)
+        op("v", "ts", ["pint"], ["pint2"], T.pint[:, 1:2], T.pint[:, 0:1], 15, None, A.bitwise_and)
+        op("v", "ts", ["pint2"], ["pm0"], T.pm[:, 0:1], T.pint[:, 1:2], 0.0, None, A.is_equal)
+        op("v", "ts", ["pint2"], ["pm1"], T.pm[:, 1:2], T.pint[:, 1:2], 1.0, None, A.is_equal)
+        op("v", "ts", ["pint2"], ["pm2"], T.pm[:, 2:3], T.pint[:, 1:2], 2.0, None, A.is_lt)
+        op("v", "ts", ["jlo", "pm0"], ["jlo"], T.jlo[:], T.jlo[:], T.pm[:, 0:1], None, A.mult)
+        op("v", "ts", ["jhi", "pm1"], ["jhi"], T.jhi[:], T.jhi[:], T.pm[:, 1:2], None, A.mult)
+        op("v", "tt", ["jlo", "jhi"], ["jv"], T.jv[:], T.jlo[:], T.jhi[:], A.add)
+        op("v", "ts", ["onf", "pm2"], ["zb"], T.zb[:, 0::16], T.onf[:, 0:9], T.pm[:, 2:3], None, A.mult)
+        op("v", "ts", ["p1"], ["so"], T.so[:], T.p1[:, 0:16], -1.0, None, A.add)
+        op("v", "copy", ["so", "jv"], ["win"], T.win[:].indirect(T.so[:]), T.jv[:])
+        for q in range(16):
+            mm(["zb", "win"], "p1", T.p1[:, 128:256], T.zb[:, 16 - q:144 - q], T.win[:, q::16], q == 0, q == 15)
+        op("v", "copy", ["p1"], ["perm"], T.plist[:], T.p1[:, 128:256])
+        fused(["perm"], [(helpers, T.plist[:], T.plist[:], sum(eng_on), len(eng_on), "parr")])
+        arrive("call", call_total, ["cd"])
+    else:
+        offset_constants()
+        arrive("cown", iR_on, ["cdown"])
+        fused(["cdown"], cnt_trs)
+        halves, mate = xplan[core]
+        arrive("xarr", xw * len(halves), ["x%d" % h for h in halves])
+        if mate is not None:
+            h = halves[0]
+            fused(["x%d" % h], [([mate], T.xb[:, 1024 * h:1024 * h + 1024], T.xb[:, 1024 * h:1024 * h + 1024], sum(eng_on), len(eng_on), "xpart")])
+            arrive("xpart", len(engines(topo.mask(mate, core))), ["x%d" % (1 - h)])
+        arrive("parr", len(eng_on), ["perm"])
+        arrive("call", call_total, ["cd"])
+
+    def sort_x():
+        op("v", "copy", ["x0", "x1", "perm"], ["xs0"], T.xs[:, 0:1024], T.xb[:].indirect(T.plist[:, 0:64]))
+        op("s", "act", ["x0", "x1", "perm"], ["xs1"], T.xs[:, 1024:2048], T.xb[:].indirect(T.plist[:, 64:128]), F.Copy)
+
+    if isR:
+        sort_x()
+    dma("y", "dcb0", ["cd", "cdown"], ["cb0"], T.cb[0:16, 0:64], T.cd[:, 0:64, 0])
+    if isR:
+        dma("y", "dcb1", ["cd", "cdown"], ["cb1"], T.cb[32:48, 64:128], T.cd[:, 0:64, 0])
+    ct, cs = T.cb[0:16, 0:64], T.cs[0:16, 0:64]
+    op("v", "scan", ["cb0", "zf"], ["cs0"], cs, ct, T.zf[0:16, 0:64], 0.0, A.add, A.add)
+    mm(["cb0", "mx"], "p2", T.p2[0:64, 1:2], ct, T.mx[:, 1:2])
+    mm(["cb0", "mx"], "p2", T.p2[0:64, 0:1], ct, T.mx[:, 0:1], True, False)
+    mm(["cs0", "onf"], "p2", T.p2[0:64, 0:1], cs, T.onf[0:16, 0:1], False, True)
+    op("v", "ts", ["dc", "p2"], ["cl"], T.cl[0:64, 0:n16], T.dc[:, 0:n16], T.p2[0:64, 0:1], T.p2[0:64, 1:2], A.subtract, A.min)
+    op("v", "ts", ["cl"], ["cl"], T.cl[0:64, 0:n16], T.cl[0:64, 0:n16], 0.0, None, A.max)
+    mm(["lq", "cl", "clc"], "p2", T.p2[:, 64:64 + n16], T.lq[:], T.cl[:, 0:n16])
+    op("v", "copy", ["p2"], ["off"], T.off[:, 0:n16], T.p2[:, 64:64 + n16])
+    if not isR:
+        sort_x()
+    xr = ["xs0", "xs1", "xpad", "off"]
+
+    def gather(q, out, key, j):
+        src = T.xs[:].indirect(T.off[:, 16 * j:16 * j + 16])
+        if q == "v":
+            op("v", "copy", xr, [key], out, src)
+        else:
+            op("s", "act", xr, [key], out, src, F.Copy)
+
+    for call in calls_of(mine, eng_off):
+        for k, (j, m, n) in enumerate(call):
+            gather("vs"[j % 2], T.msg[:, CAP * j:CAP * j + CAP], "m%d" % j, j)
+        fused(["m%d" % j for j, m, n in call],
+              [([mine[j]], T.msg[:, CAP * j:CAP * j + CAP], T.rcv[:, CAP * rk:CAP * rk + CAP], m, n, "data") for j, m, n in call])
+
+    if isR:
+        gather("s", T.rcv[:, CAP * rk:CAP * rk + CAP], "own", nd - 1)
+        (sd, ya, sc, dl, wd, r256, hif, lof), (sci, hii, loi) = [T.yf[:, 8 * i:8 * i + 8] for i in range(8)], [T.ci[:, 8 * i:8 * i + 8] for i in range(3)]
+        op("v", "set", [], ["ee"], T.ee[:], 0.0)
+        op("v", "set", [], ["sh"], T.sh[:, 0:1], 0.0)
+        op("v", "set", [], ["blk"], T.blk[:], 0.0)
+        op("v", "set", [], ["blk"], T.blk[0:64, 0:64], 1.0)
+        op("v", "set", [], ["blk"], T.blk[64:128, 64:128], 1.0)
+        for h in (0, 1):
+            p = slice(32 * h, 32 * h + 16)
+            aff(T.ee[p, 0:8], "ee", T.onf[p, 0:8], "onf", [[-1, 8]], A.is_equal, -8 * h, 1)
+            aff(T.ee[p, 8:16], "ee", T.ngf[p, 0:8], "ngf", [[-1, 8]], A.is_equal, -8 * h, 1)
+            aff(T.ee[p, 16:24], "ee", T.ngf[p, 0:8], "ngf", [[-1, 8]], A.is_ge, -8 * h, 1)
+            iota(T.yf[64 * h:64 * h + 64, 40:48], "r256", [[CAP, 8]], 8 * CAP * h, 0)
+        aff(T.sh[:, 1:64], "sh", T.onf[:, 0:63], "onf", [[1, 63]], A.is_equal, 64, -1)
+        aff(T.sh[:, 64:128], "sh", T.onf[:, 0:64], "onf", [[1, 64]], A.is_equal, 0, -1)
+        aff(T.s15[:], "s15", T.onf[:], "onf", [[0, 128]], A.is_equal, -15, 1)
+        iota(T.iq[:], "iq", [[0, 8], [1, 16]], 0, 0)
+        iota(T.ic[:], "ic", [[1, 128]], 0, 0)
+        op("v", "copy", ["pint2"], ["pm3"], T.pm[:, 3:4], T.pint[:, 1:2])
+        op("v", "ts", ["ic", "pm3"], ["ip"], T.ip[:], T.ic[:], 16.0, T.pm[:, 3:4], A.mult, A.add)
+
+        op("v", "scan", ["cb1", "zf"], ["cs1"], T.cs[32:48, 64:128], T.cb[32:48, 64:128], T.zf[32:48, 0:64], 0.0, A.add, A.add)
+        cbk, csk = ["cb0", "cb1", "ee"], ["cs0", "cs1", "ee", "onf"]
+        mm(cbk, "p3", T.p3[:, 0:8], T.cb[:], T.ee[:, 0:8])
+        mm(cbk, "p3", T.p3[:, 8:16], T.cb[:], T.ee[:, 16:24], True, False)
+        mm(csk, "p3", T.p3[:, 8:16], T.cs[:], T.onf[0:48, 0:8], False, True)
+        mm(cbk, "p3", T.p3[:, 16:24], T.cb[:], T.ee[:, 8:16], True, False)
+        mm(csk, "p3", T.p3[:, 16:24], T.cs[:], T.ee[:, 0:8], False, True)
+        op("v", "ts", ["p3"], ["sd"], sd, T.p3[:, 8:16], -float(TC * rk), None, A.add)
+        op("v", "ts", ["sd"], ["ya"], ya, sd, -1.0, 0.0, A.mult, A.max)
+        op("v", "tt", ["ya", "p3"], ["ya"], ya, ya, T.p3[:, 0:8], A.min)
+        op("v", "copy", ["p3"], ["dl"], dl, T.p3[:, 16:24])
+        op("v", "ts", ["sd"], ["sc"], sc, sd, 0.0, float(TC), A.max, A.min)
+        mm(["blk", "ya"], "p3", T.p3[:, 24:32], T.blk[:], ya)
+        op("v", "copy", ["sc"], ["sci"], sci, sc)
+        op("v", "ts", ["sci"], ["hii"], hii, sci, 4, None, A.arith_shift_right)
+        op("v", "ts", ["sci"], ["loi"], loi, sci, 15, None, A.bitwise_and)
+        op("v", "copy", ["hii"], ["hif"], hif, hii)
+        op("v", "copy", ["loi"], ["lof"], lof, loi)
+        op("v", "tt", ["dl", "p3"], ["dl"], dl, dl, T.p3[:, 24:32], A.subtract)
+        op("v", "ts", ["dl"], ["dl"], dl, dl, 0.0, float(CAP), A.max, A.min)
+        op("v", "tt", ["dl", "sc"], ["dl"], dl, dl, sc, A.subtract)
+        op("v", "tt", ["dl", "r256"], ["dl"], dl, dl, r256, A.add)
+        mm(["sh", "dl"], "p3", T.p3[:, 32:33], T.sh[:], T.yf[:, 31:32])
+        op("v", "tt", ["dl"], ["wd"], T.yf[:, 33:40], T.yf[:, 25:32], T.yf[:, 24:31], A.subtract)
+        op("v", "tt", ["dl", "p3"], ["wd"], T.yf[:, 32:33], T.yf[:, 24:25], T.p3[:, 32:33], A.subtract)
+        for i in range(8):
+            sl = slice(128 * i, 128 * i + 128)
+            op("v", "ts", ["iq", "lof"], ["aa%d" % i], T.aa[:, sl], T.iq[:], T.yf[:, 56 + i:57 + i], None, A.is_ge)
+            op("v", "ts", ["ic", "hif", "wd"], ["bb%d" % i], T.bb[:, sl], T.ic[:], T.yf[:, 48 + i:49 + i], T.yf[:, 32 + i:33 + i], A.is_equal, A.mult)
+            mm(["aa%d" % i, "bb%d" % i], "kb0", T.kb[:, 0:128], T.aa[:, sl], T.bb[:, sl], i == 0, i == 7)
+        op("v", "copy", ["kb0"], ["ds"], T.ds[:], T.kb[:, 0:128])
+        mm(["s15", "ds"], "cp", T.cp[:, 0:128], T.s15[:], T.ds[:])
+        op("v", "tt", ["ds", "ip"], ["ip"], T.ip[:], T.ds[:], T.ip[:], A.add)
+        op("v", "scan", ["cp", "zf"], ["es"], T.es[:], T.cp[:, 0:128], T.zf[:], 0.0, A.add, A.add)
+        op("v", "tt", ["ip", "es"], ["ip"], T.ip[:, 1:128], T.ip[:, 1:128], T.es[:, 0:127], A.add)
+        op("v", "copy", ["ip"], ["yoff"], T.yoff[:], T.ip[:])
+        n_in = 0
+        for c2 in P["msgs"]:
+            if topo.chip(c2) != ch:
+                e2 = engines(topo.mask(c2, R))
+                for call in calls_of(P["msgs"][c2], e2):
+                    n_in += sum(n for j, m, n in call if P["msgs"][c2][j] == R)
+        arrive("data", n_in, ["rcv"])
+        yr = ["rcv", "own", "yoff"]
+        op("v", "copy", yr, ["y0"], T.yb[:, 0:1024], T.rcv[:].indirect(T.yoff[:, 0:64]))
+        op("s", "act", yr, ["y1"], T.yb[:, 1024:2048], T.rcv[:].indirect(T.yoff[:, 64:128]), F.Copy)
+        dma("y", "dy0", ["y0"], ["yo0"], T.y[:, 0:1024], T.yb[:, 0:1024])
+        dma("s", "dy1", ["y1"], ["yo1"], T.y[:, 1024:2048], T.yb[:, 1024:2048])
+
+    for s in sorted(totals):
+        wait("g", (s, totals[s]))

@@ -6,7 +6,8 @@ NMAX = 5
 NCORES = 128
 
 F32, BF, FH, I32, U16 = "float32", "bfloat16", "float16", "int32", "uint16"
-SCRATCH = {"cd": ("dram", [N, 128, 1], F32)}
+SCRATCH = {"cd": ("dram", [N, 128, 1], F32),
+           "kd": ("dram", [128, 16], I32)}
 for _n, _p, _w, _d in (
         ("xb", 128, TC, BF), ("xs", 128, TC + CAP, BF), ("msg", 128, NMAX * CAP, BF), ("rcv", 128, N * CAP, BF),
         ("yb", 128, TC, BF), ("plist", 128, 128, U16), ("off", 128, 16 * NMAX, U16), ("yoff", 128, 128, U16),
@@ -15,16 +16,17 @@ for _n, _p, _w, _d in (
         ("k1", 128, 16, I32), ("k1f", 128, 16, F32), ("i64", 128, 64, BF), ("oh", 128, 1024, BF), ("onb", 128, 512, BF),
         ("cst", 2, 64, F32), ("kt", 8, 256, I32), ("ktb", 8, 256, BF), ("sel", 8, 512, BF), ("kcol", 128, 1, F32),
         ("ot", 128, 1024, FH), ("pr", 128, 1024, FH), ("tot", 128, 1, F32), ("wt", 128, 128, F32), ("hm", 128, 2, F32),
-        ("hmh", 128, 2, FH), ("ls", 128, 2, FH), ("so", 128, 16, U16), ("win", 128, TC, BF), ("jlo", 128, 256, BF),
-        ("jhi", 128, 256, BF), ("jv", 128, 256, BF), ("zb", 128, 144, BF), ("pint", 128, 2, I32), ("pm", 128, 4, F32),
-        ("ee", 48, 24, F32), ("yf", 128, 64, F32), ("ci", 128, 24, I32), ("blk", 128, 128, F32), ("sh", 128, 128, F32),
-        ("s15", 128, 128, F32), ("iq", 128, 128, F32), ("ic", 128, 128, F32), ("ip", 128, 128, F32), ("aa", 128, 1024, F32),
-        ("bb", 128, 1024, F32), ("ds", 128, 128, F32), ("es", 128, 128, F32)):
+        ("hmh", 128, 2, FH), ("ls", 128, 2, FH), ("so", 128, 16, U16), ("win", 128, TC, BF), ("jlo", 128, 16, BF),
+        ("jhi", 128, 16, F32), ("jv", 128, 256, BF), ("zb", 128, 144, BF), ("pint", 128, 3, I32), ("pm", 128, 4, F32),
+        ("ee", 48, 24, F32), ("yf", 128, 80, F32), ("ci", 128, 48, I32), ("blk", 128, 128, F32), ("sh", 128, 128, F32),
+        ("s15", 128, 128, F32), ("iq", 128, 128, BF), ("ic", 128, 128, BF), ("ip", 128, 128, F32), ("aa", 128, 1024, BF),
+        ("bb", 128, 2048, BF), ("ds", 128, 128, F32), ("es", 128, 128, F32)):
     SCRATCH[_n] = ("sbuf", [_p, _w], _d)
 for _n, _w in (("kb", 1024), ("cp", 1024), ("p0", 512), ("p1", 512), ("p2", 512), ("p3", 512)):
     SCRATCH[_n] = ("psum", [128, _w], F32)
-SEMAPHORES = ["sv", "st", "ss", "sg", "lsnd", "cown", "call", "xarr", "xpart", "parr", "data",
-              "dk1", "dkt0", "dkt1", "dx0", "dx1", "dcs", "dcb0", "dcb1", "dy0", "dy1"]
+SEMAPHORES = ["sv", "st", "ss", "sg", "lsnd", "cown", "call", "kown", "xarr", "xpart", "xhalf", "data",
+              "dk1", "dkd0", "dkd1", "dkt0", "dkt1", "dx0", "dx1", "dcs", "dcb0", "dcb1", "dy0", "dy1"]
+CW = 2
 
 _PLAN = {}
 
@@ -55,9 +57,12 @@ def make_plan(cores, topo):
         same = same[n // 2:] + same[:n // 2]
         order = [c for c in active[ch] if c != R]
         order = order[n % len(order):] + order[:n % len(order)] + [R]
+
+        def load(c):
+            port = sum(1 for b in order if topo.die(b) == topo.die(c) for e in msgs[b] if topo.same_plane(ch, topo.chip(e)))
+            return port, len(msgs[c])
         for d in same:
-            order_min = min(order, key=lambda c: len(msgs[c]))
-            msgs[order_min].append(d)
+            msgs[min(order, key=load)].append(d)
         dst = [d for c2 in chips if c2 != ch for d in active[c2]]
         for d in dst:
             if not topo.same_plane(ch, topo.chip(d)):
@@ -149,6 +154,9 @@ def rank_program(g, core, T, topo):
     def aff(out, w, src, rs, pat, cmp, base, cm):
         op("g", "aff", [rs], [w], out, src, pat, cmp, 0.0, base, cm)
 
+    def vset(w, ap, value):
+        op("v", "set", [], [w], ap, value)
+
     def dma(q, sem, r, w, out, in_):
         deps(q, r, w)
         Q[q].dma_start(out, in_).then_inc(T.sem[sem], 16)
@@ -167,10 +175,10 @@ def rank_program(g, core, T, topo):
 
     def fused(r, trs):
         deps("g", r, [])
-        g.remote_dma_fused([RemoteDMATransfer(dst_ids=[dst_id(d) for d in ds], dma_engine_mask=m, remote_sem=T.sem[sem],
-                                              srcs=[src], dsts=[dst for d in ds]) for ds, src, dst, m, n, sem in trs],
+        g.remote_dma_fused([RemoteDMATransfer(dst_ids=[dst_id(d) for d in ds], dma_engine_mask=sum(es), remote_sem=T.sem[sem],
+                                              srcs=[src], dsts=[dst for d in ds]) for ds, src, dst, es, sem in trs],
                            local_sem=T.sem.lsnd)
-        nsent[0] += sum(t[4] for t in trs)
+        nsent[0] += sum(len(t[3]) for t in trs)
         totals["lsnd"] = nsent[0]
 
     def mm(r, w, out, l, rh, start=True, stop=True):
@@ -180,33 +188,38 @@ def rank_program(g, core, T, topo):
     dest = [cores.index(d) for d in mine] + ([rk] if isR else [])
     nd = len(dest)
     n16 = 16 * nd
+    chip_eng = eng_off[2 * CW:3 * CW]
 
     if isR:
         dma("y", "dk1", [], ["k1"], T.k1[:], T.key[:])
+        dma("s", "dkd0", [], ["kd0"], T.kd[0:64, :], T.key[:, 0:64])
+        dma("y", "dkd1", [], ["kd1"], T.kd[64:128, :], T.key[:, 64:128])
         dma("s", "dkt0", [], ["kt0"], T.kt[0:4, :], T.key[:, 0:64])
         dma("y", "dkt1", [], ["kt1"], T.kt[4:8, :], T.key[:, 64:128])
-        dma("s", "dx0", [], ["x0"], T.xb[:, 0:1024], T.x[:, 0:1024])
+        dma("y", "dx0", [], ["x0"], T.xb[:, 0:1024], T.x[:, 0:1024])
         dma("y", "dx1", [], ["x1"], T.xb[:, 1024:2048], T.x[:, 1024:2048])
 
-    op("v", "set", [], ["onf"], T.onf[:], 1.0)
-    if isR:
-        op("v", "set", [], ["onb"], T.onb[:], 1.0)
-        op("v", "set", [], ["win"], T.win[:], 0.0)
-        op("v", "set", [], ["zb"], T.zb[:], 0.0)
-        op("v", "set", [], ["hm"], T.hm[:], 0.0)
-        op("v", "set", [], ["hm"], T.hm[0:64, 0:1], 1.0)
-        op("v", "set", [], ["hm"], T.hm[64:128, 1:2], 1.0)
-        op("v", "copy", ["hm"], ["hmh"], T.hmh[:], T.hm[:])
-    op("v", "set", [], ["ngf"], T.ngf[:], -1.0)
-    op("v", "set", [], ["zf"], T.zf[:], 0.0)
-    op("v", "set", [], ["xpad"], T.xs[:, TC:], 0.0)
-    op("v", "set", [], ["lq"], T.lq[:], 1.0)
-    op("v", "set", [], ["clc"], T.cl[64:128, :], 0.0)
-    op("v", "set", [], ["clc"], T.cl[96:97, :], 1.0)
-    for j, d in enumerate(dest):
-        op("v", "set", [], ["dc"], T.dc[:, 16 * j:16 * j + 16], float(TC * d))
-    op("v", "set", [], ["cb0", "cb1"], T.cb[:], 0.0)
-    op("v", "set", [], ["cs0", "cs1"], T.cs[:], 0.0)
+    vset("onf", T.onf[:], 1.0)
+    vset("ngf", T.ngf[:], -1.0)
+    vset("onb", T.onb[:], 1.0)
+    vset("zb", T.zb[:], 0.0)
+
+    def vector_constants():
+        vset("zf", T.zf[:], 0.0)
+        vset("xpad", T.xs[:, TC:], 0.0)
+        vset("lq", T.lq[:], 1.0)
+        vset("clc", T.cl[64:128, :], 0.0)
+        vset("clc", T.cl[96:97, :], 1.0)
+        for j, d in enumerate(dest):
+            vset("dc", T.dc[:, 16 * j:16 * j + 16], float(TC * d))
+        op("v", "set", [], ["cb0", "cb1"], T.cb[:], 0.0)
+        op("v", "set", [], ["cs0", "cs1"], T.cs[:], 0.0)
+        if isR:
+            vset("ee", T.ee[:], 0.0)
+            vset("sh", T.sh[:, 0:1], 0.0)
+            vset("blk", T.blk[:], 0.0)
+            vset("blk", T.blk[0:64, 0:64], 1.0)
+            vset("blk", T.blk[64:128, 64:128], 1.0)
 
     def offset_constants():
         iota(T.cl[64:65, 0:n16], "clc", [[0, nd], [16, 16]], 0, 0)
@@ -216,47 +229,43 @@ def rank_program(g, core, T, topo):
 
     cds = P["cnts"][core]
     half = (len(cds) + 1) // 2
-    w4 = len(eng_off) // 2
-    cnt_trs = [(ds, T.cd[rk], T.cd[rk], sum(eng_off[i * w4:(i + 1) * w4]), w4, "call")
-               for i, ds in enumerate([cds[:half], cds[half:]]) if ds]
-    call_total = 15 * w4
-    iR_on = 4
+    cnt_trs = [(ds, T.cd[rk], T.cd[rk], eng_off[i * CW:(i + 1) * CW], "call") for i, ds in enumerate([cds[:half], cds[half:]]) if ds]
 
-    xplan = {}
-    for die in (0, 1):
-        pair = [c for c in P["owners"][ch] if topo.die(c) == die]
-        if R in pair:
-            for c in pair:
-                if c != R:
-                    xplan[c] = ([0, 1], None)
-        else:
-            for i, c in enumerate(pair):
-                xplan[c] = ([i], pair[1 - i])
-    xtr = [(c, h) for c in helpers for h in xplan[c][0]]
-    xw = len(engines(topo.mask(R, helpers[0]))) // len(xtr)
+    pairs = [[c for c in helpers if topo.die(c) == die] for die in (0, 1)]
+    first = [p[0] for p in pairs]
+    later = {p[0]: p[1] for p in pairs if len(p) > 1}
+    long = max(pairs, key=len)
+    short = [c for c in helpers if c not in long]
+    x0, x1 = [T.xb[:, 1024 * h:1024 * h + 1024] for h in (0, 1)]
 
-    if isR:
+    def sort_constants():
         iota(T.i64[:], "i64", [[1, 64]], 0, 0)
         iota(T.pint[:, 0:1], "pint", [[0, 1]], 0, 1, small=False)
+        iota(T.jlo[:], "jlo", [[1, 16]], 0, 1)
+        iota(T.jhi[:], "jhi", [[128, 8], [1024, 2]], 0, 0)
         aff(T.sel[:], "sel", T.onb[0:8, :], "onb", [[-1, 4], [-4, 2], [0, 64]], A.is_equal, 0, 1)
-        iota(T.kcol[0:64, :], "kcol", [[0, 1]], 0, 1)
-        iota(T.kcol[64:128, :], "kcol", [[0, 1]], 0, 1)
-        for (a, b, cmp) in ((0, 0, A.is_gt), (64, 0, A.is_gt), (0, 64, A.is_ge), (64, 64, A.is_gt)):
-            aff(T.wt[a:a + 64, b:b + 64], "wt", T.onf[a:a + 64, 0:64], "onf", [[1, 64]], cmp, 0, -1)
-        op("v", "copy", ["k1"], ["k1f"], T.k1f[:], T.k1[:])
+        op("v", "ts", ["pint"], ["pint1"], T.pint[:, 1:2], T.pint[:, 0:1], 63, None, A.bitwise_and)
+        op("v", "ts", ["pint"], ["pint2"], T.pint[:, 2:3], T.pint[:, 0:1], 15, None, A.bitwise_and)
+        op("v", "copy", ["pint1"], ["kcol"], T.kcol[:], T.pint[:, 1:2])
+        for i, (v, cmp) in enumerate(((0.0, A.is_equal), (1.0, A.is_equal), (2.0, A.is_lt))):
+            op("v", "ts", ["pint2"], ["pm%d" % i], T.pm[:, i:i + 1], T.pint[:, 2:3], v, None, cmp)
+        op("v", "ts", ["onf", "pm2"], ["zb"], T.zb[:, 0::16], T.onf[:, 0:9], T.pm[:, 2:3], None, A.mult)
+        op("v", "ts", ["jlo", "pm0"], ["jlo"], T.jlo[:], T.jlo[:], T.pm[:, 0:1], None, A.mult)
+        op("v", "ts", ["jhi", "pm1"], ["jhi"], T.jhi[:], T.jhi[:], T.pm[:, 1:2], None, A.mult)
         for i in range(16):
-            op("v", "ts", ["i64", "k1f"], ["oh%d" % i], T.oh[:, 64 * i:64 * i + 64], T.i64[:], T.k1f[:, i:i + 1], None, A.is_equal)
-            mm(["onb", "oh%d" % i], "p0", T.p0[0:2, 0:64], T.onb[:, 0:2], T.oh[:, 64 * i:64 * i + 64], i == 0, i == 15)
-        op("v", "copy", ["kt0", "kt1"], ["ktb"], T.ktb[:], T.kt[:])
-        op("v", "copy", ["p0"], ["cst"], T.cst[:], T.p0[0:2, 0:64])
-        dma("y", "dcs", ["cst"], ["cdown"], T.cd[rk], T.cst[:])
-        ew = eng_rest[:iR_on]
-        fused(["cdown"], [(helpers, T.cd[rk], T.cd[rk], sum(ew), len(ew), "cown")] + cnt_trs)
-        fused(["x0", "x1"], [([c], T.xb[:, 1024 * h:1024 * h + 1024], T.xb[:, 1024 * h:1024 * h + 1024],
-                              sum(eng_on[xw * i:xw * i + xw]), xw, "xarr") for i, (c, h) in enumerate(xtr)])
-        iota(T.jlo[:], "jlo", [[0, 16], [1, 16]], 0, 1)
-        iota(T.jhi[:], "jhi", [[128, 8], [1024, 2], [0, 16]], 0, 0)
-        offset_constants()
+            op("s", "act", ["jlo", "jhi"], ["jv"], T.jv[:, 16 * i:16 * i + 16], T.jlo[:], F.Identity, T.jhi[:, i:i + 1], acc=True)
+
+    def sort_fills():
+        vset("win", T.win[:], 0.0)
+        vset("hm", T.hm[:], 0.0)
+        vset("hm", T.hm[0:64, 0:1], 1.0)
+        vset("hm", T.hm[64:128, 1:2], 1.0)
+        op("v", "copy", ["hm"], ["hmh"], T.hmh[:], T.hm[:])
+        for b in (0, 64):
+            op("v", "ts", ["i64", "kcol"], ["wt"], T.wt[:, b:b + 64], T.i64[:], T.kcol[:], None, A.is_gt)
+        op("v", "ts", ["i64", "kcol"], ["wt"], T.wt[0:64, 64:128], T.i64[0:64, :], T.kcol[0:64, :], None, A.is_ge)
+
+    def sort_columns():
         for a in range(4):
             mm(["sel", "ktb"], "kb%d" % (a // 2), T.kb[:, 256 * a:256 * a + 256], T.sel[:, 128 * a:128 * a + 128], T.ktb[:])
         for q in range(16):
@@ -272,33 +281,57 @@ def rank_program(g, core, T, topo):
             sl = slice(128 * b, 128 * b + 128)
             mm(["ot", "ls"], "p1", T.p1[:, 2 * b:2 * b + 2], T.ot[:, sl], T.ls[:], True, False)
             mm(["pr%d" % (b // 4), "hmh"], "p1", T.p1[:, 2 * b:2 * b + 2], T.pr[:, sl], T.hmh[:], False, True)
-        op("v", "ts", ["pint"], ["pint2"], T.pint[:, 1:2], T.pint[:, 0:1], 15, None, A.bitwise_and)
-        op("v", "ts", ["pint2"], ["pm0"], T.pm[:, 0:1], T.pint[:, 1:2], 0.0, None, A.is_equal)
-        op("v", "ts", ["pint2"], ["pm1"], T.pm[:, 1:2], T.pint[:, 1:2], 1.0, None, A.is_equal)
-        op("v", "ts", ["pint2"], ["pm2"], T.pm[:, 2:3], T.pint[:, 1:2], 2.0, None, A.is_lt)
-        op("v", "ts", ["jlo", "pm0"], ["jlo"], T.jlo[:], T.jlo[:], T.pm[:, 0:1], None, A.mult)
-        op("v", "ts", ["jhi", "pm1"], ["jhi"], T.jhi[:], T.jhi[:], T.pm[:, 1:2], None, A.mult)
-        op("v", "tt", ["jlo", "jhi"], ["jv"], T.jv[:], T.jlo[:], T.jhi[:], A.add)
-        op("v", "ts", ["onf", "pm2"], ["zb"], T.zb[:, 0::16], T.onf[:, 0:9], T.pm[:, 2:3], None, A.mult)
         op("v", "ts", ["p1"], ["so"], T.so[:], T.p1[:, 0:16], -1.0, None, A.add)
         op("v", "copy", ["so", "jv"], ["win"], T.win[:].indirect(T.so[:]), T.jv[:])
+        if isR:
+            vector_constants()
         for q in range(16):
             mm(["zb", "win"], "p1", T.p1[:, 128:256], T.zb[:, 16 - q:144 - q], T.win[:, q::16], q == 0, q == 15)
         op("v", "copy", ["p1"], ["perm"], T.plist[:], T.p1[:, 128:256])
-        fused(["perm"], [(helpers, T.plist[:], T.plist[:], sum(eng_on), len(eng_on), "parr")])
-        arrive("call", call_total, ["cd"])
-    else:
+
+    sort_constants()
+    if isR:
+        fused(["kd0", "kd1"], [(helpers, T.kd[:], T.kd[:], chip_eng, "kown")])
+        op("v", "copy", ["k1"], ["k1f"], T.k1f[:], T.k1[:])
+        for i in range(16):
+            op("v", "ts", ["i64", "k1f"], ["oh%d" % i], T.oh[:, 64 * i:64 * i + 64], T.i64[:], T.k1f[:, i:i + 1], None, A.is_equal)
+            mm(["onb", "oh%d" % i], "p0", T.p0[0:2, 0:64], T.onb[:, 0:2], T.oh[:, 64 * i:64 * i + 64], i == 0, i == 15)
+        op("v", "copy", ["kt0", "kt1"], ["ktb"], T.ktb[:], T.kt[:])
+        op("v", "copy", ["p0"], ["cst"], T.cst[:], T.p0[0:2, 0:64])
+        dma("y", "dcs", ["cst"], ["cdown"], T.cd[rk], T.cst[:])
+        fused(["x0"], [(first, x0, x0, eng_rest, "xarr")])
+        fused(["cdown"], [(helpers, T.cd[rk], T.cd[rk], chip_eng, "cown")] + cnt_trs)
+        fused(["x1"], [(long, x1, x1, eng_off, "xhalf"), (short, x1, x1, eng_rest, "xhalf")])
+        sort_fills()
+        sort_columns()
         offset_constants()
-        arrive("cown", iR_on, ["cdown"])
+        arrive("call", 15 * CW, ["cd"])
+        for h in (0, 1):
+            p = slice(32 * h, 32 * h + 16)
+            aff(T.ee[p, 0:8], "ee", T.onf[p, 0:8], "onf", [[-1, 8]], A.is_equal, -8 * h, 1)
+            aff(T.ee[p, 8:16], "ee", T.ngf[p, 0:8], "ngf", [[-1, 8]], A.is_equal, -8 * h, 1)
+            aff(T.ee[p, 16:24], "ee", T.ngf[p, 0:8], "ngf", [[-1, 8]], A.is_ge, -8 * h, 1)
+            iota(T.yf[64 * h:64 * h + 64, 40:48], "r256", [[CAP, 8]], 8 * CAP * h, 0)
+        aff(T.sh[:, 1:64], "sh", T.onf[:, 0:63], "onf", [[1, 63]], A.is_equal, 64, -1)
+        aff(T.sh[:, 64:128], "sh", T.onf[:, 0:64], "onf", [[1, 64]], A.is_equal, 0, -1)
+        aff(T.s15[:], "s15", T.onf[:], "onf", [[0, 128]], A.is_equal, -15, 1)
+        iota(T.iq[:], "iq", [[0, 8], [1, 16]], 0, 0)
+        iota(T.ic[:], "ic", [[1, 128]], 0, 0)
+    else:
+        arrive("kown", CW, ["kd"])
+        dma("y", "dkt0", ["kd"], ["kt"], T.kt[:], T.kd[:])
+        sort_fills()
+        vector_constants()
+        offset_constants()
+        op("v", "copy", ["kt"], ["ktb"], T.ktb[:], T.kt[:])
+        sort_columns()
+        arrive("cown", CW, ["cdown"])
         fused(["cdown"], cnt_trs)
-        halves, mate = xplan[core]
-        arrive("xarr", xw * len(halves), ["x%d" % h for h in halves])
-        if mate is not None:
-            h = halves[0]
-            fused(["x%d" % h], [([mate], T.xb[:, 1024 * h:1024 * h + 1024], T.xb[:, 1024 * h:1024 * h + 1024], sum(eng_on), len(eng_on), "xpart")])
-            arrive("xpart", len(engines(topo.mask(mate, core))), ["x%d" % (1 - h)])
-        arrive("parr", len(eng_on), ["perm"])
-        arrive("call", call_total, ["cd"])
+        arrive("xarr" if core in first else "xpart", len(eng_rest), ["x0"])
+        arrive("xhalf", len(eng_off if core in long else eng_rest), ["x1"])
+        if core in later:
+            fused(["x0"], [([later[core]], x0, x0, eng_rest, "xpart")])
+        arrive("call", 15 * CW, ["cd"])
 
     def sort_x():
         op("v", "copy", ["x0", "x1", "perm"], ["xs0"], T.xs[:, 0:1024], T.xb[:].indirect(T.plist[:, 0:64]))
@@ -330,33 +363,17 @@ def rank_program(g, core, T, topo):
             op("s", "act", xr, [key], out, src, F.Copy)
 
     for call in calls_of(mine, eng_off):
-        for k, (j, m, n) in enumerate(call):
+        for j, m, n in call:
             gather("vs"[j % 2], T.msg[:, CAP * j:CAP * j + CAP], "m%d" % j, j)
         fused(["m%d" % j for j, m, n in call],
-              [([mine[j]], T.msg[:, CAP * j:CAP * j + CAP], T.rcv[:, CAP * rk:CAP * rk + CAP], m, n, "data") for j, m, n in call])
+              [([mine[j]], T.msg[:, CAP * j:CAP * j + CAP], T.rcv[:, CAP * rk:CAP * rk + CAP], engines(m), "data") for j, m, n in call])
 
     if isR:
         gather("s", T.rcv[:, CAP * rk:CAP * rk + CAP], "own", nd - 1)
-        (sd, ya, sc, dl, wd, r256, hif, lof), (sci, hii, loi) = [T.yf[:, 8 * i:8 * i + 8] for i in range(8)], [T.ci[:, 8 * i:8 * i + 8] for i in range(3)]
-        op("v", "set", [], ["ee"], T.ee[:], 0.0)
-        op("v", "set", [], ["sh"], T.sh[:, 0:1], 0.0)
-        op("v", "set", [], ["blk"], T.blk[:], 0.0)
-        op("v", "set", [], ["blk"], T.blk[0:64, 0:64], 1.0)
-        op("v", "set", [], ["blk"], T.blk[64:128, 64:128], 1.0)
-        for h in (0, 1):
-            p = slice(32 * h, 32 * h + 16)
-            aff(T.ee[p, 0:8], "ee", T.onf[p, 0:8], "onf", [[-1, 8]], A.is_equal, -8 * h, 1)
-            aff(T.ee[p, 8:16], "ee", T.ngf[p, 0:8], "ngf", [[-1, 8]], A.is_equal, -8 * h, 1)
-            aff(T.ee[p, 16:24], "ee", T.ngf[p, 0:8], "ngf", [[-1, 8]], A.is_ge, -8 * h, 1)
-            iota(T.yf[64 * h:64 * h + 64, 40:48], "r256", [[CAP, 8]], 8 * CAP * h, 0)
-        aff(T.sh[:, 1:64], "sh", T.onf[:, 0:63], "onf", [[1, 63]], A.is_equal, 64, -1)
-        aff(T.sh[:, 64:128], "sh", T.onf[:, 0:64], "onf", [[1, 64]], A.is_equal, 0, -1)
-        aff(T.s15[:], "s15", T.onf[:], "onf", [[0, 128]], A.is_equal, -15, 1)
-        iota(T.iq[:], "iq", [[0, 8], [1, 16]], 0, 0)
-        iota(T.ic[:], "ic", [[1, 128]], 0, 0)
-        op("v", "copy", ["pint2"], ["pm3"], T.pm[:, 3:4], T.pint[:, 1:2])
+        sd, ya, sc, dl, wd, r256, hif, lof, wh, wl = [T.yf[:, 8 * i:8 * i + 8] for i in range(10)]
+        sci, hii, loi, wi, whi, wli = [T.ci[:, 8 * i:8 * i + 8] for i in range(6)]
+        op("v", "copy", ["pint2"], ["pm3"], T.pm[:, 3:4], T.pint[:, 2:3])
         op("v", "ts", ["ic", "pm3"], ["ip"], T.ip[:], T.ic[:], 16.0, T.pm[:, 3:4], A.mult, A.add)
-
         op("v", "scan", ["cb1", "zf"], ["cs1"], T.cs[32:48, 64:128], T.cb[32:48, 64:128], T.zf[32:48, 0:64], 0.0, A.add, A.add)
         cbk, csk = ["cb0", "cb1", "ee"], ["cs0", "cs1", "ee", "onf"]
         mm(cbk, "p3", T.p3[:, 0:8], T.cb[:], T.ee[:, 0:8])
@@ -382,11 +399,19 @@ def rank_program(g, core, T, topo):
         mm(["sh", "dl"], "p3", T.p3[:, 32:33], T.sh[:], T.yf[:, 31:32])
         op("v", "tt", ["dl"], ["wd"], T.yf[:, 33:40], T.yf[:, 25:32], T.yf[:, 24:31], A.subtract)
         op("v", "tt", ["dl", "p3"], ["wd"], T.yf[:, 32:33], T.yf[:, 24:25], T.p3[:, 32:33], A.subtract)
+        op("v", "copy", ["wd"], ["wi"], wi, wd)
+        op("v", "ts", ["wi"], ["whi"], whi, wi, 6, None, A.arith_shift_right)
+        op("v", "ts", ["wi"], ["wli"], wli, wi, 63, None, A.bitwise_and)
+        op("v", "ts", ["whi"], ["wh"], wh, whi, 64.0, None, A.mult)
+        op("v", "copy", ["wli"], ["wl"], wl, wli)
         for i in range(8):
             sl = slice(128 * i, 128 * i + 128)
             op("v", "ts", ["iq", "lof"], ["aa%d" % i], T.aa[:, sl], T.iq[:], T.yf[:, 56 + i:57 + i], None, A.is_ge)
-            op("v", "ts", ["ic", "hif", "wd"], ["bb%d" % i], T.bb[:, sl], T.ic[:], T.yf[:, 48 + i:49 + i], T.yf[:, 32 + i:33 + i], A.is_equal, A.mult)
-            mm(["aa%d" % i, "bb%d" % i], "kb0", T.kb[:, 0:128], T.aa[:, sl], T.bb[:, sl], i == 0, i == 7)
+            for k, part in ((0, "wh"), (1, "wl")):
+                s2 = slice(256 * i + 128 * k, 256 * i + 128 * k + 128)
+                op("v", "ts", ["ic", "hif", part], ["bb%d" % (2 * i + k)], T.bb[:, s2], T.ic[:], T.yf[:, 48 + i:49 + i],
+                   T.yf[:, 64 + 8 * k + i:65 + 8 * k + i], A.is_equal, A.mult)
+                mm(["aa%d" % i, "bb%d" % (2 * i + k)], "kb0", T.kb[:, 0:128], T.aa[:, sl], T.bb[:, s2], i + k == 0, i + k == 8)
         op("v", "copy", ["kb0"], ["ds"], T.ds[:], T.kb[:, 0:128])
         mm(["s15", "ds"], "cp", T.cp[:, 0:128], T.s15[:], T.ds[:])
         op("v", "tt", ["ds", "ip"], ["ip"], T.ip[:], T.ds[:], T.ip[:], A.add)
@@ -401,10 +426,11 @@ def rank_program(g, core, T, topo):
                     n_in += sum(n for j, m, n in call if P["msgs"][c2][j] == R)
         arrive("data", n_in, ["rcv"])
         yr = ["rcv", "own", "yoff"]
-        op("v", "copy", yr, ["y0"], T.yb[:, 0:1024], T.rcv[:].indirect(T.yoff[:, 0:64]))
-        op("s", "act", yr, ["y1"], T.yb[:, 1024:2048], T.rcv[:].indirect(T.yoff[:, 64:128]), F.Copy)
-        dma("y", "dy0", ["y0"], ["yo0"], T.y[:, 0:1024], T.yb[:, 0:1024])
-        dma("s", "dy1", ["y1"], ["yo1"], T.y[:, 1024:2048], T.yb[:, 1024:2048])
+        for h in (0, 1):
+            a, b, o = 1024 * h, 1024 * h + 512, 64 * h
+            op("v", "copy", yr, ["ya%d" % h], T.yb[:, a:b], T.rcv[:].indirect(T.yoff[:, o:o + 32]))
+            op("s", "act", yr, ["yb%d" % h], T.yb[:, b:b + 512], T.rcv[:].indirect(T.yoff[:, o + 32:o + 64]), F.Copy)
+            dma("y", "dy%d" % h, ["ya%d" % h, "yb%d" % h], ["yo%d" % h], T.y[:, a:a + 1024], T.yb[:, a:a + 1024])
 
     for s in sorted(totals):
         wait("g", (s, totals[s]))

@@ -4,10 +4,8 @@ from concourse.mybir import AluOpType as A, AxisListType, ActivationFunctionType
 N, TC, KB, CAP = 16, 2048, 64, 256
 NMAX = 5
 NCORES = 128
-
 F32, BF, FH, I32, U16 = "float32", "bfloat16", "float16", "int32", "uint16"
-SCRATCH = {"cd": ("dram", [N, 128, 1], F32),
-           "kd": ("dram", [128, 16], I32)}
+SCRATCH = {"cd": ("dram", [N, 128, 1], F32), "kd": ("dram", [128, 16], I32)}
 for _n, _p, _w, _d in (
         ("xb", 128, TC, BF), ("xs", 128, TC + CAP, BF), ("msg", 128, NMAX * CAP, BF), ("rcv", 128, N * CAP, BF),
         ("yb", 128, TC, BF), ("plist", 128, 128, U16), ("off", 128, 16 * NMAX, U16), ("yoff", 128, 128, U16),
@@ -27,7 +25,6 @@ for _n, _w in (("kb", 1024), ("cp", 1024), ("p0", 512), ("p1", 512), ("p2", 512)
 SEMAPHORES = ["sv", "st", "ss", "sg", "lsnd", "cown", "call", "kown", "xarr", "xpart", "xhalf", "data",
               "dk1", "dkd0", "dkd1", "dkt0", "dkt1", "dx0", "dx1", "dcs", "dcb0", "dcb1", "dy0", "dy1"]
 CW = 2
-
 _PLAN = {}
 
 
@@ -39,37 +36,40 @@ def make_plan(cores, topo):
     owners, active, helpers = {}, {}, {}
     for ch in chips:
         far = [c for c in cores if topo.mates(ch, topo.chip(c))][0]
-        here = [c for c in range(NCORES) if topo.chip(c) == ch]
         R = cores[chip_rank[ch]]
-        own = [c for c in here if topo.may_write(c, far)]
+        own = [c for c in range(NCORES) if topo.chip(c) == ch and topo.may_write(c, far)]
         owners[ch] = own
         active[ch] = own if R in own else own + [R]
         helpers[ch] = [c for c in own if c != R]
+    pair_of = {}
+    for ch in chips:
+        if ch not in pair_of:
+            k = len(pair_of) // 2
+            for c2 in chips:
+                if c2 == ch or topo.mates(ch, c2):
+                    pair_of[c2] = k
+    np_ = len(chips) // 2
     msgs, cnts = {}, {}
-    for n, ch in enumerate(chips):
+    for ch in chips:
         R = cores[chip_rank[ch]]
         for c in active[ch]:
             msgs[c], cnts[c] = [], []
-        cross = [d for d in cores if topo.chip(d) != ch and not topo.same_plane(ch, topo.chip(d))]
-        same = [d for d in cores if topo.same_plane(ch, topo.chip(d))]
-        for i, d in enumerate(cross):
-            msgs[owners[ch][(i + n // 2) % len(owners[ch])]].append(d)
-        same = same[n // 2:] + same[:n // 2]
-        order = [c for c in active[ch] if c != R]
-        order = order[n % len(order):] + order[:n % len(order)] + [R]
 
-        def load(c):
-            port = sum(1 for b in order if topo.die(b) == topo.die(c) for e in msgs[b] if topo.same_plane(ch, topo.chip(e)))
-            return port, len(msgs[c])
-        for d in same:
-            msgs[min(order, key=load)].append(d)
-        dst = [d for c2 in chips if c2 != ch for d in active[c2]]
-        for d in dst:
+        def deal(d, die, who):
+            who = [c for c in who if topo.die(c) == die]
+            msgs[min(who, key=lambda c: (len(msgs[c]), c == R))].append(d)
+        turn = [cores[(chip_rank[ch] + i) % N] for i in range(1, N)]
+        for d in turn:
             if not topo.same_plane(ch, topo.chip(d)):
-                cnts[min(owners[ch], key=lambda c: len(cnts[c]))].append(d)
-        for d in dst:
+                deal(d, 1 if (pair_of[ch] + pair_of[topo.chip(d)]) % np_ < np_ // 2 else 0, owners[ch])
+        for d in turn:
             if topo.same_plane(ch, topo.chip(d)):
-                cnts[min(active[ch], key=lambda c: len(cnts[c]))].append(d)
+                deal(d, 0 if (pair_of[ch] + pair_of[topo.chip(d)]) % np_ < np_ // 2 else 1, active[ch])
+        dst = [d for c2 in chips if c2 != ch for d in active[c2]]
+        for same in (False, True):
+            for d in dst:
+                if topo.same_plane(ch, topo.chip(d)) == same:
+                    cnts[min((active if same else owners)[ch], key=lambda c: len(cnts[c]))].append(d)
     _PLAN.update(dict(rank=chip_rank, owners=owners, active=active, helpers=helpers, msgs=msgs, cnts=cnts))
     return _PLAN
 
@@ -100,8 +100,7 @@ def rank_program(g, core, T, topo):
     far = [c for c in cores if topo.same_plane(ch, topo.chip(c))][0]
     eng_off = engines(topo.mask(core, far))
     near = [c for c in P["active"][ch] if c != core][0]
-    eng_on = engines(topo.mask(core, near))
-    eng_rest = [e for e in eng_on if e not in eng_off]
+    eng_rest = [e for e in engines(topo.mask(core, near)) if e not in eng_off]
     Q = {"v": g.vector, "t": g.tensor, "s": g.scalar, "g": g, "y": g.sync}
     cnt, seen, last, readers, totals = {}, {}, {}, {}, {}
 
@@ -189,7 +188,6 @@ def rank_program(g, core, T, topo):
     nd = len(dest)
     n16 = 16 * nd
     chip_eng = eng_off[2 * CW:3 * CW]
-
     if isR:
         dma("y", "dk1", [], ["k1"], T.k1[:], T.key[:])
         dma("s", "dkd0", [], ["kd0"], T.kd[0:64, :], T.key[:, 0:64])
@@ -198,28 +196,30 @@ def rank_program(g, core, T, topo):
         dma("y", "dkt1", [], ["kt1"], T.kt[4:8, :], T.key[:, 64:128])
         dma("y", "dx0", [], ["x0"], T.xb[:, 0:1024], T.x[:, 0:1024])
         dma("y", "dx1", [], ["x1"], T.xb[:, 1024:2048], T.x[:, 1024:2048])
-
     vset("onf", T.onf[:], 1.0)
     vset("ngf", T.ngf[:], -1.0)
     vset("onb", T.onb[:], 1.0)
     vset("zb", T.zb[:], 0.0)
 
     def vector_constants():
-        vset("zf", T.zf[:], 0.0)
-        vset("xpad", T.xs[:, TC:], 0.0)
         vset("lq", T.lq[:], 1.0)
         vset("clc", T.cl[64:128, :], 0.0)
         vset("clc", T.cl[96:97, :], 1.0)
+        if isR:
+            vset("ee", T.ee[:], 0.0)
+        vset("zf", T.zf[:], 0.0)
+        vset("xpad", T.xs[:, TC:], 0.0)
         for j, d in enumerate(dest):
             vset("dc", T.dc[:, 16 * j:16 * j + 16], float(TC * d))
         op("v", "set", [], ["cb0", "cb1"], T.cb[:], 0.0)
         op("v", "set", [], ["cs0", "cs1"], T.cs[:], 0.0)
         if isR:
-            vset("ee", T.ee[:], 0.0)
-            vset("sh", T.sh[:, 0:1], 0.0)
+            vset("sh0", T.sh[:, 0:1], 0.0)
             vset("blk", T.blk[:], 0.0)
             vset("blk", T.blk[0:64, 0:64], 1.0)
             vset("blk", T.blk[64:128, 64:128], 1.0)
+            op("v", "copy", ["pint2"], ["pm3"], T.pm[:, 3:4], T.pint[:, 2:3])
+            op("v", "ts", ["ic", "pm3"], ["ip"], T.ip[:], T.ic[:], 16.0, T.pm[:, 3:4], A.mult, A.add)
 
     def offset_constants():
         iota(T.cl[64:65, 0:n16], "clc", [[0, nd], [16, 16]], 0, 0)
@@ -230,7 +230,6 @@ def rank_program(g, core, T, topo):
     cds = P["cnts"][core]
     half = (len(cds) + 1) // 2
     cnt_trs = [(ds, T.cd[rk], T.cd[rk], eng_off[i * CW:(i + 1) * CW], "call") for i, ds in enumerate([cds[:half], cds[half:]]) if ds]
-
     pairs = [[c for c in helpers if topo.die(c) == die] for die in (0, 1)]
     first = [p[0] for p in pairs]
     later = {p[0]: p[1] for p in pairs if len(p) > 1}
@@ -285,9 +284,10 @@ def rank_program(g, core, T, topo):
         op("v", "copy", ["so", "jv"], ["win"], T.win[:].indirect(T.so[:]), T.jv[:])
         if isR:
             vector_constants()
-        for q in range(16):
-            mm(["zb", "win"], "p1", T.p1[:, 128:256], T.zb[:, 16 - q:144 - q], T.win[:, q::16], q == 0, q == 15)
-        op("v", "copy", ["p1"], ["perm"], T.plist[:], T.p1[:, 128:256])
+        for h, (key, ps) in enumerate((("p1", T.p1[:, 128:192]), ("p0", T.p0[:, 128:192]))):
+            for q in range(16):
+                mm(["zb", "win"], key, ps, T.zb[:, 16 - q:144 - q], T.win[:, 1024 * h + q:1024 * h + 1024:16], q == 0, q == 15)
+            op("v", "copy", [key], ["perm%d" % h], T.plist[:, 64 * h:64 * h + 64], ps)
 
     sort_constants()
     if isR:
@@ -296,12 +296,18 @@ def rank_program(g, core, T, topo):
         for i in range(16):
             op("v", "ts", ["i64", "k1f"], ["oh%d" % i], T.oh[:, 64 * i:64 * i + 64], T.i64[:], T.k1f[:, i:i + 1], None, A.is_equal)
             mm(["onb", "oh%d" % i], "p0", T.p0[0:2, 0:64], T.onb[:, 0:2], T.oh[:, 64 * i:64 * i + 64], i == 0, i == 15)
-        op("v", "copy", ["kt0", "kt1"], ["ktb"], T.ktb[:], T.kt[:])
         op("v", "copy", ["p0"], ["cst"], T.cst[:], T.p0[0:2, 0:64])
         dma("y", "dcs", ["cst"], ["cdown"], T.cd[rk], T.cst[:])
-        fused(["x0"], [(first, x0, x0, eng_rest, "xarr")])
+        op("v", "copy", ["kt0", "kt1"], ["ktb"], T.ktb[:], T.kt[:])
         fused(["cdown"], [(helpers, T.cd[rk], T.cd[rk], chip_eng, "cown")] + cnt_trs)
+        fused(["x0"], [(first, x0, x0, eng_rest, "xarr")])
         fused(["x1"], [(long, x1, x1, eng_off, "xhalf"), (short, x1, x1, eng_rest, "xhalf")])
+        iota(T.ic[:], "ic", [[1, 128]], 0, 0)
+        iota(T.iq[:], "iq", [[0, 8], [1, 16]], 0, 0)
+        aff(T.sh[:, 1:64], "sh", T.onf[:, 0:63], "onf", [[1, 63]], A.is_equal, 64, -1)
+        aff(T.sh[:, 64:128], "sh", T.onf[:, 0:64], "onf", [[1, 64]], A.is_equal, 0, -1)
+        for h in (0, 1):
+            iota(T.yf[64 * h:64 * h + 64, 40:48], "r256", [[CAP, 8]], 8 * CAP * h, 0)
         sort_fills()
         sort_columns()
         offset_constants()
@@ -311,12 +317,7 @@ def rank_program(g, core, T, topo):
             aff(T.ee[p, 0:8], "ee", T.onf[p, 0:8], "onf", [[-1, 8]], A.is_equal, -8 * h, 1)
             aff(T.ee[p, 8:16], "ee", T.ngf[p, 0:8], "ngf", [[-1, 8]], A.is_equal, -8 * h, 1)
             aff(T.ee[p, 16:24], "ee", T.ngf[p, 0:8], "ngf", [[-1, 8]], A.is_ge, -8 * h, 1)
-            iota(T.yf[64 * h:64 * h + 64, 40:48], "r256", [[CAP, 8]], 8 * CAP * h, 0)
-        aff(T.sh[:, 1:64], "sh", T.onf[:, 0:63], "onf", [[1, 63]], A.is_equal, 64, -1)
-        aff(T.sh[:, 64:128], "sh", T.onf[:, 0:64], "onf", [[1, 64]], A.is_equal, 0, -1)
         aff(T.s15[:], "s15", T.onf[:], "onf", [[0, 128]], A.is_equal, -15, 1)
-        iota(T.iq[:], "iq", [[0, 8], [1, 16]], 0, 0)
-        iota(T.ic[:], "ic", [[1, 128]], 0, 0)
     else:
         arrive("kown", CW, ["kd"])
         dma("y", "dkt0", ["kd"], ["kt"], T.kt[:], T.kd[:])
@@ -333,12 +334,20 @@ def rank_program(g, core, T, topo):
             fused(["x0"], [([later[core]], x0, x0, eng_rest, "xpart")])
         arrive("call", 15 * CW, ["cd"])
 
-    def sort_x():
-        op("v", "copy", ["x0", "x1", "perm"], ["xs0"], T.xs[:, 0:1024], T.xb[:].indirect(T.plist[:, 0:64]))
-        op("s", "act", ["x0", "x1", "perm"], ["xs1"], T.xs[:, 1024:2048], T.xb[:].indirect(T.plist[:, 64:128]), F.Copy)
+    def sort_x(q, a, b):
+        r = ["x0", "x1"] + ["perm%d" % h for h in (0, 1) if a < 1024 * (h + 1) and b > 1024 * h]
+        out, src = T.xs[:, a:b], T.xb[:].indirect(T.plist[:, a // 16:b // 16])
+        if q == "v":
+            op("v", "copy", r, ["xs%d" % a], out, src)
+        else:
+            op("s", "act", r, ["xs%d" % a], out, src, F.Copy)
 
+    cut = 1024 if isR else 1280
+    sort_x("s", 0, 1024)
     if isR:
-        sort_x()
+        sort_x("v", cut, TC)
+    else:
+        sort_x("s", 1024, cut)
     dma("y", "dcb0", ["cd", "cdown"], ["cb0"], T.cb[0:16, 0:64], T.cd[:, 0:64, 0])
     if isR:
         dma("y", "dcb1", ["cd", "cdown"], ["cb1"], T.cb[32:48, 64:128], T.cd[:, 0:64, 0])
@@ -352,8 +361,8 @@ def rank_program(g, core, T, topo):
     mm(["lq", "cl", "clc"], "p2", T.p2[:, 64:64 + n16], T.lq[:], T.cl[:, 0:n16])
     op("v", "copy", ["p2"], ["off"], T.off[:, 0:n16], T.p2[:, 64:64 + n16])
     if not isR:
-        sort_x()
-    xr = ["xs0", "xs1", "xpad", "off"]
+        sort_x("v", cut, TC)
+    xr = sorted(set(["xs0", "xs1024", "xs%d" % cut])) + ["xpad", "off"]
 
     def gather(q, out, key, j):
         src = T.xs[:].indirect(T.off[:, 16 * j:16 * j + 16])
@@ -364,7 +373,7 @@ def rank_program(g, core, T, topo):
 
     for call in calls_of(mine, eng_off):
         for j, m, n in call:
-            gather("vs"[j % 2], T.msg[:, CAP * j:CAP * j + CAP], "m%d" % j, j)
+            gather("s" if isR else "vs"[j % 2], T.msg[:, CAP * j:CAP * j + CAP], "m%d" % j, j)
         fused(["m%d" % j for j, m, n in call],
               [([mine[j]], T.msg[:, CAP * j:CAP * j + CAP], T.rcv[:, CAP * rk:CAP * rk + CAP], engines(m), "data") for j, m, n in call])
 
@@ -372,8 +381,6 @@ def rank_program(g, core, T, topo):
         gather("s", T.rcv[:, CAP * rk:CAP * rk + CAP], "own", nd - 1)
         sd, ya, sc, dl, wd, r256, hif, lof, wh, wl = [T.yf[:, 8 * i:8 * i + 8] for i in range(10)]
         sci, hii, loi, wi, whi, wli = [T.ci[:, 8 * i:8 * i + 8] for i in range(6)]
-        op("v", "copy", ["pint2"], ["pm3"], T.pm[:, 3:4], T.pint[:, 2:3])
-        op("v", "ts", ["ic", "pm3"], ["ip"], T.ip[:], T.ic[:], 16.0, T.pm[:, 3:4], A.mult, A.add)
         op("v", "scan", ["cb1", "zf"], ["cs1"], T.cs[32:48, 64:128], T.cb[32:48, 64:128], T.zf[32:48, 0:64], 0.0, A.add, A.add)
         cbk, csk = ["cb0", "cb1", "ee"], ["cs0", "cs1", "ee", "onf"]
         mm(cbk, "p3", T.p3[:, 0:8], T.cb[:], T.ee[:, 0:8])
@@ -385,8 +392,8 @@ def rank_program(g, core, T, topo):
         op("v", "ts", ["sd"], ["ya"], ya, sd, -1.0, 0.0, A.mult, A.max)
         op("v", "tt", ["ya", "p3"], ["ya"], ya, ya, T.p3[:, 0:8], A.min)
         op("v", "copy", ["p3"], ["dl"], dl, T.p3[:, 16:24])
-        op("v", "ts", ["sd"], ["sc"], sc, sd, 0.0, float(TC), A.max, A.min)
         mm(["blk", "ya"], "p3", T.p3[:, 24:32], T.blk[:], ya)
+        op("v", "ts", ["sd"], ["sc"], sc, sd, 0.0, float(TC), A.max, A.min)
         op("v", "copy", ["sc"], ["sci"], sci, sc)
         op("v", "ts", ["sci"], ["hii"], hii, sci, 4, None, A.arith_shift_right)
         op("v", "ts", ["sci"], ["loi"], loi, sci, 15, None, A.bitwise_and)
@@ -396,7 +403,9 @@ def rank_program(g, core, T, topo):
         op("v", "ts", ["dl"], ["dl"], dl, dl, 0.0, float(CAP), A.max, A.min)
         op("v", "tt", ["dl", "sc"], ["dl"], dl, dl, sc, A.subtract)
         op("v", "tt", ["dl", "r256"], ["dl"], dl, dl, r256, A.add)
-        mm(["sh", "dl"], "p3", T.p3[:, 32:33], T.sh[:], T.yf[:, 31:32])
+        mm(["sh", "sh0", "dl"], "p3", T.p3[:, 32:33], T.sh[:], T.yf[:, 31:32])
+        for i in range(4):
+            op("v", "ts", ["iq", "lof"], ["aa%d" % i], T.aa[:, 128 * i:128 * i + 128], T.iq[:], T.yf[:, 56 + i:57 + i], None, A.is_ge)
         op("v", "tt", ["dl"], ["wd"], T.yf[:, 33:40], T.yf[:, 25:32], T.yf[:, 24:31], A.subtract)
         op("v", "tt", ["dl", "p3"], ["wd"], T.yf[:, 32:33], T.yf[:, 24:25], T.p3[:, 32:33], A.subtract)
         op("v", "copy", ["wd"], ["wi"], wi, wd)
@@ -406,7 +415,8 @@ def rank_program(g, core, T, topo):
         op("v", "copy", ["wli"], ["wl"], wl, wli)
         for i in range(8):
             sl = slice(128 * i, 128 * i + 128)
-            op("v", "ts", ["iq", "lof"], ["aa%d" % i], T.aa[:, sl], T.iq[:], T.yf[:, 56 + i:57 + i], None, A.is_ge)
+            if i >= 4:
+                op("v", "ts", ["iq", "lof"], ["aa%d" % i], T.aa[:, sl], T.iq[:], T.yf[:, 56 + i:57 + i], None, A.is_ge)
             for k, part in ((0, "wh"), (1, "wl")):
                 s2 = slice(256 * i + 128 * k, 256 * i + 128 * k + 128)
                 op("v", "ts", ["ic", "hif", part], ["bb%d" % (2 * i + k)], T.bb[:, s2], T.ic[:], T.yf[:, 48 + i:49 + i],
@@ -421,8 +431,7 @@ def rank_program(g, core, T, topo):
         n_in = 0
         for c2 in P["msgs"]:
             if topo.chip(c2) != ch:
-                e2 = engines(topo.mask(c2, R))
-                for call in calls_of(P["msgs"][c2], e2):
+                for call in calls_of(P["msgs"][c2], engines(topo.mask(c2, R))):
                     n_in += sum(n for j, m, n in call if P["msgs"][c2][j] == R)
         arrive("data", n_in, ["rcv"])
         yr = ["rcv", "own", "yoff"]
@@ -431,6 +440,5 @@ def rank_program(g, core, T, topo):
             op("v", "copy", yr, ["ya%d" % h], T.yb[:, a:b], T.rcv[:].indirect(T.yoff[:, o:o + 32]))
             op("s", "act", yr, ["yb%d" % h], T.yb[:, b:b + 512], T.rcv[:].indirect(T.yoff[:, o + 32:o + 64]), F.Copy)
             dma("y", "dy%d" % h, ["ya%d" % h, "yb%d" % h], ["yo%d" % h], T.y[:, a:a + 1024], T.yb[:, a:a + 1024])
-
     for s in sorted(totals):
         wait("g", (s, totals[s]))

@@ -5,26 +5,27 @@ N, TC, KB, CAP = 16, 2048, 64, 256
 NMAX = 5
 NCORES = 128
 F32, BF, FH, I32, U16 = "float32", "bfloat16", "float16", "int32", "uint16"
-SCRATCH = {"cd": ("dram", [N, 128, 1], F32), "kd": ("dram", [128, 16], I32)}
+SCRATCH = {"cd": ("dram", [N, 128, 1], FH), "kd": ("dram", [128, 16], I32)}
 for _n, _p, _w, _d in (
         ("xb", 128, TC, BF), ("xs", 128, TC + CAP, BF), ("msg", 128, NMAX * CAP, BF), ("rcv", 128, N * CAP, BF),
         ("yb", 128, TC, BF), ("plist", 128, 128, U16), ("off", 128, 16 * NMAX, U16), ("yoff", 128, 128, U16),
-        ("cb", 48, 128, F32), ("cs", 48, 128, F32), ("mx", 16, 4, F32), ("dc", 64, 16 * NMAX, F32),
-        ("cl", 128, 16 * NMAX, F32), ("lq", 128, 128, F32), ("zf", 128, 128, F32), ("onf", 128, 128, F32), ("ngf", 128, 8, F32),
+        ("pf", 64, 66, F32), ("pb", 64, 66, FH), ("mxf", 64, 164, F32), ("mx", 64, 164, FH), ("clf", 128, 80, F32),
+        ("cl", 128, 80, FH), ("lqf", 128, 256, F32), ("lq", 128, 256, FH), ("onf", 128, 128, F32), ("ngf", 128, 80, F32),
         ("k1", 128, 16, I32), ("k1f", 128, 16, F32), ("i64", 128, 64, BF), ("oh", 128, 1024, BF), ("onb", 128, 512, BF),
-        ("cst", 2, 64, F32), ("kt", 8, 256, I32), ("ktb", 8, 256, BF), ("sel", 8, 512, BF), ("kcol", 128, 1, F32),
+        ("cst", 2, 64, FH), ("kt", 8, 256, I32), ("ktb", 8, 256, BF), ("sel", 8, 512, BF), ("kcol", 128, 1, F32),
         ("ot", 128, 1024, FH), ("pr", 128, 1024, FH), ("tot", 128, 1, F32), ("wt", 128, 128, F32), ("hm", 128, 2, F32),
         ("hmh", 128, 2, FH), ("ls", 128, 2, FH), ("so", 128, 16, U16), ("win", 128, TC, BF), ("jlo", 128, 16, BF),
-        ("jhi", 128, 16, F32), ("jv", 128, 256, BF), ("zb", 128, 144, BF), ("pint", 128, 3, I32), ("pm", 128, 4, F32),
-        ("ee", 48, 24, F32), ("yf", 128, 80, F32), ("ci", 128, 48, I32), ("blk", 128, 128, F32), ("sh", 128, 128, F32),
-        ("s15", 128, 128, F32), ("iq", 128, 128, BF), ("ic", 128, 128, BF), ("ip", 128, 128, F32), ("aa", 128, 1024, BF),
-        ("bb", 128, 2048, BF), ("ds", 128, 128, F32), ("es", 128, 128, F32)):
+        ("jhi", 128, 16, F32), ("jv", 128, 256, BF), ("zb", 128, 144, BF), ("pint", 128, 3, I32), ("pm", 128, 3, F32),
+        ("eef", 64, 192, F32), ("ee", 64, 192, FH), ("trf", 128, 256, F32), ("tmf", 128, 128, F32), ("tr", 128, 384, FH),
+        ("iq", 128, 128, BF), ("ic", 128, 129, BF), ("sc", 128, 10, FH), ("sci", 128, 16, I32), ("hif", 128, 8, F32),
+        ("aa", 128, 2048, FH), ("zz", 128, 1088, FH)):
     SCRATCH[_n] = ("sbuf", [_p, _w], _d)
 for _n, _w in (("kb", 1024), ("cp", 1024), ("p0", 512), ("p1", 512), ("p2", 512), ("p3", 512)):
     SCRATCH[_n] = ("psum", [128, _w], F32)
 SEMAPHORES = ["sv", "st", "ss", "sg", "lsnd", "cown", "call", "kown", "xarr", "xpart", "xhalf", "data",
-              "dk1", "dkd0", "dkd1", "dkt0", "dkt1", "dx0", "dx1", "dcs", "dcb0", "dcb1", "dy0", "dy1"]
+              "dk1", "dkd0", "dkd1", "dkt0", "dkt1", "dx0", "dx1", "dcs", "dcb", "dy0", "dy1"]
 CW = 2
+SLOT = [2 * r + 1 if r < N // 2 else 2 * (N - 1 - r) for r in range(N)]
 _PLAN = {}
 
 
@@ -100,7 +101,7 @@ def rank_program(g, core, T, topo):
     far = [c for c in cores if topo.same_plane(ch, topo.chip(c))][0]
     eng_off = engines(topo.mask(core, far))
     near = [c for c in P["active"][ch] if c != core][0]
-    eng_rest = [e for e in engines(topo.mask(core, near)) if e not in eng_off]
+    eng_all = engines(topo.mask(core, near))
     Q = {"v": g.vector, "t": g.tensor, "s": g.scalar, "g": g, "y": g.sync}
     cnt, seen, last, readers, totals = {}, {}, {}, {}, {}
 
@@ -187,7 +188,7 @@ def rank_program(g, core, T, topo):
     dest = [cores.index(d) for d in mine] + ([rk] if isR else [])
     nd = len(dest)
     n16 = 16 * nd
-    chip_eng = eng_off[2 * CW:3 * CW]
+    chip_eng = eng_off[2 * CW:4 * CW]
     if isR:
         dma("y", "dk1", [], ["k1"], T.k1[:], T.key[:])
         dma("s", "dkd0", [], ["kd0"], T.kd[0:64, :], T.key[:, 0:64])
@@ -196,36 +197,65 @@ def rank_program(g, core, T, topo):
         dma("y", "dkt1", [], ["kt1"], T.kt[4:8, :], T.key[:, 64:128])
         dma("y", "dx0", [], ["x0"], T.xb[:, 0:1024], T.x[:, 0:1024])
         dma("y", "dx1", [], ["x1"], T.xb[:, 1024:2048], T.x[:, 1024:2048])
+    vset("onb", T.onb[:], 1.0)
+    vset("win", T.win[:], 0.0)
     vset("onf", T.onf[:], 1.0)
     vset("ngf", T.ngf[:], -1.0)
-    vset("onb", T.onb[:], 1.0)
-    vset("zb", T.zb[:], 0.0)
-
-    def vector_constants():
-        vset("lq", T.lq[:], 1.0)
-        vset("clc", T.cl[64:128, :], 0.0)
-        vset("clc", T.cl[96:97, :], 1.0)
-        if isR:
-            vset("ee", T.ee[:], 0.0)
-        vset("zf", T.zf[:], 0.0)
-        vset("xpad", T.xs[:, TC:], 0.0)
-        for j, d in enumerate(dest):
-            vset("dc", T.dc[:, 16 * j:16 * j + 16], float(TC * d))
-        op("v", "set", [], ["cb0", "cb1"], T.cb[:], 0.0)
-        op("v", "set", [], ["cs0", "cs1"], T.cs[:], 0.0)
-        if isR:
-            vset("sh0", T.sh[:, 0:1], 0.0)
-            vset("blk", T.blk[:], 0.0)
-            vset("blk", T.blk[0:64, 0:64], 1.0)
-            vset("blk", T.blk[64:128, 64:128], 1.0)
-            op("v", "copy", ["pint2"], ["pm3"], T.pm[:, 3:4], T.pint[:, 2:3])
-            op("v", "ts", ["ic", "pm3"], ["ip"], T.ip[:], T.ic[:], 16.0, T.pm[:, 3:4], A.mult, A.add)
 
     def offset_constants():
-        iota(T.cl[64:65, 0:n16], "clc", [[0, nd], [16, 16]], 0, 0)
-        iota(T.lq[96:97, :], "lq", [[0, 8], [1, 16]], 0, 0)
-        aff(T.mx[:, 0:1], "mx", T.ngf[0:16, 0:1], "ngf", [[0, 1]], A.is_ge, -rk, 1)
-        aff(T.mx[:, 1:2], "mx", T.onf[0:16, 0:1], "onf", [[0, 1]], A.is_equal, -rk, 1)
+        aff(T.mxf[0:64, 0:n16], "mxf", T.ngf[0:64, 0:n16], "ngf", [[0, n16]], A.is_gt, rk, -1)
+        aff(T.mxf[0:64, 82:82 + n16], "mxf", T.ngf[0:64, 0:n16], "ngf", [[0, n16]], A.is_ge, -rk, 1)
+        aff(T.mxf[0:64, n16:n16 + 1], "mxf", T.onf[0:64, 0:1], "onf", [[0, 1]], A.is_equal, -rk, 1)
+        aff(T.mxf[0:64, 82 + n16:83 + n16], "mxf", T.ngf[0:64, 0:1], "ngf", [[0, 1]], A.is_equal, -rk, 1)
+        aff(T.clf[64:128, 0:n16], "clf", T.onf[64:128, 0:n16], "onf", [[0, n16]], A.is_equal, -32, 1)
+        iota(T.clf[64:65, 0:n16], "clf", [[0, nd], [16, 16]], 0, 0)
+        iota(T.lqf[96:97, 0:128], "lqf", [[0, 8], [1, 16]], 0, 0)
+
+    def offset_fills():
+        vset("pf", T.pf[:], 1.0)
+        vset("pf", T.pf[:, 0:2], 0.0)
+        op("v", "copy", ["pf"], ["pb"], T.pb[:], T.pf[:])
+        vset("xpad", T.xs[:, TC:], 0.0)
+        for j, d in enumerate(dest):
+            vset("mxf", T.mxf[32:33, 16 * j:16 * j + 16], float(TC * d))
+        op("v", "copy", ["mxf"], ["mx"], T.mx[:, 0:n16 + 1], T.mxf[:, 0:n16 + 1])
+        op("v", "copy", ["mxf"], ["mx"], T.mx[:, 82:83 + n16], T.mxf[:, 82:83 + n16])
+        op("v", "copy", ["clf"], ["clc"], T.cl[64:128, 0:n16], T.clf[64:128, 0:n16])
+        op("v", "copy", ["onf"], ["lq"], T.lq[:, 0:128], T.onf[:])
+        op("v", "copy", ["lqf"], ["lq"], T.lq[96:97, 0:128], T.lqf[96:97, 0:128])
+
+    def list_constants():
+        iota(T.iq[:], "iq", [[0, 8], [1, 16]], 0, 0)
+        iota(T.ic[:], "ic", [[16, 129]], 0, 0)
+        aff(T.lqf[64:128, 128:256], "ipf", T.onf[64:128, :], "onf", [[0, 128]], A.is_equal, -32, 1)
+        iota(T.lqf[64:65, 128:256], "ipf", [[16, 128]], 0, 0)
+        for h in (0, 1):
+            r0 = 8 * h - 1
+            aff(T.eef[0:64, 10 * h:10 * h + 10], "eef", T.onf[0:64, 0:10], "onf", [[1, 10]], A.is_gt, r0, -1)
+            aff(T.eef[0:64, 20 + 10 * h:30 + 10 * h], "eef", T.onf[0:64, 0:10], "onf", [[-1, 10]], A.is_ge, -r0, 1)
+        aff(T.eef[0:16, 20:21], "eef", T.onf[0:16, 0:1], "onf", [[0, 1]], A.is_ge, N - 2, -1)
+        aff(T.eef[0:64, 40:50], "eef", T.onf[0:64, 0:10], "onf", [[1, 10]], A.is_equal, N - 1, -1)
+        for h in (0, 1):
+            aff(T.eef[0:64, 64 + 64 * h:128 + 64 * h], "hsf", T.onf[0:64, 0:64], "onf", [[0, 64]], A.is_equal, -32 * h, 1)
+
+    def list_fills():
+        vset("trf", T.trf[:], 0.0)
+        for i, cmp in enumerate((A.is_gt, A.is_ge)):
+            for h in (0, 1):
+                p, c = slice(64 * h, 64 * h + 64), 128 * i + 64 * h
+                aff(T.trf[p, c:c + 64], "trf", T.onf[p, 0:64], "onf", [[1, 64]], cmp, 0, -1)
+        vset("eef", T.eef[32:33, 0:50], -float(TC * rk))
+        for h, p in ((0, slice(0, 64)), (1, slice(32, 33))):
+            vset("hsf", T.eef[p, 56:57], float(CAP * (SLOT[8 * h] - SLOT[8 * h - 1])))
+            vset("hsf", T.eef[p, 57:64], float(CAP * (SLOT[8 * h + 1] - SLOT[8 * h])))
+
+    def list_copies():
+        op("v", "copy", ["eef"], ["ee"], T.ee[:, 0:50], T.eef[:, 0:50])
+        op("v", "copy", ["trf"], ["tr"], T.tr[:, 0:256], T.trf[:])
+        op("v", "tt", ["trf"], ["tmf"], T.tmf[:], T.trf[:, 0:128], T.trf[:, 128:256], A.add)
+        op("v", "copy", ["hsf"], ["hs"], T.ee[:, 56:192], T.eef[:, 56:192])
+        op("v", "copy", ["ipf"], ["ip"], T.lq[64:128, 128:256], T.lqf[64:128, 128:256])
+        op("v", "ts", ["tmf"], ["tr2"], T.tr[:, 256:384], T.tmf[:], -1.0, None, A.mult)
 
     cds = P["cnts"][core]
     half = (len(cds) + 1) // 2
@@ -233,29 +263,17 @@ def rank_program(g, core, T, topo):
     pairs = [[c for c in helpers if topo.die(c) == die] for die in (0, 1)]
     first = [p[0] for p in pairs]
     later = {p[0]: p[1] for p in pairs if len(p) > 1}
-    long = max(pairs, key=len)
-    short = [c for c in helpers if c not in long]
     x0, x1 = [T.xb[:, 1024 * h:1024 * h + 1024] for h in (0, 1)]
 
     def sort_constants():
-        iota(T.i64[:], "i64", [[1, 64]], 0, 0)
         iota(T.pint[:, 0:1], "pint", [[0, 1]], 0, 1, small=False)
+        aff(T.sel[:], "sel", T.onb[0:8, :], "onb", [[-1, 4], [-4, 2], [0, 64]], A.is_equal, 0, 1)
         iota(T.jlo[:], "jlo", [[1, 16]], 0, 1)
         iota(T.jhi[:], "jhi", [[128, 8], [1024, 2]], 0, 0)
-        aff(T.sel[:], "sel", T.onb[0:8, :], "onb", [[-1, 4], [-4, 2], [0, 64]], A.is_equal, 0, 1)
         op("v", "ts", ["pint"], ["pint1"], T.pint[:, 1:2], T.pint[:, 0:1], 63, None, A.bitwise_and)
-        op("v", "ts", ["pint"], ["pint2"], T.pint[:, 2:3], T.pint[:, 0:1], 15, None, A.bitwise_and)
         op("v", "copy", ["pint1"], ["kcol"], T.kcol[:], T.pint[:, 1:2])
-        for i, (v, cmp) in enumerate(((0.0, A.is_equal), (1.0, A.is_equal), (2.0, A.is_lt))):
-            op("v", "ts", ["pint2"], ["pm%d" % i], T.pm[:, i:i + 1], T.pint[:, 2:3], v, None, cmp)
-        op("v", "ts", ["onf", "pm2"], ["zb"], T.zb[:, 0::16], T.onf[:, 0:9], T.pm[:, 2:3], None, A.mult)
-        op("v", "ts", ["jlo", "pm0"], ["jlo"], T.jlo[:], T.jlo[:], T.pm[:, 0:1], None, A.mult)
-        op("v", "ts", ["jhi", "pm1"], ["jhi"], T.jhi[:], T.jhi[:], T.pm[:, 1:2], None, A.mult)
-        for i in range(16):
-            op("s", "act", ["jlo", "jhi"], ["jv"], T.jv[:, 16 * i:16 * i + 16], T.jlo[:], F.Identity, T.jhi[:, i:i + 1], acc=True)
 
     def sort_fills():
-        vset("win", T.win[:], 0.0)
         vset("hm", T.hm[:], 0.0)
         vset("hm", T.hm[0:64, 0:1], 1.0)
         vset("hm", T.hm[64:128, 1:2], 1.0)
@@ -263,12 +281,22 @@ def rank_program(g, core, T, topo):
         for b in (0, 64):
             op("v", "ts", ["i64", "kcol"], ["wt"], T.wt[:, b:b + 64], T.i64[:], T.kcol[:], None, A.is_gt)
         op("v", "ts", ["i64", "kcol"], ["wt"], T.wt[0:64, 64:128], T.i64[0:64, :], T.kcol[0:64, :], None, A.is_ge)
+        vset("zb", T.zb[:], 0.0)
+        op("v", "ts", ["pint"], ["pint2"], T.pint[:, 2:3], T.pint[:, 0:1], 15, None, A.bitwise_and)
+        for i, (v, cmp) in enumerate(((0.0, A.is_equal), (1.0, A.is_equal), (2.0, A.is_lt))):
+            op("v", "ts", ["pint2"], ["pm%d" % i], T.pm[:, i:i + 1], T.pint[:, 2:3], v, None, cmp)
+        op("v", "ts", ["jlo", "pm0"], ["jlo"], T.jlo[:], T.jlo[:], T.pm[:, 0:1], None, A.mult)
+        op("v", "ts", ["jhi", "pm1"], ["jhi"], T.jhi[:], T.jhi[:], T.pm[:, 1:2], None, A.mult)
+        op("v", "ts", ["onf", "pm2"], ["zb"], T.zb[:, 0::16], T.onf[:, 0:9], T.pm[:, 2:3], None, A.mult)
+        for i in range(16):
+            op("s", "act", ["jlo", "jhi"], ["jv"], T.jv[:, 16 * i:16 * i + 16], T.jlo[:], F.Identity, T.jhi[:, i:i + 1], acc=True)
 
     def sort_columns():
         for a in range(4):
-            mm(["sel", "ktb"], "kb%d" % (a // 2), T.kb[:, 256 * a:256 * a + 256], T.sel[:, 128 * a:128 * a + 128], T.ktb[:])
-        for q in range(16):
-            op("v", "ts", ["kb%d" % (q // 8), "kcol"], ["ot"], T.ot[:, q::16], T.kb[:, 64 * q:64 * q + 64], T.kcol[:], None, A.is_equal, acc=True)
+            kq = [T.p0, T.p1, T.p2, T.p3][a]
+            mm(["sel", "ktb"], "p%d" % a, kq[:, 0:256], T.sel[:, 128 * a:128 * a + 128], T.ktb[:])
+            for q in range(4):
+                op("v", "ts", ["p%d" % a, "kcol"], ["ot"], T.ot[:, 4 * a + q::16], kq[:, 64 * q:64 * q + 64], T.kcol[:], None, A.is_equal, acc=True)
         op("v", "scan", ["ot"], ["cp"], T.cp[:], T.ot[:], T.ot[:], 0.0, A.add, A.max)
         op("v", "copy", ["cp"], ["tot"], T.tot[:], T.cp[:, 1023:1024])
         mm(["wt", "tot"], "p0", T.p0[:, 64:65], T.wt[:], T.tot[:])
@@ -283,86 +311,89 @@ def rank_program(g, core, T, topo):
         op("v", "ts", ["p1"], ["so"], T.so[:], T.p1[:, 0:16], -1.0, None, A.add)
         op("v", "copy", ["so", "jv"], ["win"], T.win[:].indirect(T.so[:]), T.jv[:])
         if isR:
-            vector_constants()
+            offset_fills()
+            list_fills()
         for h, (key, ps) in enumerate((("p1", T.p1[:, 128:192]), ("p0", T.p0[:, 128:192]))):
             for q in range(16):
                 mm(["zb", "win"], key, ps, T.zb[:, 16 - q:144 - q], T.win[:, 1024 * h + q:1024 * h + 1024:16], q == 0, q == 15)
             op("v", "copy", [key], ["perm%d" % h], T.plist[:, 64 * h:64 * h + 64], ps)
+            if h == 0 and not isR:
+                places()
+                sort_x("v", 0, 512)
+                sort_x("s", 512, 1024)
 
-    sort_constants()
-    if isR:
-        fused(["kd0", "kd1"], [(helpers, T.kd[:], T.kd[:], chip_eng, "kown")])
-        op("v", "copy", ["k1"], ["k1f"], T.k1f[:], T.k1[:])
-        for i in range(16):
-            op("v", "ts", ["i64", "k1f"], ["oh%d" % i], T.oh[:, 64 * i:64 * i + 64], T.i64[:], T.k1f[:, i:i + 1], None, A.is_equal)
-            mm(["onb", "oh%d" % i], "p0", T.p0[0:2, 0:64], T.onb[:, 0:2], T.oh[:, 64 * i:64 * i + 64], i == 0, i == 15)
-        op("v", "copy", ["p0"], ["cst"], T.cst[:], T.p0[0:2, 0:64])
-        dma("y", "dcs", ["cst"], ["cdown"], T.cd[rk], T.cst[:])
-        op("v", "copy", ["kt0", "kt1"], ["ktb"], T.ktb[:], T.kt[:])
-        fused(["cdown"], [(helpers, T.cd[rk], T.cd[rk], chip_eng, "cown")] + cnt_trs)
-        fused(["x0"], [(first, x0, x0, eng_rest, "xarr")])
-        fused(["x1"], [(long, x1, x1, eng_off, "xhalf"), (short, x1, x1, eng_rest, "xhalf")])
-        iota(T.ic[:], "ic", [[1, 128]], 0, 0)
-        iota(T.iq[:], "iq", [[0, 8], [1, 16]], 0, 0)
-        aff(T.sh[:, 1:64], "sh", T.onf[:, 0:63], "onf", [[1, 63]], A.is_equal, 64, -1)
-        aff(T.sh[:, 64:128], "sh", T.onf[:, 0:64], "onf", [[1, 64]], A.is_equal, 0, -1)
-        for h in (0, 1):
-            iota(T.yf[64 * h:64 * h + 64, 40:48], "r256", [[CAP, 8]], 8 * CAP * h, 0)
-        sort_fills()
-        sort_columns()
-        offset_constants()
-        arrive("call", 15 * CW, ["cd"])
-        for h in (0, 1):
-            p = slice(32 * h, 32 * h + 16)
-            aff(T.ee[p, 0:8], "ee", T.onf[p, 0:8], "onf", [[-1, 8]], A.is_equal, -8 * h, 1)
-            aff(T.ee[p, 8:16], "ee", T.ngf[p, 0:8], "ngf", [[-1, 8]], A.is_equal, -8 * h, 1)
-            aff(T.ee[p, 16:24], "ee", T.ngf[p, 0:8], "ngf", [[-1, 8]], A.is_ge, -8 * h, 1)
-        aff(T.s15[:], "s15", T.onf[:], "onf", [[0, 128]], A.is_equal, -15, 1)
-    else:
-        arrive("kown", CW, ["kd"])
-        dma("y", "dkt0", ["kd"], ["kt"], T.kt[:], T.kd[:])
-        sort_fills()
-        vector_constants()
-        offset_constants()
-        op("v", "copy", ["kt"], ["ktb"], T.ktb[:], T.kt[:])
-        sort_columns()
-        arrive("cown", CW, ["cdown"])
-        fused(["cdown"], cnt_trs)
-        arrive("xarr" if core in first else "xpart", len(eng_rest), ["x0"])
-        arrive("xhalf", len(eng_off if core in long else eng_rest), ["x1"])
-        if core in later:
-            fused(["x0"], [([later[core]], x0, x0, eng_rest, "xpart")])
-        arrive("call", 15 * CW, ["cd"])
+    xs_parts = []
 
     def sort_x(q, a, b):
         r = ["x0", "x1"] + ["perm%d" % h for h in (0, 1) if a < 1024 * (h + 1) and b > 1024 * h]
         out, src = T.xs[:, a:b], T.xb[:].indirect(T.plist[:, a // 16:b // 16])
+        xs_parts.append("xs%d" % a)
         if q == "v":
             op("v", "copy", r, ["xs%d" % a], out, src)
         else:
             op("s", "act", r, ["xs%d" % a], out, src, F.Copy)
 
-    cut = 1024 if isR else 1280
-    sort_x("s", 0, 1024)
+    upto, below, below2 = T.pb[0:33, 2:66], T.pb[0:16, 1:65], T.pb[0:16, 0:64]
+
+    def places():
+        mm(["cb", "mx"], "p2", T.p2[0:64, 0:n16 + 1], upto, T.mx[0:33, 0:n16 + 1], True, False)
+        mm(["cb", "mx"], "p2", T.p2[0:64, 0:n16 + 1], below, T.mx[0:16, 82:83 + n16], False, True)
+        op("v", "ts", ["p2"], ["cl"], T.cl[0:64, 0:n16], T.p2[0:64, 0:n16], 0.0, T.p2[0:64, n16:n16 + 1], A.max, A.min)
+
+    def starts():
+        mm(["lq", "cl", "clc"], "p2", T.p2[:, 128:128 + n16], T.lq[:, 0:128], T.cl[:, 0:n16])
+        op("v", "copy", ["p2"], ["off"], T.off[:, 0:n16], T.p2[:, 128:128 + n16])
+
+    def load_counts():
+        arrive("call", 15 * CW, ["cd"])
+        dma("y", "dcb", ["cd", "cdown", "pb"], ["cb"], T.pb[0:16, 2:66], T.cd[:, 0:64, 0])
+
+    iota(T.i64[:], "i64", [[1, 64]], 0, 0)
     if isR:
-        sort_x("v", cut, TC)
+        fused(["kd0", "kd1"], [(helpers, T.kd[:], T.kd[:], chip_eng, "kown")])
+        op("v", "copy", ["k1"], ["k1f"], T.k1f[:], T.k1[:])
+        for i in range(16):
+            op("v", "ts", ["i64", "k1f"], ["oh%d" % i], T.oh[:, 64 * i:64 * i + 64], T.i64[:], T.k1f[:, i:i + 1], None, A.is_ge)
+            mm(["onb", "oh%d" % i], "p0", T.p0[0:2, 0:64], T.onb[:, 0:2], T.oh[:, 64 * i:64 * i + 64], i == 0, i == 15)
+        op("v", "copy", ["p0"], ["cst"], T.cst[:], T.p0[0:2, 0:64])
+        dma("y", "dcs", ["cst"], ["cdown"], T.cd[rk], T.cst[:])
+        sort_constants()
+        op("v", "copy", ["kt0", "kt1"], ["ktb"], T.ktb[:], T.kt[:])
+        fused(["cdown"], [(helpers, T.cd[rk], T.cd[rk], chip_eng, "cown")] + cnt_trs)
+        fused(["x0"], [(first, x0, x0, eng_all, "xarr")])
+        fused(["x1"], [(helpers, x1, x1, eng_all, "xhalf")])
+        sort_fills()
+        offset_constants()
+        list_constants()
+        sort_columns()
     else:
-        sort_x("s", 1024, cut)
-    dma("y", "dcb0", ["cd", "cdown"], ["cb0"], T.cb[0:16, 0:64], T.cd[:, 0:64, 0])
+        sort_constants()
+        arrive("kown", len(chip_eng), ["kd"])
+        dma("y", "dkt0", ["kd"], ["kt"], T.kt[:], T.kd[:])
+        sort_fills()
+        offset_constants()
+        offset_fills()
+        op("v", "copy", ["kt"], ["ktb"], T.ktb[:], T.kt[:])
+        arrive("cown", len(chip_eng), ["cdown"])
+        arrive("xarr" if core in first else "xpart", len(eng_all), ["x0"])
+        arrive("xhalf", len(eng_all), ["x1"])
+        fused(["cdown"], cnt_trs)
+        load_counts()
+        if core in later:
+            fused(["x0"], [([later[core]], x0, x0, eng_all, "xpart")])
+        sort_columns()
+
     if isR:
-        dma("y", "dcb1", ["cd", "cdown"], ["cb1"], T.cb[32:48, 64:128], T.cd[:, 0:64, 0])
-    ct, cs = T.cb[0:16, 0:64], T.cs[0:16, 0:64]
-    op("v", "scan", ["cb0", "zf"], ["cs0"], cs, ct, T.zf[0:16, 0:64], 0.0, A.add, A.add)
-    mm(["cb0", "mx"], "p2", T.p2[0:64, 1:2], ct, T.mx[:, 1:2])
-    mm(["cb0", "mx"], "p2", T.p2[0:64, 0:1], ct, T.mx[:, 0:1], True, False)
-    mm(["cs0", "onf"], "p2", T.p2[0:64, 0:1], cs, T.onf[0:16, 0:1], False, True)
-    op("v", "ts", ["dc", "p2"], ["cl"], T.cl[0:64, 0:n16], T.dc[:, 0:n16], T.p2[0:64, 0:1], T.p2[0:64, 1:2], A.subtract, A.min)
-    op("v", "ts", ["cl"], ["cl"], T.cl[0:64, 0:n16], T.cl[0:64, 0:n16], 0.0, None, A.max)
-    mm(["lq", "cl", "clc"], "p2", T.p2[:, 64:64 + n16], T.lq[:], T.cl[:, 0:n16])
-    op("v", "copy", ["p2"], ["off"], T.off[:, 0:n16], T.p2[:, 64:64 + n16])
-    if not isR:
-        sort_x("v", cut, TC)
-    xr = sorted(set(["xs0", "xs1024", "xs%d" % cut])) + ["xpad", "off"]
+        sort_x("s", 0, 1024)
+        sort_x("v", 1024, TC)
+        load_counts()
+        places()
+        starts()
+    else:
+        starts()
+        sort_x("s", 1024, 1536)
+        sort_x("v", 1536, TC)
+    xr = xs_parts + ["xpad", "off"]
 
     def gather(q, out, key, j):
         src = T.xs[:].indirect(T.off[:, 16 * j:16 * j + 16])
@@ -373,61 +404,38 @@ def rank_program(g, core, T, topo):
 
     for call in calls_of(mine, eng_off):
         for j, m, n in call:
-            gather("s" if isR else "vs"[j % 2], T.msg[:, CAP * j:CAP * j + CAP], "m%d" % j, j)
+            on_v = j == 1 if isR else j % 2 == 0
+            gather("v" if on_v else "s", T.msg[:, CAP * j:CAP * j + CAP], "m%d" % j, j)
         fused(["m%d" % j for j, m, n in call],
-              [([mine[j]], T.msg[:, CAP * j:CAP * j + CAP], T.rcv[:, CAP * rk:CAP * rk + CAP], engines(m), "data") for j, m, n in call])
+              [([mine[j]], T.msg[:, CAP * j:CAP * j + CAP], T.rcv[:, CAP * SLOT[rk]:CAP * SLOT[rk] + CAP], engines(m), "data") for j, m, n in call])
 
     if isR:
-        gather("s", T.rcv[:, CAP * rk:CAP * rk + CAP], "own", nd - 1)
-        sd, ya, sc, dl, wd, r256, hif, lof, wh, wl = [T.yf[:, 8 * i:8 * i + 8] for i in range(10)]
-        sci, hii, loi, wi, whi, wli = [T.ci[:, 8 * i:8 * i + 8] for i in range(6)]
-        op("v", "scan", ["cb1", "zf"], ["cs1"], T.cs[32:48, 64:128], T.cb[32:48, 64:128], T.zf[32:48, 0:64], 0.0, A.add, A.add)
-        cbk, csk = ["cb0", "cb1", "ee"], ["cs0", "cs1", "ee", "onf"]
-        mm(cbk, "p3", T.p3[:, 0:8], T.cb[:], T.ee[:, 0:8])
-        mm(cbk, "p3", T.p3[:, 8:16], T.cb[:], T.ee[:, 16:24], True, False)
-        mm(csk, "p3", T.p3[:, 8:16], T.cs[:], T.onf[0:48, 0:8], False, True)
-        mm(cbk, "p3", T.p3[:, 16:24], T.cb[:], T.ee[:, 8:16], True, False)
-        mm(csk, "p3", T.p3[:, 16:24], T.cs[:], T.ee[:, 0:8], False, True)
-        op("v", "ts", ["p3"], ["sd"], sd, T.p3[:, 8:16], -float(TC * rk), None, A.add)
-        op("v", "ts", ["sd"], ["ya"], ya, sd, -1.0, 0.0, A.mult, A.max)
-        op("v", "tt", ["ya", "p3"], ["ya"], ya, ya, T.p3[:, 0:8], A.min)
-        op("v", "copy", ["p3"], ["dl"], dl, T.p3[:, 16:24])
-        mm(["blk", "ya"], "p3", T.p3[:, 24:32], T.blk[:], ya)
-        op("v", "ts", ["sd"], ["sc"], sc, sd, 0.0, float(TC), A.max, A.min)
-        op("v", "copy", ["sc"], ["sci"], sci, sc)
-        op("v", "ts", ["sci"], ["hii"], hii, sci, 4, None, A.arith_shift_right)
-        op("v", "ts", ["sci"], ["loi"], loi, sci, 15, None, A.bitwise_and)
-        op("v", "copy", ["hii"], ["hif"], hif, hii)
-        op("v", "copy", ["loi"], ["lof"], lof, loi)
-        op("v", "tt", ["dl", "p3"], ["dl"], dl, dl, T.p3[:, 24:32], A.subtract)
-        op("v", "ts", ["dl"], ["dl"], dl, dl, 0.0, float(CAP), A.max, A.min)
-        op("v", "tt", ["dl", "sc"], ["dl"], dl, dl, sc, A.subtract)
-        op("v", "tt", ["dl", "r256"], ["dl"], dl, dl, r256, A.add)
-        mm(["sh", "sh0", "dl"], "p3", T.p3[:, 32:33], T.sh[:], T.yf[:, 31:32])
-        for i in range(4):
-            op("v", "ts", ["iq", "lof"], ["aa%d" % i], T.aa[:, 128 * i:128 * i + 128], T.iq[:], T.yf[:, 56 + i:57 + i], None, A.is_ge)
-        op("v", "tt", ["dl"], ["wd"], T.yf[:, 33:40], T.yf[:, 25:32], T.yf[:, 24:31], A.subtract)
-        op("v", "tt", ["dl", "p3"], ["wd"], T.yf[:, 32:33], T.yf[:, 24:25], T.p3[:, 32:33], A.subtract)
-        op("v", "copy", ["wd"], ["wi"], wi, wd)
-        op("v", "ts", ["wi"], ["whi"], whi, wi, 6, None, A.arith_shift_right)
-        op("v", "ts", ["wi"], ["wli"], wli, wi, 63, None, A.bitwise_and)
-        op("v", "ts", ["whi"], ["wh"], wh, whi, 64.0, None, A.mult)
-        op("v", "copy", ["wli"], ["wl"], wl, wli)
+        gather("s", T.rcv[:, CAP * SLOT[rk]:CAP * SLOT[rk] + CAP], "own", nd - 1)
+        list_copies()
+        mm(["cb", "ee"], "p3", T.p3[0:64, 0:10], upto, T.ee[0:33, 0:10], True, False)
+        mm(["cb", "ee"], "p3", T.p3[0:64, 0:10], below, T.ee[0:16, 20:30], False, False)
+        mm(["cb", "ee"], "p3", T.p3[0:64, 0:10], below2, T.ee[0:16, 40:50], False, True)
+        mm(["cb", "ee"], "p3", T.p3[64:128, 0:10], upto, T.ee[0:33, 10:20], True, False)
+        mm(["cb", "ee"], "p3", T.p3[64:128, 0:10], below, T.ee[0:16, 30:40], False, True)
+        op("v", "ts", ["p3"], ["sc"], T.sc[:], T.p3[:, 0:10], 0.0, float(TC), A.max, A.min)
+        op("v", "ts", ["p3"], ["sci"], T.sci[:, 0:8], T.p3[:, 1:9], 0.0, float(TC), A.max, A.min)
+        op("v", "ts", ["sci"], ["scm"], T.sci[:, 8:16], T.sci[:, 0:8], 2 * TC - 16, None, A.bitwise_and)
+        op("v", "copy", ["scm"], ["hif"], T.hif[:], T.sci[:, 8:16])
+        mm(["hs"], "cp", T.cp[:, 0:8], T.ee[0:33, 64:192], T.ee[0:33, 56:64], True, False)
+        mm(["tr", "sc"], "cp", T.cp[:, 0:8], T.tr[:, 0:128], T.sc[:, 2:10], False, False)
+        mm(["tr", "sc"], "cp", T.cp[:, 0:8], T.tr[:, 128:256], T.sc[:, 0:8], False, False)
+        mm(["tr2", "sc"], "cp", T.cp[:, 0:8], T.tr[:, 256:384], T.sc[:, 1:9], False, True)
+        mm(["lq", "ip"], "kb", T.kb[:, 0:128], T.lq[64:128, 0:128], T.lq[64:128, 128:256], True, False)
         for i in range(8):
-            sl = slice(128 * i, 128 * i + 128)
-            if i >= 4:
-                op("v", "ts", ["iq", "lof"], ["aa%d" % i], T.aa[:, sl], T.iq[:], T.yf[:, 56 + i:57 + i], None, A.is_ge)
-            for k, part in ((0, "wh"), (1, "wl")):
-                s2 = slice(256 * i + 128 * k, 256 * i + 128 * k + 128)
-                op("v", "ts", ["ic", "hif", part], ["bb%d" % (2 * i + k)], T.bb[:, s2], T.ic[:], T.yf[:, 48 + i:49 + i],
-                   T.yf[:, 64 + 8 * k + i:65 + 8 * k + i], A.is_equal, A.mult)
-                mm(["aa%d" % i, "bb%d" % (2 * i + k)], "kb0", T.kb[:, 0:128], T.aa[:, sl], T.bb[:, s2], i + k == 0, i + k == 8)
-        op("v", "copy", ["kb0"], ["ds"], T.ds[:], T.kb[:, 0:128])
-        mm(["s15", "ds"], "cp", T.cp[:, 0:128], T.s15[:], T.ds[:])
-        op("v", "tt", ["ds", "ip"], ["ip"], T.ip[:], T.ds[:], T.ip[:], A.add)
-        op("v", "scan", ["cp", "zf"], ["es"], T.es[:], T.cp[:, 0:128], T.zf[:], 0.0, A.add, A.add)
-        op("v", "tt", ["ip", "es"], ["ip"], T.ip[:, 1:128], T.ip[:, 1:128], T.es[:, 0:127], A.add)
-        op("v", "copy", ["ip"], ["yoff"], T.yoff[:], T.ip[:])
+            a0, z0 = 256 * i, 136 * i
+            na, ya, zi = T.aa[:, a0:a0 + 128], T.aa[:, a0 + 128:a0 + 256], T.zz[:, z0:z0 + 129]
+            hi, pl, st = T.hif[:, i:i + 1], T.p3[:, 1 + i:2 + i], T.cp[:, i:i + 1]
+            op("v", "ts", ["iq", "hif", "p3"], ["na%d" % i], na, T.iq[:], hi, pl, A.add, A.is_lt)
+            op("v", "ts", ["iq", "hif", "p3"], ["ya%d" % i], ya, T.iq[:], hi, pl, A.add, A.is_ge)
+            op("v", "ts", ["ic", "hif", "cp"], ["zz%d" % i], zi, T.ic[:], hi, st, A.is_gt, A.mult)
+            mm(["na%d" % i, "zz%d" % i], "kb", T.kb[:, 0:128], na, T.zz[:, z0:z0 + 128], False, False)
+            mm(["ya%d" % i, "zz%d" % i], "kb", T.kb[:, 0:128], ya, T.zz[:, z0 + 1:z0 + 129], False, i == 7)
+        op("v", "copy", ["kb"], ["yoff"], T.yoff[:], T.kb[:, 0:128])
         n_in = 0
         for c2 in P["msgs"]:
             if topo.chip(c2) != ch:
@@ -437,8 +445,8 @@ def rank_program(g, core, T, topo):
         yr = ["rcv", "own", "yoff"]
         for h in (0, 1):
             a, b, o = 1024 * h, 1024 * h + 512, 64 * h
-            op("v", "copy", yr, ["ya%d" % h], T.yb[:, a:b], T.rcv[:].indirect(T.yoff[:, o:o + 32]))
-            op("s", "act", yr, ["yb%d" % h], T.yb[:, b:b + 512], T.rcv[:].indirect(T.yoff[:, o + 32:o + 64]), F.Copy)
-            dma("y", "dy%d" % h, ["ya%d" % h, "yb%d" % h], ["yo%d" % h], T.y[:, a:a + 1024], T.yb[:, a:a + 1024])
+            op("v", "copy", yr, ["yl%d" % h], T.yb[:, a:b], T.rcv[:].indirect(T.yoff[:, o:o + 32]))
+            op("s", "act", yr, ["yr%d" % h], T.yb[:, b:b + 512], T.rcv[:].indirect(T.yoff[:, o + 32:o + 64]), F.Copy)
+            dma("y", "dy%d" % h, ["yl%d" % h, "yr%d" % h], ["yo%d" % h], T.y[:, a:a + 1024], T.yb[:, a:a + 1024])
     for s in sorted(totals):
         wait("g", (s, totals[s]))

@@ -2,30 +2,31 @@ from concourse.bass import DstId, RemoteDMATransfer
 from concourse.mybir import AluOpType as A, AxisListType, ActivationFunctionType as F
 
 N, TC, KB, CAP = 16, 2048, 64, 256
-NMAX = 5
+NMAX = 4
 NCORES = 128
 F32, BF, FH, I32, U16 = "float32", "bfloat16", "float16", "int32", "uint16"
-SCRATCH = {"cd": ("dram", [N, 128, 1], FH), "kd": ("dram", [128, 16], I32)}
+OMA, OMB, OCL, OLQ, OPB, OCW = 0, 66, 132, 196, 324, 390
+LHS, LTR, LIP, LIQ, LIC, LCW = 56, 192, 576, 704, 832, 962
+SCRATCH = {"cd": ("dram", [N, 128, 1], FH)}
 for _n, _p, _w, _d in (
         ("xb", 128, TC, BF), ("xs", 128, TC + CAP, BF), ("msg", 128, NMAX * CAP, BF), ("rcv", 128, N * CAP, BF),
         ("yb", 128, TC, BF), ("plist", 128, 128, U16), ("off", 128, 16 * NMAX, U16), ("yoff", 128, 128, U16),
-        ("pf", 64, 66, F32), ("pb", 64, 66, FH), ("mxf", 64, 164, F32), ("mx", 64, 164, FH), ("clf", 128, 80, F32),
-        ("cl", 128, 80, FH), ("lqf", 128, 256, F32), ("lq", 128, 256, FH), ("onf", 128, 128, F32), ("ngf", 128, 80, F32),
-        ("k1", 128, 16, I32), ("k1f", 128, 16, F32), ("i64", 128, 64, BF), ("oh", 128, 1024, BF), ("onb", 128, 512, BF),
-        ("cst", 2, 64, FH), ("kt", 8, 256, I32), ("ktb", 8, 256, BF), ("sel", 8, 512, BF), ("kcol", 128, 1, F32),
-        ("ot", 128, 1024, FH), ("pr", 128, 1024, FH), ("tot", 128, 1, F32), ("wt", 128, 128, F32), ("hm", 128, 2, F32),
-        ("hmh", 128, 2, FH), ("ls", 128, 2, FH), ("so", 128, 16, U16), ("win", 128, TC, BF), ("jlo", 128, 16, BF),
-        ("jhi", 128, 16, F32), ("jv", 128, 256, BF), ("zb", 128, 144, BF), ("pint", 128, 3, I32), ("pm", 128, 3, F32),
-        ("eef", 64, 192, F32), ("ee", 64, 192, FH), ("trf", 128, 256, F32), ("tmf", 128, 128, F32), ("tr", 128, 384, FH),
-        ("iq", 128, 128, BF), ("ic", 128, 129, BF), ("sc", 128, 10, FH), ("sci", 128, 16, I32), ("hif", 128, 8, F32),
-        ("aa", 128, 2048, FH), ("zz", 128, 1088, FH)):
+        ("ocf", 128, OCW, F32), ("oc", 128, OCW, FH), ("lcf", 128, LCW, F32), ("lc", 128, LCW, FH),
+        ("onf", 128, 128, F32), ("ngf", 64, 80, F32),
+        ("kt", 8, 256, I32), ("ktb", 8, 256, BF), ("hs8", 8, 128, BF), ("sel", 8, 512, BF), ("kcol", 128, 1, F32),
+        ("i65", 128, 66, BF), ("w1", 128, 66, FH), ("w2", 128, 64, FH), ("cst", 2, 64, FH), ("hmh", 128, 2, FH),
+        ("ot", 128, 1024, FH), ("cp", 128, 1024, FH), ("pr", 128, 1024, FH), ("ls", 128, 2, FH), ("so", 128, 16, U16),
+        ("win", 128, TC, BF), ("one9", 128, 9, F32), ("jlo", 128, 16, BF), ("jhi", 128, 16, F32), ("jv", 128, 256, BF),
+        ("zb", 128, 144, BF), ("pint", 128, 3, I32), ("pm", 128, 3, F32),
+        ("sc", 128, 10, FH), ("sci", 128, 16, I32), ("hif", 128, 8, F32), ("aa", 128, 2048, FH), ("zz", 128, 1088, FH)):
     SCRATCH[_n] = ("sbuf", [_p, _w], _d)
-for _n, _w in (("kb", 1024), ("cp", 1024), ("p0", 512), ("p1", 512), ("p2", 512), ("p3", 512)):
-    SCRATCH[_n] = ("psum", [128, _w], F32)
-SEMAPHORES = ["sv", "st", "ss", "sg", "lsnd", "cown", "call", "kown", "xarr", "xpart", "xhalf", "data",
-              "dk1", "dkd0", "dkd1", "dkt0", "dkt1", "dx0", "dx1", "dcs", "dcb", "dy0", "dy1"]
+for _i in range(8):
+    SCRATCH["p%d" % _i] = ("psum", [128, 512], F32)
+SEMAPHORES = ["sv", "st", "ss", "sg", "lsnd", "cown", "call", "xh0", "xh1", "soar", "kc0", "kc1", "kc2", "data",
+              "dkt0", "dkt1", "dx0", "dx1", "dcs", "dcb", "dy0", "dy1", "dy2"]
 CW = 2
 SLOT = [2 * r + 1 if r < N // 2 else 2 * (N - 1 - r) for r in range(N)]
+YPART = [0, 1024, 1536, 2048]
 _PLAN = {}
 
 
@@ -34,14 +35,20 @@ def make_plan(cores, topo):
         return _PLAN
     chip_rank = {topo.chip(c): r for r, c in enumerate(cores)}
     chips = sorted(chip_rank)
-    owners, active, helpers = {}, {}, {}
+    owners, senders, consts = {}, {}, {}
     for ch in chips:
         far = [c for c in cores if topo.mates(ch, topo.chip(c))][0]
         R = cores[chip_rank[ch]]
-        own = [c for c in range(NCORES) if topo.chip(c) == ch and topo.may_write(c, far)]
-        owners[ch] = own
-        active[ch] = own if R in own else own + [R]
-        helpers[ch] = [c for c in own if c != R]
+        here = [c for c in range(NCORES) if topo.chip(c) == ch and c != R]
+        here.sort(key=lambda c: topo.die(c) != topo.die(R))
+        own = [c for c in here if topo.may_write(c, far)]
+        rest = [c for c in here if c not in own]
+        near = [c for c in own if topo.die(c) == topo.die(R)]
+        if topo.may_write(R, far):
+            near.append(rest.pop(0))
+        senders[ch] = [c for p in zip(near, [c for c in own if c not in near]) for c in p]
+        owners[ch] = [c for c in senders[ch] if c in own]
+        consts[ch] = rest[:3]
     pair_of = {}
     for ch in chips:
         if ch not in pair_of:
@@ -53,25 +60,24 @@ def make_plan(cores, topo):
     msgs, cnts = {}, {}
     for ch in chips:
         R = cores[chip_rank[ch]]
-        for c in active[ch]:
+        for c in senders[ch] + [R]:
             msgs[c], cnts[c] = [], []
 
         def deal(d, die, who):
             who = [c for c in who if topo.die(c) == die]
-            msgs[min(who, key=lambda c: (len(msgs[c]), c == R))].append(d)
+            msgs[min(who, key=lambda c: len(msgs[c]))].append(d)
         turn = [cores[(chip_rank[ch] + i) % N] for i in range(1, N)]
         for d in turn:
             if not topo.same_plane(ch, topo.chip(d)):
                 deal(d, 1 if (pair_of[ch] + pair_of[topo.chip(d)]) % np_ < np_ // 2 else 0, owners[ch])
         for d in turn:
             if topo.same_plane(ch, topo.chip(d)):
-                deal(d, 0 if (pair_of[ch] + pair_of[topo.chip(d)]) % np_ < np_ // 2 else 1, active[ch])
-        dst = [d for c2 in chips if c2 != ch for d in active[c2]]
-        for same in (False, True):
-            for d in dst:
-                if topo.same_plane(ch, topo.chip(d)) == same:
-                    cnts[min((active if same else owners)[ch], key=lambda c: len(cnts[c]))].append(d)
-    _PLAN.update(dict(rank=chip_rank, owners=owners, active=active, helpers=helpers, msgs=msgs, cnts=cnts))
+                deal(d, 0 if (pair_of[ch] + pair_of[topo.chip(d)]) % np_ < np_ // 2 else 1, senders[ch])
+        dst = [d for c2 in chips if c2 != ch for d in senders[c2] + [cores[chip_rank[c2]]]]
+        for d in sorted(dst, key=lambda d: topo.same_plane(ch, topo.chip(d))):
+            who = [c for c in senders[ch] + [R] if topo.may_write(c, d)]
+            cnts[min(who, key=lambda c: len(cnts[c]))].append(d)
+    _PLAN.update(dict(rank=chip_rank, senders=senders, consts=consts, msgs=msgs, cnts=cnts))
     return _PLAN
 
 
@@ -92,16 +98,17 @@ def rank_program(g, core, T, topo):
     cores = list(T.cores)
     P = make_plan(cores, topo)
     ch = topo.chip(core)
-    if ch not in P["rank"] or core not in P["active"][ch]:
+    if ch not in P["rank"]:
         return
     rk = P["rank"][ch]
     R = cores[rk]
     isR = core == R
-    helpers = P["helpers"][ch]
+    senders, consts = P["senders"][ch], P["consts"][ch]
+    if not isR and core not in senders and core not in consts:
+        return
     far = [c for c in cores if topo.same_plane(ch, topo.chip(c))][0]
     eng_off = engines(topo.mask(core, far))
-    near = [c for c in P["active"][ch] if c != core][0]
-    eng_all = engines(topo.mask(core, near))
+    eng_all = engines(topo.mask(core, R if not isR else senders[0]))
     Q = {"v": g.vector, "t": g.tensor, "s": g.scalar, "g": g, "y": g.sync}
     cnt, seen, last, readers, totals = {}, {}, {}, {}, {}
 
@@ -184,143 +191,100 @@ def rank_program(g, core, T, topo):
     def mm(r, w, out, l, rh, start=True, stop=True):
         op("t", "mm", r, [w], out, l, rh, start, stop, acc=True)
 
+    def finish():
+        for s in sorted(totals):
+            wait("g", (s, totals[s]))
+
+    def offset_constants(dest):
+        n16 = 16 * len(dest)
+        f = T.ocf
+        vset("ngf", T.ngf[:], -1.0)
+        vset("onf", T.onf[:], 1.0)
+        vset("ocf", f[:], 0.0)
+        vset("ocf", f[:, OLQ:OLQ + 128], 1.0)
+        vset("ocf", f[0:64, OPB + 2:OPB + 66], 1.0)
+        aff(f[0:64, OMA:OMA + n16], "ocf", T.ngf[:, 0:n16], "ngf", [[0, n16]], A.is_gt, rk, -1)
+        aff(f[0:64, OMB:OMB + n16], "ocf", T.ngf[:, 0:n16], "ngf", [[0, n16]], A.is_ge, -rk, 1)
+        aff(f[0:64, OMA + n16:OMA + n16 + 1], "ocf", T.onf[0:64, 0:1], "onf", [[0, 1]], A.is_equal, -rk, 1)
+        aff(f[0:64, OMB + n16:OMB + n16 + 1], "ocf", T.ngf[:, 0:1], "ngf", [[0, 1]], A.is_equal, -rk, 1)
+        aff(f[64:128, OCL:OCL + n16], "ocf", T.onf[64:128, 0:n16], "onf", [[0, n16]], A.is_equal, -32, 1)
+        iota(f[64:65, OCL:OCL + n16], "ocf", [[0, len(dest)], [16, 16]], 0, 0)
+        iota(f[96:97, OLQ:OLQ + 128], "ocf", [[0, 8], [1, 16]], 0, 0)
+        for j, d in enumerate(dest):
+            vset("ocf", f[32:33, OMA + 16 * j:OMA + 16 * j + 16], float(TC * d))
+        op("v", "copy", ["ocf"], ["oc"], T.oc[:], f[:])
+
+    def list_constants(part):
+        f = T.lcf
+        vset("onf", T.onf[:], 1.0)
+        if part == 1:
+            vset("lcf", f[:, LIP:LCW], 0.0)
+            aff(f[64:128, LIP:LIP + 128], "lcf", T.onf[64:128, :], "onf", [[0, 128]], A.is_equal, -32, 1)
+            iota(f[64:65, LIP:LIP + 128], "lcf", [[16, 128]], 0, 0)
+            iota(f[:, LIQ:LIQ + 128], "lcf", [[0, 8], [1, 16]], 0, 0)
+            iota(f[:, LIC:LIC + 129], "lcf", [[16, 129]], 0, 0)
+            op("v", "copy", ["lcf"], ["lc"], T.lc[:, LIP:LCW], f[:, LIP:LCW])
+            return
+        vset("lcf", f[:, 0:LIP], 0.0)
+        for i, cmp in enumerate((A.is_gt, A.is_ge)):
+            for h in (0, 1):
+                p, c = slice(64 * h, 64 * h + 64), LTR + 128 * i + 64 * h
+                aff(f[p, c:c + 64], "lcf", T.onf[p, 0:64], "onf", [[1, 64]], cmp, 0, -1)
+        for h in (0, 1):
+            r0 = 8 * h - 1
+            aff(f[0:64, 10 * h:10 * h + 10], "lcf", T.onf[0:64, 0:10], "onf", [[1, 10]], A.is_gt, r0, -1)
+            aff(f[0:64, 20 + 10 * h:30 + 10 * h], "lcf", T.onf[0:64, 0:10], "onf", [[-1, 10]], A.is_ge, -r0, 1)
+        aff(f[0:16, 20:21], "lcf", T.onf[0:16, 0:1], "onf", [[0, 1]], A.is_ge, N - 2, -1)
+        aff(f[0:64, 40:50], "lcf", T.onf[0:64, 0:10], "onf", [[1, 10]], A.is_equal, N - 1, -1)
+        for h in (0, 1):
+            c = LHS + 8 + 64 * h
+            aff(f[0:64, c:c + 64], "lcf", T.onf[0:64, 0:64], "onf", [[0, 64]], A.is_equal, -32 * h, 1)
+        vset("lcf", f[32:33, 0:50], -float(TC * rk))
+        for h, p in ((0, slice(0, 64)), (1, slice(32, 33))):
+            vset("lcf", f[p, LHS:LHS + 1], float(CAP * (SLOT[8 * h] - SLOT[8 * h - 1])))
+            vset("lcf", f[p, LHS + 1:LHS + 8], float(CAP * (SLOT[8 * h + 1] - SLOT[8 * h])))
+        both = f[:, LTR + 256:LTR + 384]
+        op("v", "tt", ["lcf"], ["lcf"], both, f[:, LTR:LTR + 128], f[:, LTR + 128:LTR + 256], A.add)
+        op("v", "ts", ["lcf"], ["lcf"], both, both, -1.0, None, A.mult)
+        op("v", "copy", ["lcf"], ["lc"], T.lc[:, 0:LIP], f[:, 0:LIP])
+
+    if core in consts:
+        i = consts.index(core)
+        if i == 0:
+            offset_constants([rk])
+            part = T.oc[:]
+        else:
+            list_constants(i - 1)
+            part = T.lc[:, 0:LIP] if i == 1 else T.lc[:, LIP:LCW]
+        fused(["lc" if i else "oc"], [([R], part, part, eng_all[:4], "kc%d" % i)])
+        finish()
+        return
+
     mine = P["msgs"][core]
-    dest = [cores.index(d) for d in mine] + ([rk] if isR else [])
+    dest = [rk] if isR else [cores.index(d) for d in mine]
     nd = len(dest)
     n16 = 16 * nd
     chip_eng = eng_off[2 * CW:4 * CW]
-    if isR:
-        dma("y", "dk1", [], ["k1"], T.k1[:], T.key[:])
-        dma("s", "dkd0", [], ["kd0"], T.kd[0:64, :], T.key[:, 0:64])
-        dma("y", "dkd1", [], ["kd1"], T.kd[64:128, :], T.key[:, 64:128])
-        dma("s", "dkt0", [], ["kt0"], T.kt[0:4, :], T.key[:, 0:64])
-        dma("y", "dkt1", [], ["kt1"], T.kt[4:8, :], T.key[:, 64:128])
-        dma("y", "dx0", [], ["x0"], T.xb[:, 0:1024], T.x[:, 0:1024])
-        dma("y", "dx1", [], ["x1"], T.xb[:, 1024:2048], T.x[:, 1024:2048])
-    vset("onb", T.onb[:], 1.0)
-    vset("win", T.win[:], 0.0)
-    vset("onf", T.onf[:], 1.0)
-    vset("ngf", T.ngf[:], -1.0)
-
-    def offset_constants():
-        aff(T.mxf[0:64, 0:n16], "mxf", T.ngf[0:64, 0:n16], "ngf", [[0, n16]], A.is_gt, rk, -1)
-        aff(T.mxf[0:64, 82:82 + n16], "mxf", T.ngf[0:64, 0:n16], "ngf", [[0, n16]], A.is_ge, -rk, 1)
-        aff(T.mxf[0:64, n16:n16 + 1], "mxf", T.onf[0:64, 0:1], "onf", [[0, 1]], A.is_equal, -rk, 1)
-        aff(T.mxf[0:64, 82 + n16:83 + n16], "mxf", T.ngf[0:64, 0:1], "ngf", [[0, 1]], A.is_equal, -rk, 1)
-        aff(T.clf[64:128, 0:n16], "clf", T.onf[64:128, 0:n16], "onf", [[0, n16]], A.is_equal, -32, 1)
-        iota(T.clf[64:65, 0:n16], "clf", [[0, nd], [16, 16]], 0, 0)
-        iota(T.lqf[96:97, 0:128], "lqf", [[0, 8], [1, 16]], 0, 0)
-
-    def offset_fills():
-        vset("pf", T.pf[:], 1.0)
-        vset("pf", T.pf[:, 0:2], 0.0)
-        op("v", "copy", ["pf"], ["pb"], T.pb[:], T.pf[:])
-        vset("xpad", T.xs[:, TC:], 0.0)
-        for j, d in enumerate(dest):
-            vset("mxf", T.mxf[32:33, 16 * j:16 * j + 16], float(TC * d))
-        op("v", "copy", ["mxf"], ["mx"], T.mx[:, 0:n16 + 1], T.mxf[:, 0:n16 + 1])
-        op("v", "copy", ["mxf"], ["mx"], T.mx[:, 82:83 + n16], T.mxf[:, 82:83 + n16])
-        op("v", "copy", ["clf"], ["clc"], T.cl[64:128, 0:n16], T.clf[64:128, 0:n16])
-        op("v", "copy", ["onf"], ["lq"], T.lq[:, 0:128], T.onf[:])
-        op("v", "copy", ["lqf"], ["lq"], T.lq[96:97, 0:128], T.lqf[96:97, 0:128])
-
-    def list_constants():
-        iota(T.iq[:], "iq", [[0, 8], [1, 16]], 0, 0)
-        iota(T.ic[:], "ic", [[16, 129]], 0, 0)
-        aff(T.lqf[64:128, 128:256], "ipf", T.onf[64:128, :], "onf", [[0, 128]], A.is_equal, -32, 1)
-        iota(T.lqf[64:65, 128:256], "ipf", [[16, 128]], 0, 0)
-        for h in (0, 1):
-            r0 = 8 * h - 1
-            aff(T.eef[0:64, 10 * h:10 * h + 10], "eef", T.onf[0:64, 0:10], "onf", [[1, 10]], A.is_gt, r0, -1)
-            aff(T.eef[0:64, 20 + 10 * h:30 + 10 * h], "eef", T.onf[0:64, 0:10], "onf", [[-1, 10]], A.is_ge, -r0, 1)
-        aff(T.eef[0:16, 20:21], "eef", T.onf[0:16, 0:1], "onf", [[0, 1]], A.is_ge, N - 2, -1)
-        aff(T.eef[0:64, 40:50], "eef", T.onf[0:64, 0:10], "onf", [[1, 10]], A.is_equal, N - 1, -1)
-        for h in (0, 1):
-            aff(T.eef[0:64, 64 + 64 * h:128 + 64 * h], "hsf", T.onf[0:64, 0:64], "onf", [[0, 64]], A.is_equal, -32 * h, 1)
-
-    def list_fills():
-        vset("trf", T.trf[:], 0.0)
-        for i, cmp in enumerate((A.is_gt, A.is_ge)):
-            for h in (0, 1):
-                p, c = slice(64 * h, 64 * h + 64), 128 * i + 64 * h
-                aff(T.trf[p, c:c + 64], "trf", T.onf[p, 0:64], "onf", [[1, 64]], cmp, 0, -1)
-        vset("eef", T.eef[32:33, 0:50], -float(TC * rk))
-        for h, p in ((0, slice(0, 64)), (1, slice(32, 33))):
-            vset("hsf", T.eef[p, 56:57], float(CAP * (SLOT[8 * h] - SLOT[8 * h - 1])))
-            vset("hsf", T.eef[p, 57:64], float(CAP * (SLOT[8 * h + 1] - SLOT[8 * h])))
-
-    def list_copies():
-        op("v", "copy", ["eef"], ["ee"], T.ee[:, 0:50], T.eef[:, 0:50])
-        op("v", "copy", ["trf"], ["tr"], T.tr[:, 0:256], T.trf[:])
-        op("v", "tt", ["trf"], ["tmf"], T.tmf[:], T.trf[:, 0:128], T.trf[:, 128:256], A.add)
-        op("v", "copy", ["hsf"], ["hs"], T.ee[:, 56:192], T.eef[:, 56:192])
-        op("v", "copy", ["ipf"], ["ip"], T.lq[64:128, 128:256], T.lqf[64:128, 128:256])
-        op("v", "ts", ["tmf"], ["tr2"], T.tr[:, 256:384], T.tmf[:], -1.0, None, A.mult)
-
     cds = P["cnts"][core]
     half = (len(cds) + 1) // 2
     cnt_trs = [(ds, T.cd[rk], T.cd[rk], eng_off[i * CW:(i + 1) * CW], "call") for i, ds in enumerate([cds[:half], cds[half:]]) if ds]
-    pairs = [[c for c in helpers if topo.die(c) == die] for die in (0, 1)]
-    first = [p[0] for p in pairs]
-    later = {p[0]: p[1] for p in pairs if len(p) > 1}
-    x0, x1 = [T.xb[:, 1024 * h:1024 * h + 1024] for h in (0, 1)]
+    xh = [T.xb[:, 1024 * h:1024 * h + 1024] for h in (0, 1)]
+    xw = len(eng_all) // 2
 
-    def sort_constants():
-        iota(T.pint[:, 0:1], "pint", [[0, 1]], 0, 1, small=False)
-        aff(T.sel[:], "sel", T.onb[0:8, :], "onb", [[-1, 4], [-4, 2], [0, 64]], A.is_equal, 0, 1)
-        iota(T.jlo[:], "jlo", [[1, 16]], 0, 1)
-        iota(T.jhi[:], "jhi", [[128, 8], [1024, 2]], 0, 0)
-        op("v", "ts", ["pint"], ["pint1"], T.pint[:, 1:2], T.pint[:, 0:1], 63, None, A.bitwise_and)
-        op("v", "copy", ["pint1"], ["kcol"], T.kcol[:], T.pint[:, 1:2])
+    upto, below, below2 = T.oc[0:33, OPB + 2:OPB + 66], T.oc[0:16, OPB + 1:OPB + 65], T.oc[0:16, OPB:OPB + 64]
 
-    def sort_fills():
-        vset("hm", T.hm[:], 0.0)
-        vset("hm", T.hm[0:64, 0:1], 1.0)
-        vset("hm", T.hm[64:128, 1:2], 1.0)
-        op("v", "copy", ["hm"], ["hmh"], T.hmh[:], T.hm[:])
-        for b in (0, 64):
-            op("v", "ts", ["i64", "kcol"], ["wt"], T.wt[:, b:b + 64], T.i64[:], T.kcol[:], None, A.is_gt)
-        op("v", "ts", ["i64", "kcol"], ["wt"], T.wt[0:64, 64:128], T.i64[0:64, :], T.kcol[0:64, :], None, A.is_ge)
-        vset("zb", T.zb[:], 0.0)
-        op("v", "ts", ["pint"], ["pint2"], T.pint[:, 2:3], T.pint[:, 0:1], 15, None, A.bitwise_and)
-        for i, (v, cmp) in enumerate(((0.0, A.is_equal), (1.0, A.is_equal), (2.0, A.is_lt))):
-            op("v", "ts", ["pint2"], ["pm%d" % i], T.pm[:, i:i + 1], T.pint[:, 2:3], v, None, cmp)
-        op("v", "ts", ["jlo", "pm0"], ["jlo"], T.jlo[:], T.jlo[:], T.pm[:, 0:1], None, A.mult)
-        op("v", "ts", ["jhi", "pm1"], ["jhi"], T.jhi[:], T.jhi[:], T.pm[:, 1:2], None, A.mult)
-        op("v", "ts", ["onf", "pm2"], ["zb"], T.zb[:, 0::16], T.onf[:, 0:9], T.pm[:, 2:3], None, A.mult)
-        for i in range(16):
-            op("s", "act", ["jlo", "jhi"], ["jv"], T.jv[:, 16 * i:16 * i + 16], T.jlo[:], F.Identity, T.jhi[:, i:i + 1], acc=True)
+    def load_counts():
+        arrive("call", 15 * CW, ["cd"])
+        dma("y", "dcb", ["cd", "cdown", "oc"], ["cb"], T.oc[0:16, OPB + 2:OPB + 66], T.cd[:, 64:128, 0])
 
-    def sort_columns():
-        for a in range(4):
-            kq = [T.p0, T.p1, T.p2, T.p3][a]
-            mm(["sel", "ktb"], "p%d" % a, kq[:, 0:256], T.sel[:, 128 * a:128 * a + 128], T.ktb[:])
-            for q in range(4):
-                op("v", "ts", ["p%d" % a, "kcol"], ["ot"], T.ot[:, 4 * a + q::16], kq[:, 64 * q:64 * q + 64], T.kcol[:], None, A.is_equal, acc=True)
-        op("v", "scan", ["ot"], ["cp"], T.cp[:], T.ot[:], T.ot[:], 0.0, A.add, A.max)
-        op("v", "copy", ["cp"], ["tot"], T.tot[:], T.cp[:, 1023:1024])
-        mm(["wt", "tot"], "p0", T.p0[:, 64:65], T.wt[:], T.tot[:])
-        for h in (0, 1):
-            op("v", "tt", ["ot", "cp"], ["pr%d" % h], T.pr[:, 512 * h:512 * h + 512], T.ot[:, 512 * h:512 * h + 512], T.cp[:, 512 * h:512 * h + 512], A.mult)
-            if h == 0:
-                op("v", "ts", ["hm", "p0"], ["ls"], T.ls[:], T.hm[:], T.p0[:, 64:65], None, A.mult)
-        for b in range(8):
-            sl = slice(128 * b, 128 * b + 128)
-            mm(["ot", "ls"], "p1", T.p1[:, 2 * b:2 * b + 2], T.ot[:, sl], T.ls[:], True, False)
-            mm(["pr%d" % (b // 4), "hmh"], "p1", T.p1[:, 2 * b:2 * b + 2], T.pr[:, sl], T.hmh[:], False, True)
-        op("v", "ts", ["p1"], ["so"], T.so[:], T.p1[:, 0:16], -1.0, None, A.add)
-        op("v", "copy", ["so", "jv"], ["win"], T.win[:].indirect(T.so[:]), T.jv[:])
-        if isR:
-            offset_fills()
-            list_fills()
-        for h, (key, ps) in enumerate((("p1", T.p1[:, 128:192]), ("p0", T.p0[:, 128:192]))):
-            for q in range(16):
-                mm(["zb", "win"], key, ps, T.zb[:, 16 - q:144 - q], T.win[:, 1024 * h + q:1024 * h + 1024:16], q == 0, q == 15)
-            op("v", "copy", [key], ["perm%d" % h], T.plist[:, 64 * h:64 * h + 64], ps)
-            if h == 0 and not isR:
-                places()
-                sort_x("v", 0, 512)
-                sort_x("s", 512, 1024)
+    def places():
+        mm(["cb", "oc"], "p0", T.p0[0:64, 0:n16 + 1], upto, T.oc[0:33, OMA:OMA + n16 + 1], True, False)
+        mm(["cb", "oc"], "p0", T.p0[0:64, 0:n16 + 1], below, T.oc[0:16, OMB:OMB + n16 + 1], False, True)
+        op("v", "ts", ["p0"], ["cl"], T.oc[0:64, OCL:OCL + n16], T.p0[0:64, 0:n16], 0.0, T.p0[0:64, n16:n16 + 1], A.max, A.min)
+
+    def starts():
+        mm(["oc", "cl"], "p1", T.p1[:, 0:n16], T.oc[:, OLQ:OLQ + 128], T.oc[:, OCL:OCL + n16])
+        op("v", "copy", ["p1"], ["off"], T.off[:, 0:n16], T.p1[:, 0:n16])
 
     xs_parts = []
 
@@ -333,120 +297,164 @@ def rank_program(g, core, T, topo):
         else:
             op("s", "act", r, ["xs%d" % a], out, src, F.Copy)
 
-    upto, below, below2 = T.pb[0:33, 2:66], T.pb[0:16, 1:65], T.pb[0:16, 0:64]
-
-    def places():
-        mm(["cb", "mx"], "p2", T.p2[0:64, 0:n16 + 1], upto, T.mx[0:33, 0:n16 + 1], True, False)
-        mm(["cb", "mx"], "p2", T.p2[0:64, 0:n16 + 1], below, T.mx[0:16, 82:83 + n16], False, True)
-        op("v", "ts", ["p2"], ["cl"], T.cl[0:64, 0:n16], T.p2[0:64, 0:n16], 0.0, T.p2[0:64, n16:n16 + 1], A.max, A.min)
-
-    def starts():
-        mm(["lq", "cl", "clc"], "p2", T.p2[:, 128:128 + n16], T.lq[:, 0:128], T.cl[:, 0:n16])
-        op("v", "copy", ["p2"], ["off"], T.off[:, 0:n16], T.p2[:, 128:128 + n16])
-
-    def load_counts():
-        arrive("call", 15 * CW, ["cd"])
-        dma("y", "dcb", ["cd", "cdown", "pb"], ["cb"], T.pb[0:16, 2:66], T.cd[:, 0:64, 0])
-
-    iota(T.i64[:], "i64", [[1, 64]], 0, 0)
-    if isR:
-        fused(["kd0", "kd1"], [(helpers, T.kd[:], T.kd[:], chip_eng, "kown")])
-        op("v", "copy", ["k1"], ["k1f"], T.k1f[:], T.k1[:])
-        for i in range(16):
-            op("v", "ts", ["i64", "k1f"], ["oh%d" % i], T.oh[:, 64 * i:64 * i + 64], T.i64[:], T.k1f[:, i:i + 1], None, A.is_ge)
-            mm(["onb", "oh%d" % i], "p0", T.p0[0:2, 0:64], T.onb[:, 0:2], T.oh[:, 64 * i:64 * i + 64], i == 0, i == 15)
-        op("v", "copy", ["p0"], ["cst"], T.cst[:], T.p0[0:2, 0:64])
-        dma("y", "dcs", ["cst"], ["cdown"], T.cd[rk], T.cst[:])
-        sort_constants()
-        op("v", "copy", ["kt0", "kt1"], ["ktb"], T.ktb[:], T.kt[:])
-        fused(["cdown"], [(helpers, T.cd[rk], T.cd[rk], chip_eng, "cown")] + cnt_trs)
-        fused(["x0"], [(first, x0, x0, eng_all, "xarr")])
-        fused(["x1"], [(helpers, x1, x1, eng_all, "xhalf")])
-        sort_fills()
-        offset_constants()
-        list_constants()
-        sort_columns()
-    else:
-        sort_constants()
-        arrive("kown", len(chip_eng), ["kd"])
-        dma("y", "dkt0", ["kd"], ["kt"], T.kt[:], T.kd[:])
-        sort_fills()
-        offset_constants()
-        offset_fills()
-        op("v", "copy", ["kt"], ["ktb"], T.ktb[:], T.kt[:])
-        arrive("cown", len(chip_eng), ["cdown"])
-        arrive("xarr" if core in first else "xpart", len(eng_all), ["x0"])
-        arrive("xhalf", len(eng_all), ["x1"])
-        fused(["cdown"], cnt_trs)
-        load_counts()
-        if core in later:
-            fused(["x0"], [([later[core]], x0, x0, eng_all, "xpart")])
-        sort_columns()
-
-    if isR:
-        sort_x("s", 0, 1024)
-        sort_x("v", 1024, TC)
-        load_counts()
-        places()
-        starts()
-    else:
-        starts()
-        sort_x("s", 1024, 1536)
-        sort_x("v", 1536, TC)
-    xr = xs_parts + ["xpad", "off"]
-
     def gather(q, out, key, j):
         src = T.xs[:].indirect(T.off[:, 16 * j:16 * j + 16])
+        r = xs_parts + ["xpad", "off"]
         if q == "v":
-            op("v", "copy", xr, [key], out, src)
+            op("v", "copy", r, [key], out, src)
         else:
-            op("s", "act", xr, [key], out, src, F.Copy)
+            op("s", "act", r, [key], out, src, F.Copy)
 
-    for call in calls_of(mine, eng_off):
-        for j, m, n in call:
-            on_v = j == 1 if isR else j % 2 == 0
-            gather("v" if on_v else "s", T.msg[:, CAP * j:CAP * j + CAP], "m%d" % j, j)
-        fused(["m%d" % j for j, m, n in call],
-              [([mine[j]], T.msg[:, CAP * j:CAP * j + CAP], T.rcv[:, CAP * SLOT[rk]:CAP * SLOT[rk] + CAP], engines(m), "data") for j, m, n in call])
+    def inverse_constants():
+        iota(T.jlo[:], "jlo", [[1, 16]], 0, 1)
+        iota(T.jhi[:], "jhi", [[128, 8], [1024, 2]], 0, 0)
+        op("v", "ts", ["pint"], ["pint2"], T.pint[:, 2:3], T.pint[:, 0:1], 15, None, A.bitwise_and)
+        for i, (v, cmp) in enumerate(((0.0, A.is_equal), (1.0, A.is_equal), (2.0, A.is_lt))):
+            op("v", "ts", ["pint2"], ["pm%d" % i], T.pm[:, i:i + 1], T.pint[:, 2:3], v, None, cmp)
+        op("v", "ts", ["jlo", "pm0"], ["jlo"], T.jlo[:], T.jlo[:], T.pm[:, 0:1], None, A.mult)
+        op("v", "ts", ["jhi", "pm1"], ["jhi"], T.jhi[:], T.jhi[:], T.pm[:, 1:2], None, A.mult)
+        for i in range(16):
+            op("s", "act", ["jlo", "jhi"], ["jv"], T.jv[:, 16 * i:16 * i + 16], T.jlo[:], F.Identity, T.jhi[:, i:i + 1], acc=True)
+        vset("one9", T.one9[:], 1.0)
+        vset("zb", T.zb[:], 0.0)
+        op("v", "ts", ["one9", "pm2"], ["zb"], T.zb[:, 0::16], T.one9[:], T.pm[:, 2:3], None, A.mult)
+        vset("win", T.win[:], 0.0)
 
-    if isR:
-        gather("s", T.rcv[:, CAP * SLOT[rk]:CAP * SLOT[rk] + CAP], "own", nd - 1)
-        list_copies()
-        mm(["cb", "ee"], "p3", T.p3[0:64, 0:10], upto, T.ee[0:33, 0:10], True, False)
-        mm(["cb", "ee"], "p3", T.p3[0:64, 0:10], below, T.ee[0:16, 20:30], False, False)
-        mm(["cb", "ee"], "p3", T.p3[0:64, 0:10], below2, T.ee[0:16, 40:50], False, True)
-        mm(["cb", "ee"], "p3", T.p3[64:128, 0:10], upto, T.ee[0:33, 10:20], True, False)
-        mm(["cb", "ee"], "p3", T.p3[64:128, 0:10], below, T.ee[0:16, 30:40], False, True)
-        op("v", "ts", ["p3"], ["sc"], T.sc[:], T.p3[:, 0:10], 0.0, float(TC), A.max, A.min)
-        op("v", "ts", ["p3"], ["sci"], T.sci[:, 0:8], T.p3[:, 1:9], 0.0, float(TC), A.max, A.min)
-        op("v", "ts", ["sci"], ["scm"], T.sci[:, 8:16], T.sci[:, 0:8], 2 * TC - 16, None, A.bitwise_and)
-        op("v", "copy", ["scm"], ["hif"], T.hif[:], T.sci[:, 8:16])
-        mm(["hs"], "cp", T.cp[:, 0:8], T.ee[0:33, 64:192], T.ee[0:33, 56:64], True, False)
-        mm(["tr", "sc"], "cp", T.cp[:, 0:8], T.tr[:, 0:128], T.sc[:, 2:10], False, False)
-        mm(["tr", "sc"], "cp", T.cp[:, 0:8], T.tr[:, 128:256], T.sc[:, 0:8], False, False)
-        mm(["tr2", "sc"], "cp", T.cp[:, 0:8], T.tr[:, 256:384], T.sc[:, 1:9], False, True)
-        mm(["lq", "ip"], "kb", T.kb[:, 0:128], T.lq[64:128, 0:128], T.lq[64:128, 128:256], True, False)
-        for i in range(8):
-            a0, z0 = 256 * i, 136 * i
-            na, ya, zi = T.aa[:, a0:a0 + 128], T.aa[:, a0 + 128:a0 + 256], T.zz[:, z0:z0 + 129]
-            hi, pl, st = T.hif[:, i:i + 1], T.p3[:, 1 + i:2 + i], T.cp[:, i:i + 1]
-            op("v", "ts", ["iq", "hif", "p3"], ["na%d" % i], na, T.iq[:], hi, pl, A.add, A.is_lt)
-            op("v", "ts", ["iq", "hif", "p3"], ["ya%d" % i], ya, T.iq[:], hi, pl, A.add, A.is_ge)
-            op("v", "ts", ["ic", "hif", "cp"], ["zz%d" % i], zi, T.ic[:], hi, st, A.is_gt, A.mult)
-            mm(["na%d" % i, "zz%d" % i], "kb", T.kb[:, 0:128], na, T.zz[:, z0:z0 + 128], False, False)
-            mm(["ya%d" % i, "zz%d" % i], "kb", T.kb[:, 0:128], ya, T.zz[:, z0 + 1:z0 + 129], False, i == 7)
-        op("v", "copy", ["kb"], ["yoff"], T.yoff[:], T.kb[:, 0:128])
-        n_in = 0
-        for c2 in P["msgs"]:
-            if topo.chip(c2) != ch:
-                for call in calls_of(P["msgs"][c2], engines(topo.mask(c2, R))):
-                    n_in += sum(n for j, m, n in call if P["msgs"][c2][j] == R)
-        arrive("data", n_in, ["rcv"])
-        yr = ["rcv", "own", "yoff"]
-        for h in (0, 1):
-            a, b, o = 1024 * h, 1024 * h + 512, 64 * h
-            op("v", "copy", yr, ["yl%d" % h], T.yb[:, a:b], T.rcv[:].indirect(T.yoff[:, o:o + 32]))
-            op("s", "act", yr, ["yr%d" % h], T.yb[:, b:b + 512], T.rcv[:].indirect(T.yoff[:, o + 32:o + 64]), F.Copy)
-            dma("y", "dy%d" % h, ["yl%d" % h, "yr%d" % h], ["yo%d" % h], T.y[:, a:a + 1024], T.yb[:, a:a + 1024])
-    for s in sorted(totals):
-        wait("g", (s, totals[s]))
+    def scatter():
+        op("v", "copy", ["so", "jv"], ["win"], T.win[:].indirect(T.so[:]), T.jv[:])
+
+    def inverse(h):
+        key, ps = (("p6", T.p6), ("p7", T.p7))[h]
+        for q in range(16):
+            mm(["zb", "win"], key, ps[:, 0:64], T.zb[:, 16 - q:144 - q], T.win[:, 1024 * h + q:1024 * h + 1024:16], q == 0, q == 15)
+        op("v", "copy", [key], ["perm%d" % h], T.plist[:, 64 * h:64 * h + 64], ps[:, 0:64])
+
+    iota(T.pint[:, 0:1], "pint", [[0, 1]], 0, 1, small=False)
+    if not isR:
+        h = senders.index(core) // 2
+        partner = [c for c in senders if c != core and topo.die(c) == topo.die(core)][0]
+        vset("xpad", T.xs[:, TC:], 0.0)
+        inverse_constants()
+        offset_constants(dest)
+        arrive("xh0", xw, ["x0"])
+        arrive("xh1", xw, ["x1"])
+        arrive("cown", len(chip_eng), ["cdown"])
+        arrive("soar", len(eng_all), ["so"])
+        fused(["x%d" % h], [([partner], xh[h], xh[h], eng_all[xw:], "xh%d" % h)])
+        fused(["cdown"], cnt_trs)
+        load_counts()
+        scatter()
+        inverse(0)
+        sort_x("v", 0, 512)
+        sort_x("s", 512, 1024)
+        inverse(1)
+        sort_x("s", 1024, 1536)
+        places()
+        sort_x("v", 1536, TC)
+        starts()
+        for call in calls_of(mine, eng_off):
+            for j, m, n in call:
+                gather("v" if j % 2 == 0 else "s", T.msg[:, CAP * j:CAP * j + CAP], "m%d" % j, j)
+            fused(["m%d" % j for j, m, n in call],
+                  [([mine[j]], T.msg[:, CAP * j:CAP * j + CAP], T.rcv[:, CAP * SLOT[rk]:CAP * SLOT[rk] + CAP], engines(m), "data") for j, m, n in call])
+        finish()
+        return
+
+    dma("s", "dkt0", [], ["kt0"], T.kt[0:4, :], T.key[:, 0:64])
+    dma("y", "dkt1", [], ["kt1"], T.kt[4:8, :], T.key[:, 64:128])
+    dma("y", "dx0", [], ["x0"], T.xb[:, 0:1024], T.x[:, 0:1024])
+    dma("y", "dx1", [], ["x1"], T.xb[:, 1024:2048], T.x[:, 1024:2048])
+    iota(T.i65[:], "i65", [[1, 66]], 0, 0)
+    for h in (0, 1):
+        fused(["x%d" % h], [([c], xh[h], xh[h], eng_all[i::2], "xh%d" % h) for i, c in enumerate(senders[2 * h:2 * h + 2])])
+    vset("hs8", T.hs8[:, 0:64], 0.0)
+    vset("hs8", T.hs8[:, 64:128], 4.0)
+    op("v", "ts", ["pint"], ["pint1"], T.pint[:, 1:2], T.pint[:, 0:1], 63, None, A.bitwise_and)
+    op("v", "copy", ["pint1"], ["kcol"], T.kcol[:], T.pint[:, 1:2])
+    for a in range(4):
+        op("v", "ts", ["hs8", "kcol"], ["sel"], T.sel[:, 128 * a:128 * a + 128], T.hs8[:], float(a), T.kcol[0:8, :], A.add, A.is_equal, acc=True)
+    for i, v in enumerate((A.is_lt, A.is_ge)):
+        op("v", "ts", ["pint"], ["hmh"], T.hmh[:, i:i + 1], T.pint[:, 0:1], 64.0, None, v, acc=True)
+    op("v", "copy", ["kt0", "kt1"], ["ktb"], T.ktb[:], T.kt[:])
+    op("v", "ts", ["i65", "kcol"], ["w1"], T.w1[:], T.i65[:], T.kcol[:], None, A.is_gt)
+    op("v", "ts", ["i65", "kcol"], ["w2"], T.w2[0:64, :], T.i65[0:64, 0:64], T.kcol[0:64, :], None, A.is_ge, acc=True)
+    op("v", "ts", ["i65", "kcol"], ["w2"], T.w2[64:128, :], T.i65[64:128, 0:64], T.kcol[64:128, :], None, A.is_gt, acc=True)
+    for a in range(4):
+        kq = [T.p0, T.p1, T.p2, T.p3][a]
+        mm(["sel", "ktb"], "p%d" % a, kq[:, 0:256], T.sel[:, 128 * a:128 * a + 128], T.ktb[:])
+        for q in range(4):
+            op("v", "ts", ["p%d" % a, "kcol"], ["ot"], T.ot[:, 4 * a + q::16], kq[:, 64 * q:64 * q + 64], T.kcol[:], None, A.is_equal, acc=True)
+    op("v", "scan", ["ot"], ["cp"], T.cp[:], T.ot[:], T.ot[:], 0.0, A.add, A.max)
+    mm(["w1", "cp"], "p4", T.p4[0:2, 0:64], T.cp[:, 1022:1024], T.w1[:, 1:65])
+    mm(["w1", "cp"], "p4", T.p4[0:64, 64:65], T.w1[:, 0:64], T.cp[:, 1023:1024])
+    mm(["w2", "cp"], "p4", T.p4[64:128, 64:65], T.w2[:], T.cp[:, 1023:1024])
+
+    def masked(h):
+        sl = slice(512 * h, 512 * h + 512)
+        op("v", "scan", ["ot", "cp"], ["pr%d" % h], T.pr[:, sl], T.cp[:, sl], T.ot[:, sl], 0.0, A.max, A.mult)
+
+    masked(0)
+    op("v", "copy", ["p4"], ["cst"], T.cst[:], T.p4[0:2, 0:64])
+    op("v", "ts", ["hmh", "p4"], ["ls"], T.ls[:], T.hmh[:], T.p4[:, 64:65], None, A.mult)
+    masked(1)
+    dma("y", "dcs", ["cst"], ["cdown"], T.cd[rk], T.cst[:])
+    for b in range(8):
+        sl = slice(128 * b, 128 * b + 128)
+        mm(["ot", "ls"], "p5", T.p5[:, 2 * b:2 * b + 2], T.ot[:, sl], T.ls[:], True, False)
+        mm(["pr%d" % (b // 4), "hmh"], "p5", T.p5[:, 2 * b:2 * b + 2], T.pr[:, sl], T.hmh[:], False, True)
+    op("v", "ts", ["p5"], ["so"], T.so[:], T.p5[:, 0:16], -1.0, None, A.add)
+    fused(["so"], [(senders, T.so[:], T.so[:], eng_all, "soar")])
+    fused(["cdown"], [(senders, T.cd[rk], T.cd[rk], chip_eng, "cown")] + cnt_trs)
+    vset("xpad", T.xs[:, TC:], 0.0)
+    inverse_constants()
+    scatter()
+    for h in (0, 1):
+        inverse(h)
+        sort_x("s", 1024 * h, 1024 * h + 1024)
+    arrive("kc0", 4, ["oc"])
+    arrive("kc1", 4, ["lc"])
+    arrive("kc2", 4, ["lc2"])
+    load_counts()
+    places()
+    starts()
+    gather("s", T.rcv[:, CAP * SLOT[rk]:CAP * SLOT[rk] + CAP], "own", 0)
+    lc = T.lc
+    mm(["cb", "lc"], "p2", T.p2[0:64, 0:10], upto, lc[0:33, 0:10], True, False)
+    mm(["cb", "lc"], "p2", T.p2[0:64, 0:10], below, lc[0:16, 20:30], False, False)
+    mm(["cb", "lc"], "p2", T.p2[0:64, 0:10], below2, lc[0:16, 40:50], False, True)
+    mm(["cb", "lc"], "p2", T.p2[64:128, 0:10], upto, lc[0:33, 10:20], True, False)
+    mm(["cb", "lc"], "p2", T.p2[64:128, 0:10], below, lc[0:16, 30:40], False, True)
+    op("v", "ts", ["p2"], ["sc"], T.sc[:], T.p2[:, 0:10], 0.0, float(TC), A.max, A.min)
+    op("v", "ts", ["p2"], ["sci"], T.sci[:, 0:8], T.p2[:, 1:9], 0.0, float(TC), A.max, A.min)
+    op("v", "ts", ["sci"], ["scm"], T.sci[:, 8:16], T.sci[:, 0:8], 2 * TC - 16, None, A.bitwise_and)
+    op("v", "copy", ["scm"], ["hif"], T.hif[:], T.sci[:, 8:16])
+    mm(["lc"], "p3", T.p3[:, 0:8], lc[0:33, LHS + 8:LHS + 136], lc[0:33, LHS:LHS + 8], True, False)
+    mm(["lc", "sc"], "p3", T.p3[:, 0:8], lc[:, LTR:LTR + 128], T.sc[:, 2:10], False, False)
+    mm(["lc", "sc"], "p3", T.p3[:, 0:8], lc[:, LTR + 128:LTR + 256], T.sc[:, 0:8], False, False)
+    mm(["lc", "sc"], "p3", T.p3[:, 0:8], lc[:, LTR + 256:LTR + 384], T.sc[:, 1:9], False, True)
+    mm(["oc", "lc2"], "p4", T.p4[:, 0:128], T.oc[64:128, OLQ:OLQ + 128], lc[64:128, LIP:LIP + 128], True, False)
+    iq, ic = lc[:, LIQ:LIQ + 128], lc[:, LIC:LIC + 129]
+    for i in range(8):
+        a0, z0 = 256 * i, 136 * i
+        na, ya, zi = T.aa[:, a0:a0 + 128], T.aa[:, a0 + 128:a0 + 256], T.zz[:, z0:z0 + 129]
+        hi, pl, st = T.hif[:, i:i + 1], T.p2[:, 1 + i:2 + i], T.p3[:, i:i + 1]
+        op("v", "ts", ["lc2", "hif", "p2"], ["na%d" % i], na, iq, hi, pl, A.add, A.is_lt)
+        op("v", "ts", ["lc2", "hif", "p2"], ["ya%d" % i], ya, iq, hi, pl, A.add, A.is_ge)
+        op("v", "ts", ["lc2", "hif", "p3"], ["zz%d" % i], zi, ic, hi, st, A.is_gt, A.mult)
+        mm(["na%d" % i, "zz%d" % i], "p4", T.p4[:, 0:128], na, T.zz[:, z0:z0 + 128], False, False)
+        mm(["ya%d" % i, "zz%d" % i], "p4", T.p4[:, 0:128], ya, T.zz[:, z0 + 1:z0 + 129], False, i == 7)
+    op("v", "copy", ["p4"], ["yoff"], T.yoff[:], T.p4[:, 0:128])
+    n_in = 0
+    for c2 in P["msgs"]:
+        if topo.chip(c2) != ch:
+            for call in calls_of(P["msgs"][c2], engines(topo.mask(c2, R))):
+                n_in += sum(n for j, m, n in call if P["msgs"][c2][j] == R)
+    arrive("data", n_in, ["rcv"])
+    yr = ["rcv", "own", "yoff"]
+    for h in range(3):
+        a, c = YPART[h], YPART[h + 1]
+        b = (a + c) // 2
+        op("v", "copy", yr, ["yl%d" % h], T.yb[:, a:b], T.rcv[:].indirect(T.yoff[:, a // 16:b // 16]))
+        op("s", "act", yr, ["yr%d" % h], T.yb[:, b:c], T.rcv[:].indirect(T.yoff[:, b // 16:c // 16]), F.Copy)
+        dma("y", "dy%d" % h, ["yl%d" % h, "yr%d" % h], ["yo%d" % h], T.y[:, a:c], T.yb[:, a:c])
+    finish()

@@ -11,9 +11,9 @@ SCRATCH = {"cd": ("dram", [N, 128, 1], FH)}
 for _n, _p, _w, _d in (
         ("xb", 128, TC, BF), ("xs", 128, TC + CAP, BF), ("msg", 128, NMAX * CAP, BF), ("rcv", 128, N * CAP, BF),
         ("yb", 128, TC, BF), ("plist", 128, 128, U16), ("off", 128, 16 * NMAX, U16), ("yoff", 128, 128, U16),
-        ("ocf", 128, OCW, F32), ("oc", 128, OCW, FH), ("lcf", 128, LCW, F32), ("lc", 128, LCW, FH),
-        ("onf", 128, 128, F32), ("ngf", 64, 80, F32),
-        ("kt", 8, 256, I32), ("ktb", 8, 256, BF), ("hs8", 8, 128, BF), ("sel", 8, 512, BF), ("kcol", 128, 1, F32),
+        ("ocf", 128, OCW, BF), ("oc", 128, OCW, FH), ("oneb", 128, 64, BF), ("cab", 128, 3, F32),
+        ("lcf", 128, LCW, F32), ("lc", 128, LCW, FH), ("onf", 128, 128, F32),
+        ("kt", 16, 128, I32), ("ktb", 16, 128, BF), ("hs8", 16, 128, BF), ("sel", 16, 1024, BF), ("kcol", 128, 1, F32),
         ("i65", 128, 66, BF), ("w1", 128, 66, FH), ("w2", 128, 64, FH), ("cst", 2, 64, FH), ("hmh", 128, 2, FH),
         ("ot", 128, 1024, FH), ("cp", 128, 1024, FH), ("pr", 128, 1024, FH), ("ls", 128, 2, FH), ("so", 128, 16, U16),
         ("win", 128, TC, BF), ("one9", 128, 9, F32), ("jlo", 128, 16, BF), ("jhi", 128, 16, F32), ("jv", 128, 256, BF),
@@ -22,11 +22,12 @@ for _n, _p, _w, _d in (
     SCRATCH[_n] = ("sbuf", [_p, _w], _d)
 for _i in range(8):
     SCRATCH["p%d" % _i] = ("psum", [128, 512], F32)
-SEMAPHORES = ["sv", "st", "ss", "sg", "lsnd", "cown", "call", "xh0", "xh1", "soar", "kc0", "kc1", "kc2", "data",
-              "dkt0", "dkt1", "dx0", "dx1", "dcs", "dcb", "dy0", "dy1", "dy2"]
+SEMAPHORES = ["sv", "st", "ss", "sg", "lsnd", "cown", "call", "xq0", "xq1", "xq2", "xq3", "soar", "kc0", "kc1", "kc2",
+              "data", "dkt0", "dkt1", "dx0", "dx1", "dcs", "dcb", "dy0", "dy1", "dy2"]
 CW = 2
 SLOT = [2 * r + 1 if r < N // 2 else 2 * (N - 1 - r) for r in range(N)]
 YPART = [0, 1024, 1536, 2048]
+XQ = ["x0", "x1", "x2", "x3"]
 _PLAN = {}
 
 
@@ -198,21 +199,21 @@ def rank_program(g, core, T, topo):
     def offset_constants(dest):
         n16 = 16 * len(dest)
         f = T.ocf
-        vset("ngf", T.ngf[:], -1.0)
-        vset("onf", T.onf[:], 1.0)
         vset("ocf", f[:], 0.0)
-        vset("ocf", f[:, OLQ:OLQ + 128], 1.0)
-        vset("ocf", f[0:64, OPB + 2:OPB + 66], 1.0)
-        aff(f[0:64, OMA:OMA + n16], "ocf", T.ngf[:, 0:n16], "ngf", [[0, n16]], A.is_gt, rk, -1)
-        aff(f[0:64, OMB:OMB + n16], "ocf", T.ngf[:, 0:n16], "ngf", [[0, n16]], A.is_ge, -rk, 1)
-        aff(f[0:64, OMA + n16:OMA + n16 + 1], "ocf", T.onf[0:64, 0:1], "onf", [[0, 1]], A.is_equal, -rk, 1)
-        aff(f[0:64, OMB + n16:OMB + n16 + 1], "ocf", T.ngf[:, 0:1], "ngf", [[0, 1]], A.is_equal, -rk, 1)
-        aff(f[64:128, OCL:OCL + n16], "ocf", T.onf[64:128, 0:n16], "onf", [[0, n16]], A.is_equal, -32, 1)
-        iota(f[64:65, OCL:OCL + n16], "ocf", [[0, len(dest)], [16, 16]], 0, 0)
-        iota(f[96:97, OLQ:OLQ + 128], "ocf", [[0, 8], [1, 16]], 0, 0)
+        vset("oneb", T.oneb[:], 1.0)
+        for i, (v, s, cmp) in enumerate(((rk, -1.0, A.is_lt), (rk, -1.0, A.is_ge), (96, 1.0, A.is_equal))):
+            op("v", "ts", ["pint"], ["cab"], T.cab[:, i:i + 1], T.pint[:, 0:1], float(v), s, cmp, A.mult, acc=True)
+        op("v", "set", ["ocf"], ["olq"], f[:, OLQ:OLQ + 128], 1.0)
+        op("v", "ts", ["ocf", "cab", "oneb"], ["ocl"], f[64:128, OCL:OCL + n16], T.oneb[64:128, 0:n16], T.cab[64:128, 2:3], None, A.mult)
+        iota(f[64:65, OCL:OCL + n16], "ocl", [[0, len(dest)], [16, 16]], 0, 0)
+        iota(f[96:97, OLQ:OLQ + 128], "olq", [[0, 8], [1, 16]], 0, 0)
+        for i, c in enumerate((OMA, OMB)):
+            op("v", "ts", ["ocf", "cab", "oneb"], ["om%d" % i], f[0:64, c:c + n16], T.oneb[0:64, 0:n16], T.cab[0:64, i:i + 1], None, A.mult)
+            op("v", "ts", ["ocf", "pint"], ["om%d" % i], f[0:64, c + n16:c + n16 + 1], T.pint[0:64, 0:1], float(rk), 1.0 - 2 * i, A.is_equal, A.mult, acc=True)
+        op("v", "set", ["ocf"], ["opb"], f[0:64, OPB + 2:OPB + 66], 1.0)
         for j, d in enumerate(dest):
-            vset("ocf", f[32:33, OMA + 16 * j:OMA + 16 * j + 16], float(TC * d))
-        op("v", "copy", ["ocf"], ["oc"], T.oc[:], f[:])
+            op("v", "set", ["om0"], ["om2"], f[32:33, OMA + 16 * j:OMA + 16 * j + 16], float(TC * d), acc=True)
+        op("v", "copy", ["om0", "om1", "om2", "opb", "ocl", "olq"], ["oc"], T.oc[:], f[:])
 
     def list_constants(part):
         f = T.lcf
@@ -248,6 +249,7 @@ def rank_program(g, core, T, topo):
         op("v", "ts", ["lcf"], ["lcf"], both, both, -1.0, None, A.mult)
         op("v", "copy", ["lcf"], ["lc"], T.lc[:, 0:LIP], f[:, 0:LIP])
 
+    iota(T.pint[:, 0:1], "pint", [[0, 1]], 0, 1, small=False)
     if core in consts:
         i = consts.index(core)
         if i == 0:
@@ -268,7 +270,7 @@ def rank_program(g, core, T, topo):
     cds = P["cnts"][core]
     half = (len(cds) + 1) // 2
     cnt_trs = [(ds, T.cd[rk], T.cd[rk], eng_off[i * CW:(i + 1) * CW], "call") for i, ds in enumerate([cds[:half], cds[half:]]) if ds]
-    xh = [T.xb[:, 1024 * h:1024 * h + 1024] for h in (0, 1)]
+    xq = [T.xb[:, 512 * i:512 * i + 512] for i in range(4)]
     xw = len(eng_all) // 2
 
     upto, below, below2 = T.oc[0:33, OPB + 2:OPB + 66], T.oc[0:16, OPB + 1:OPB + 65], T.oc[0:16, OPB:OPB + 64]
@@ -289,7 +291,7 @@ def rank_program(g, core, T, topo):
     xs_parts = []
 
     def sort_x(q, a, b):
-        r = ["x0", "x1"] + ["perm%d" % h for h in (0, 1) if a < 1024 * (h + 1) and b > 1024 * h]
+        r = XQ + ["perm%d" % h for h in (0, 1) if a < 1024 * (h + 1) and b > 1024 * h]
         out, src = T.xs[:, a:b], T.xb[:].indirect(T.plist[:, a // 16:b // 16])
         xs_parts.append("xs%d" % a)
         if q == "v":
@@ -305,7 +307,7 @@ def rank_program(g, core, T, topo):
         else:
             op("s", "act", r, [key], out, src, F.Copy)
 
-    def inverse_constants():
+    def inverse_numbers():
         iota(T.jlo[:], "jlo", [[1, 16]], 0, 1)
         iota(T.jhi[:], "jhi", [[128, 8], [1024, 2]], 0, 0)
         op("v", "ts", ["pint"], ["pint2"], T.pint[:, 2:3], T.pint[:, 0:1], 15, None, A.bitwise_and)
@@ -315,6 +317,8 @@ def rank_program(g, core, T, topo):
         op("v", "ts", ["jhi", "pm1"], ["jhi"], T.jhi[:], T.jhi[:], T.pm[:, 1:2], None, A.mult)
         for i in range(16):
             op("s", "act", ["jlo", "jhi"], ["jv"], T.jv[:, 16 * i:16 * i + 16], T.jlo[:], F.Identity, T.jhi[:, i:i + 1], acc=True)
+
+    def inverse_window():
         vset("one9", T.one9[:], 1.0)
         vset("zb", T.zb[:], 0.0)
         op("v", "ts", ["one9", "pm2"], ["zb"], T.zb[:, 0::16], T.one9[:], T.pm[:, 2:3], None, A.mult)
@@ -329,18 +333,19 @@ def rank_program(g, core, T, topo):
             mm(["zb", "win"], key, ps[:, 0:64], T.zb[:, 16 - q:144 - q], T.win[:, 1024 * h + q:1024 * h + 1024:16], q == 0, q == 15)
         op("v", "copy", [key], ["perm%d" % h], T.plist[:, 64 * h:64 * h + 64], ps[:, 0:64])
 
-    iota(T.pint[:, 0:1], "pint", [[0, 1]], 0, 1, small=False)
     if not isR:
-        h = senders.index(core) // 2
-        partner = [c for c in senders if c != core and topo.die(c) == topo.die(core)][0]
+        qn = senders.index(core)
+        others = [c for c in senders if c != core]
+        pass_eng = [eng_all[2 * CW + i::3] for i in range(3)]
         vset("xpad", T.xs[:, TC:], 0.0)
-        inverse_constants()
+        inverse_numbers()
         offset_constants(dest)
-        arrive("xh0", xw, ["x0"])
-        arrive("xh1", xw, ["x1"])
+        inverse_window()
+        for i in range(4):
+            arrive("xq%d" % i, xw if i == qn else len(pass_eng[0]), ["x%d" % i])
         arrive("cown", len(chip_eng), ["cdown"])
         arrive("soar", len(eng_all), ["so"])
-        fused(["x%d" % h], [([partner], xh[h], xh[h], eng_all[xw:], "xh%d" % h)])
+        fused(["x%d" % qn], [([c], xq[qn], xq[qn], es, "xq%d" % qn) for c, es in zip(others, pass_eng)])
         fused(["cdown"], cnt_trs)
         load_counts()
         scatter()
@@ -360,53 +365,53 @@ def rank_program(g, core, T, topo):
         finish()
         return
 
-    dma("s", "dkt0", [], ["kt0"], T.kt[0:4, :], T.key[:, 0:64])
-    dma("y", "dkt1", [], ["kt1"], T.kt[4:8, :], T.key[:, 64:128])
-    dma("y", "dx0", [], ["x0"], T.xb[:, 0:1024], T.x[:, 0:1024])
-    dma("y", "dx1", [], ["x1"], T.xb[:, 1024:2048], T.x[:, 1024:2048])
+    dma("s", "dkt0", [], ["kt0"], T.kt[0:8, :], T.key[:, 0:64])
+    dma("y", "dkt1", [], ["kt1"], T.kt[8:16, :], T.key[:, 64:128])
+    dma("y", "dx0", [], XQ[0:2], T.xb[:, 0:1024], T.x[:, 0:1024])
+    dma("s", "dx1", [], XQ[2:4], T.xb[:, 1024:2048], T.x[:, 1024:2048])
     iota(T.i65[:], "i65", [[1, 66]], 0, 0)
     for h in (0, 1):
-        fused(["x%d" % h], [([c], xh[h], xh[h], eng_all[i::2], "xh%d" % h) for i, c in enumerate(senders[2 * h:2 * h + 2])])
+        fused([XQ[2 * h]], [([senders[q]], xq[q], xq[q], eng_all[q % 2::2], "xq%d" % q) for q in (2 * h, 2 * h + 1)])
     vset("hs8", T.hs8[:, 0:64], 0.0)
-    vset("hs8", T.hs8[:, 64:128], 4.0)
+    vset("hs8", T.hs8[:, 64:128], 8.0)
     op("v", "ts", ["pint"], ["pint1"], T.pint[:, 1:2], T.pint[:, 0:1], 63, None, A.bitwise_and)
     op("v", "copy", ["pint1"], ["kcol"], T.kcol[:], T.pint[:, 1:2])
-    for a in range(4):
-        op("v", "ts", ["hs8", "kcol"], ["sel"], T.sel[:, 128 * a:128 * a + 128], T.hs8[:], float(a), T.kcol[0:8, :], A.add, A.is_equal, acc=True)
+    for a in range(8):
+        op("v", "ts", ["hs8", "kcol"], ["sel"], T.sel[:, 128 * a:128 * a + 128], T.hs8[:], float(a), T.kcol[0:16, :], A.add, A.is_equal, acc=True)
     for i, v in enumerate((A.is_lt, A.is_ge)):
         op("v", "ts", ["pint"], ["hmh"], T.hmh[:, i:i + 1], T.pint[:, 0:1], 64.0, None, v, acc=True)
     op("v", "copy", ["kt0", "kt1"], ["ktb"], T.ktb[:], T.kt[:])
     op("v", "ts", ["i65", "kcol"], ["w1"], T.w1[:], T.i65[:], T.kcol[:], None, A.is_gt)
     op("v", "ts", ["i65", "kcol"], ["w2"], T.w2[0:64, :], T.i65[0:64, 0:64], T.kcol[0:64, :], None, A.is_ge, acc=True)
     op("v", "ts", ["i65", "kcol"], ["w2"], T.w2[64:128, :], T.i65[64:128, 0:64], T.kcol[64:128, :], None, A.is_gt, acc=True)
-    for a in range(4):
-        kq = [T.p0, T.p1, T.p2, T.p3][a]
-        mm(["sel", "ktb"], "p%d" % a, kq[:, 0:256], T.sel[:, 128 * a:128 * a + 128], T.ktb[:])
-        for q in range(4):
-            op("v", "ts", ["p%d" % a, "kcol"], ["ot"], T.ot[:, 4 * a + q::16], kq[:, 64 * q:64 * q + 64], T.kcol[:], None, A.is_equal, acc=True)
+    for a in range(8):
+        kq = T["p%d" % a]
+        mm(["sel", "ktb"], "p%d" % a, kq[:, 0:128], T.sel[:, 128 * a:128 * a + 128], T.ktb[:])
+        for q in range(2):
+            op("v", "ts", ["p%d" % a, "kcol"], ["ot"], T.ot[:, 2 * a + q::16], kq[:, 64 * q:64 * q + 64], T.kcol[:], None, A.is_equal, acc=True)
     op("v", "scan", ["ot"], ["cp"], T.cp[:], T.ot[:], T.ot[:], 0.0, A.add, A.max)
     mm(["w1", "cp"], "p4", T.p4[0:2, 0:64], T.cp[:, 1022:1024], T.w1[:, 1:65])
     mm(["w1", "cp"], "p4", T.p4[0:64, 64:65], T.w1[:, 0:64], T.cp[:, 1023:1024])
     mm(["w2", "cp"], "p4", T.p4[64:128, 64:65], T.w2[:], T.cp[:, 1023:1024])
 
-    def masked(h):
-        sl = slice(512 * h, 512 * h + 512)
-        op("v", "scan", ["ot", "cp"], ["pr%d" % h], T.pr[:, sl], T.cp[:, sl], T.ot[:, sl], 0.0, A.max, A.mult)
+    def masked(i, a, c):
+        op("v", "scan", ["ot", "cp"], ["pr%d" % i], T.pr[:, a:c], T.cp[:, a:c], T.ot[:, a:c], 0.0, A.max, A.mult)
 
-    masked(0)
+    masked(0, 0, 256)
     op("v", "copy", ["p4"], ["cst"], T.cst[:], T.p4[0:2, 0:64])
     op("v", "ts", ["hmh", "p4"], ["ls"], T.ls[:], T.hmh[:], T.p4[:, 64:65], None, A.mult)
-    masked(1)
+    masked(1, 256, 1024)
     dma("y", "dcs", ["cst"], ["cdown"], T.cd[rk], T.cst[:])
     for b in range(8):
         sl = slice(128 * b, 128 * b + 128)
         mm(["ot", "ls"], "p5", T.p5[:, 2 * b:2 * b + 2], T.ot[:, sl], T.ls[:], True, False)
-        mm(["pr%d" % (b // 4), "hmh"], "p5", T.p5[:, 2 * b:2 * b + 2], T.pr[:, sl], T.hmh[:], False, True)
+        mm(["pr%d" % min(b // 2, 1), "hmh"], "p5", T.p5[:, 2 * b:2 * b + 2], T.pr[:, sl], T.hmh[:], False, True)
     op("v", "ts", ["p5"], ["so"], T.so[:], T.p5[:, 0:16], -1.0, None, A.add)
     fused(["so"], [(senders, T.so[:], T.so[:], eng_all, "soar")])
     fused(["cdown"], [(senders, T.cd[rk], T.cd[rk], chip_eng, "cown")] + cnt_trs)
     vset("xpad", T.xs[:, TC:], 0.0)
-    inverse_constants()
+    inverse_numbers()
+    inverse_window()
     scatter()
     for h in (0, 1):
         inverse(h)

from concourse.bass import DstId, RemoteDMATransfer
from concourse.mybir import AluOpType as A, AxisListType, ActivationFunctionType as F

N, TC, KB, CAP = 16, 2048, 64, 256
NMAX = 4
NCORES = 128
F32, BF, FH, I32, U16 = "float32", "bfloat16", "float16", "int32", "uint16"
OMA, OMB, OCL, OLQ, OPB, OCW = 0, 66, 132, 196, 324, 390
LHS, LTR, LIP, LIQ, LIC, LCW = 56, 192, 576, 704, 832, 962
SCRATCH = {"cd": ("dram", [N, 128, 1], FH)}
for _n, _p, _w, _d in (
        ("xb", 128, TC, BF), ("xs", 128, TC + CAP, BF), ("msg", 128, NMAX * CAP, BF), ("rcv", 128, N * CAP, BF),
        ("yb", 128, TC, BF), ("plist", 128, 128, U16), ("off", 128, 16 * NMAX, U16), ("yoff", 128, 128, U16),
        ("ocf", 128, OCW, BF), ("oc", 128, OCW, FH), ("oneb", 128, 64, BF), ("cab", 128, 3, F32),
        ("lcf", 128, LCW, F32), ("lc", 128, LCW, FH), ("onf", 128, 128, F32),
        ("kt", 16, 128, I32), ("ktb", 16, 128, BF), ("hs8", 16, 128, BF), ("sel", 16, 1024, BF), ("kcol", 128, 1, F32),
        ("i65", 128, 66, BF), ("w1", 128, 66, FH), ("w2", 128, 64, FH), ("cst", 2, 64, FH), ("hmh", 128, 2, FH),
        ("ot", 128, 1024, FH), ("cp", 128, 1024, FH), ("pr", 128, 1024, FH), ("ls", 128, 2, FH), ("so", 128, 16, U16),
        ("win", 128, TC, BF), ("one9", 128, 9, F32), ("jlo", 128, 16, BF), ("jhi", 128, 16, F32), ("jv", 128, 256, BF),
        ("zb", 128, 144, BF), ("pint", 128, 3, I32), ("pm", 128, 3, F32),
        ("sc", 128, 10, FH), ("sci", 128, 16, I32), ("hif", 128, 8, F32), ("aa", 128, 2048, FH), ("zz", 128, 1088, FH)):
    SCRATCH[_n] = ("sbuf", [_p, _w], _d)
for _i in range(8):
    SCRATCH["p%d" % _i] = ("psum", [128, 512], F32)
SEMAPHORES = ["sv", "st", "ss", "sg", "lsnd", "cown", "call", "xq0", "xq1", "xq2", "xq3", "soar", "kc0", "kc1", "kc2",
              "data", "dkt0", "dkt1", "dx0", "dx1", "dcs", "dcb", "dy0", "dy1", "dy2"]
CW = 2
SLOT = [2 * r + 1 if r < N // 2 else 2 * (N - 1 - r) for r in range(N)]
YPART = [0, 1024, 1536, 2048]
XQ = ["x0", "x1", "x2", "x3"]
_PLAN = {}


def make_plan(cores, topo):
    if _PLAN:
        return _PLAN
    chip_rank = {topo.chip(c): r for r, c in enumerate(cores)}
    chips = sorted(chip_rank)
    owners, senders, consts = {}, {}, {}
    for ch in chips:
        far = [c for c in cores if topo.mates(ch, topo.chip(c))][0]
        R = cores[chip_rank[ch]]
        here = [c for c in range(NCORES) if topo.chip(c) == ch and c != R]
        here.sort(key=lambda c: topo.die(c) != topo.die(R))
        own = [c for c in here if topo.may_write(c, far)]
        rest = [c for c in here if c not in own]
        near = [c for c in own if topo.die(c) == topo.die(R)]
        if topo.may_write(R, far):
            near.append(rest.pop(0))
        senders[ch] = [c for p in zip(near, [c for c in own if c not in near]) for c in p]
        owners[ch] = [c for c in senders[ch] if c in own]
        consts[ch] = rest[:3]
    pair_of = {}
    for ch in chips:
        if ch not in pair_of:
            k = len(pair_of) // 2
            for c2 in chips:
                if c2 == ch or topo.mates(ch, c2):
                    pair_of[c2] = k
    np_ = len(chips) // 2
    msgs, cnts = {}, {}
    for ch in chips:
        R = cores[chip_rank[ch]]
        for c in senders[ch] + [R]:
            msgs[c], cnts[c] = [], []

        def deal(d, die, who):
            who = [c for c in who if topo.die(c) == die]
            msgs[min(who, key=lambda c: len(msgs[c]))].append(d)
        turn = [cores[(chip_rank[ch] + i) % N] for i in range(1, N)]
        for d in turn:
            if not topo.same_plane(ch, topo.chip(d)):
                deal(d, 1 if (pair_of[ch] + pair_of[topo.chip(d)]) % np_ < np_ // 2 else 0, owners[ch])
        for d in turn:
            if topo.same_plane(ch, topo.chip(d)):
                deal(d, 0 if (pair_of[ch] + pair_of[topo.chip(d)]) % np_ < np_ // 2 else 1, senders[ch])
        dst = [d for c2 in chips if c2 != ch for d in senders[c2] + [cores[chip_rank[c2]]]]
        for d in sorted(dst, key=lambda d: topo.same_plane(ch, topo.chip(d))):
            who = [c for c in senders[ch] + [R] if topo.may_write(c, d)]
            cnts[min(who, key=lambda c: len(cnts[c]))].append(d)
    _PLAN.update(dict(rank=chip_rank, senders=senders, consts=consts, msgs=msgs, cnts=cnts))
    return _PLAN


def engines(mask):
    return [1 << e for e in range(16) if mask >> e & 1]


def calls_of(m, eng):
    out = []
    for i in range(0, len(m), 2):
        part = list(range(i, min(i + 2, len(m))))
        w = len(eng) // len(part)
        out.append([(j, sum(eng[k * w:(k + 1) * w]), w) for k, j in enumerate(part)])
    return out


def rank_program(g, core, T, topo):
    cores = list(T.cores)
    P = make_plan(cores, topo)
    ch = topo.chip(core)
    if ch not in P["rank"]:
        return
    rk = P["rank"][ch]
    R = cores[rk]
    isR = core == R
    senders, consts = P["senders"][ch], P["consts"][ch]
    if not isR and core not in senders and core not in consts:
        return
    far = [c for c in cores if topo.same_plane(ch, topo.chip(c))][0]
    eng_off = engines(topo.mask(core, far))
    eng_all = engines(topo.mask(core, R if not isR else senders[0]))
    Q = {"v": g.vector, "t": g.tensor, "s": g.scalar, "g": g, "y": g.sync}
    cnt, seen, last, readers, totals = {}, {}, {}, {}, {}

    def wait(q, tok):
        if seen.get((q, tok[0]), 0) < tok[1]:
            Q[q].wait_ge(T.sem[tok[0]], tok[1])
            seen[(q, tok[0])] = tok[1]

    def deps(q, r, w, acc=False):
        own = "s" + q
        for k in r:
            if k in last:
                wait(q, last[k])
        for k in w:
            if k in last and not (acc and last[k][0] == own):
                wait(q, last[k])
            for t in readers.get(k, []):
                if t[0] != own:
                    wait(q, t)

    def note(tok, r, w):
        for k in r:
            readers.setdefault(k, []).append(tok)
        for k in w:
            last[k] = tok
            readers[k] = []

    def op(q, name, r, w, *args, acc=False, **kw):
        s = "s" + q
        if q == "g" and s in cnt:
            wait(q, (s, cnt[s]))
        deps(q, r, w, acc)
        f = {"copy": lambda: Q[q].tensor_copy(*args), "tt": lambda: Q[q].tensor_tensor(*args),
             "ts": lambda: Q[q].tensor_scalar(*args), "scan": lambda: Q[q].tensor_tensor_scan(*args),
             "set": lambda: Q[q].memset(*args), "mm": lambda: Q[q].matmul(*args),
             "act": lambda: Q[q].activation(*args), "iota": lambda: Q[q].iota(*args, **kw),
             "aff": lambda: Q[q].affine_select(*args)}[name]
        ins = f()
        cnt[s] = cnt.get(s, 0) + 1
        ins.then_inc(T.sem[s], 1)
        totals[s] = cnt[s]
        note((s, cnt[s]), r, w)

    def iota(out, w, pat, base, cm, small=True):
        if small:
            op("g", "iota", [], [w], out, pat, base, cm, allow_small_or_imprecise_dtypes=True)
        else:
            op("g", "iota", [], [w], out, pat, base, cm)

    def aff(out, w, src, rs, pat, cmp, base, cm):
        op("g", "aff", [rs], [w], out, src, pat, cmp, 0.0, base, cm)

    def vset(w, ap, value):
        op("v", "set", [], [w], ap, value)

    def dma(q, sem, r, w, out, in_):
        deps(q, r, w)
        Q[q].dma_start(out, in_).then_inc(T.sem[sem], 16)
        totals[sem] = 16
        note((sem, 16), r, w)

    def arrive(sem, n, w):
        totals[sem] = n
        note((sem, n), [], w)

    def dst_id(d):
        a = topo.addr(d)
        return DstId(rid=a[0], pnc=a[1])

    nsent = [0]

    def fused(r, trs):
        deps("g", r, [])
        g.remote_dma_fused([RemoteDMATransfer(dst_ids=[dst_id(d) for d in ds], dma_engine_mask=sum(es), remote_sem=T.sem[sem],
                                              srcs=[src], dsts=[dst for d in ds]) for ds, src, dst, es, sem in trs],
                           local_sem=T.sem.lsnd)
        nsent[0] += sum(len(t[3]) for t in trs)
        totals["lsnd"] = nsent[0]

    def mm(r, w, out, l, rh, start=True, stop=True):
        op("t", "mm", r, [w], out, l, rh, start, stop, acc=True)

    def finish():
        for s in sorted(totals):
            wait("g", (s, totals[s]))

    def offset_constants(dest):
        n16 = 16 * len(dest)
        f = T.ocf
        vset("ocf", f[:], 0.0)
        vset("oneb", T.oneb[:], 1.0)
        for i, (v, s, cmp) in enumerate(((rk, -1.0, A.is_lt), (rk, -1.0, A.is_ge), (96, 1.0, A.is_equal))):
            op("v", "ts", ["pint"], ["cab"], T.cab[:, i:i + 1], T.pint[:, 0:1], float(v), s, cmp, A.mult, acc=True)
        op("v", "set", ["ocf"], ["olq"], f[:, OLQ:OLQ + 128], 1.0)
        op("v", "ts", ["ocf", "cab", "oneb"], ["ocl"], f[64:128, OCL:OCL + n16], T.oneb[64:128, 0:n16], T.cab[64:128, 2:3], None, A.mult)
        iota(f[64:65, OCL:OCL + n16], "ocl", [[0, len(dest)], [16, 16]], 0, 0)
        iota(f[96:97, OLQ:OLQ + 128], "olq", [[0, 8], [1, 16]], 0, 0)
        for i, c in enumerate((OMA, OMB)):
            op("v", "ts", ["ocf", "cab", "oneb"], ["om%d" % i], f[0:64, c:c + n16], T.oneb[0:64, 0:n16], T.cab[0:64, i:i + 1], None, A.mult)
            op("v", "ts", ["ocf", "pint"], ["om%d" % i], f[0:64, c + n16:c + n16 + 1], T.pint[0:64, 0:1], float(rk), 1.0 - 2 * i, A.is_equal, A.mult, acc=True)
        op("v", "set", ["ocf"], ["opb"], f[0:64, OPB + 2:OPB + 66], 1.0)
        for j, d in enumerate(dest):
            op("v", "set", ["om0"], ["om2"], f[32:33, OMA + 16 * j:OMA + 16 * j + 16], float(TC * d), acc=True)
        op("v", "copy", ["om0", "om1", "om2", "opb", "ocl", "olq"], ["oc"], T.oc[:], f[:])

    def list_constants(part):
        f = T.lcf
        vset("onf", T.onf[:], 1.0)
        if part == 1:
            vset("lcf", f[:, LIP:LCW], 0.0)
            aff(f[64:128, LIP:LIP + 128], "lcf", T.onf[64:128, :], "onf", [[0, 128]], A.is_equal, -32, 1)
            iota(f[64:65, LIP:LIP + 128], "lcf", [[16, 128]], 0, 0)
            iota(f[:, LIQ:LIQ + 128], "lcf", [[0, 8], [1, 16]], 0, 0)
            iota(f[:, LIC:LIC + 129], "lcf", [[16, 129]], 0, 0)
            op("v", "copy", ["lcf"], ["lc"], T.lc[:, LIP:LCW], f[:, LIP:LCW])
            return
        vset("lcf", f[:, 0:LIP], 0.0)
        for i, cmp in enumerate((A.is_gt, A.is_ge)):
            for h in (0, 1):
                p, c = slice(64 * h, 64 * h + 64), LTR + 128 * i + 64 * h
                aff(f[p, c:c + 64], "lcf", T.onf[p, 0:64], "onf", [[1, 64]], cmp, 0, -1)
        for h in (0, 1):
            r0 = 8 * h - 1
            aff(f[0:64, 10 * h:10 * h + 10], "lcf", T.onf[0:64, 0:10], "onf", [[1, 10]], A.is_gt, r0, -1)
            aff(f[0:64, 20 + 10 * h:30 + 10 * h], "lcf", T.onf[0:64, 0:10], "onf", [[-1, 10]], A.is_ge, -r0, 1)
        aff(f[0:16, 20:21], "lcf", T.onf[0:16, 0:1], "onf", [[0, 1]], A.is_ge, N - 2, -1)
        aff(f[0:64, 40:50], "lcf", T.onf[0:64, 0:10], "onf", [[1, 10]], A.is_equal, N - 1, -1)
        for h in (0, 1):
            c = LHS + 8 + 64 * h
            aff(f[0:64, c:c + 64], "lcf", T.onf[0:64, 0:64], "onf", [[0, 64]], A.is_equal, -32 * h, 1)
        vset("lcf", f[32:33, 0:50], -float(TC * rk))
        for h, p in ((0, slice(0, 64)), (1, slice(32, 33))):
            vset("lcf", f[p, LHS:LHS + 1], float(CAP * (SLOT[8 * h] - SLOT[8 * h - 1])))
            vset("lcf", f[p, LHS + 1:LHS + 8], float(CAP * (SLOT[8 * h + 1] - SLOT[8 * h])))
        both = f[:, LTR + 256:LTR + 384]
        op("v", "tt", ["lcf"], ["lcf"], both, f[:, LTR:LTR + 128], f[:, LTR + 128:LTR + 256], A.add)
        op("v", "ts", ["lcf"], ["lcf"], both, both, -1.0, None, A.mult)
        op("v", "copy", ["lcf"], ["lc"], T.lc[:, 0:LIP], f[:, 0:LIP])

    iota(T.pint[:, 0:1], "pint", [[0, 1]], 0, 1, small=False)
    if core in consts:
        i = consts.index(core)
        if i == 0:
            offset_constants([rk])
            part = T.oc[:]
        else:
            list_constants(i - 1)
            part = T.lc[:, 0:LIP] if i == 1 else T.lc[:, LIP:LCW]
        fused(["lc" if i else "oc"], [([R], part, part, eng_all[:4], "kc%d" % i)])
        finish()
        return

    mine = P["msgs"][core]
    dest = [rk] if isR else [cores.index(d) for d in mine]
    nd = len(dest)
    n16 = 16 * nd
    chip_eng = eng_off[2 * CW:4 * CW]
    cds = P["cnts"][core]
    half = (len(cds) + 1) // 2
    cnt_trs = [(ds, T.cd[rk], T.cd[rk], eng_off[i * CW:(i + 1) * CW], "call") for i, ds in enumerate([cds[:half], cds[half:]]) if ds]
    xq = [T.xb[:, 512 * i:512 * i + 512] for i in range(4)]
    xw = len(eng_all) // 2

    upto, below, below2 = T.oc[0:33, OPB + 2:OPB + 66], T.oc[0:16, OPB + 1:OPB + 65], T.oc[0:16, OPB:OPB + 64]

    def load_counts():
        arrive("call", 15 * CW, ["cd"])
        dma("y", "dcb", ["cd", "cdown", "oc"], ["cb"], T.oc[0:16, OPB + 2:OPB + 66], T.cd[:, 64:128, 0])

    def places():
        mm(["cb", "oc"], "p0", T.p0[0:64, 0:n16 + 1], upto, T.oc[0:33, OMA:OMA + n16 + 1], True, False)
        mm(["cb", "oc"], "p0", T.p0[0:64, 0:n16 + 1], below, T.oc[0:16, OMB:OMB + n16 + 1], False, True)
        op("v", "ts", ["p0"], ["cl"], T.oc[0:64, OCL:OCL + n16], T.p0[0:64, 0:n16], 0.0, T.p0[0:64, n16:n16 + 1], A.max, A.min)

    def starts():
        mm(["oc", "cl"], "p1", T.p1[:, 0:n16], T.oc[:, OLQ:OLQ + 128], T.oc[:, OCL:OCL + n16])
        op("v", "copy", ["p1"], ["off"], T.off[:, 0:n16], T.p1[:, 0:n16])

    xs_parts = []

    def sort_x(q, a, b):
        r = XQ + ["perm%d" % h for h in (0, 1) if a < 1024 * (h + 1) and b > 1024 * h]
        out, src = T.xs[:, a:b], T.xb[:].indirect(T.plist[:, a // 16:b // 16])
        xs_parts.append("xs%d" % a)
        if q == "v":
            op("v", "copy", r, ["xs%d" % a], out, src)
        else:
            op("s", "act", r, ["xs%d" % a], out, src, F.Copy)

    def gather(q, out, key, j):
        src = T.xs[:].indirect(T.off[:, 16 * j:16 * j + 16])
        r = xs_parts + ["xpad", "off"]
        if q == "v":
            op("v", "copy", r, [key], out, src)
        else:
            op("s", "act", r, [key], out, src, F.Copy)

    def inverse_numbers():
        iota(T.jlo[:], "jlo", [[1, 16]], 0, 1)
        iota(T.jhi[:], "jhi", [[128, 8], [1024, 2]], 0, 0)
        op("v", "ts", ["pint"], ["pint2"], T.pint[:, 2:3], T.pint[:, 0:1], 15, None, A.bitwise_and)
        for i, (v, cmp) in enumerate(((0.0, A.is_equal), (1.0, A.is_equal), (2.0, A.is_lt))):
            op("v", "ts", ["pint2"], ["pm%d" % i], T.pm[:, i:i + 1], T.pint[:, 2:3], v, None, cmp)
        op("v", "ts", ["jlo", "pm0"], ["jlo"], T.jlo[:], T.jlo[:], T.pm[:, 0:1], None, A.mult)
        op("v", "ts", ["jhi", "pm1"], ["jhi"], T.jhi[:], T.jhi[:], T.pm[:, 1:2], None, A.mult)
        for i in range(16):
            op("s", "act", ["jlo", "jhi"], ["jv"], T.jv[:, 16 * i:16 * i + 16], T.jlo[:], F.Identity, T.jhi[:, i:i + 1], acc=True)

    def inverse_window():
        vset("one9", T.one9[:], 1.0)
        vset("zb", T.zb[:], 0.0)
        op("v", "ts", ["one9", "pm2"], ["zb"], T.zb[:, 0::16], T.one9[:], T.pm[:, 2:3], None, A.mult)
        vset("win", T.win[:], 0.0)

    def scatter():
        op("v", "copy", ["so", "jv"], ["win"], T.win[:].indirect(T.so[:]), T.jv[:])

    def inverse(h):
        key, ps = (("p6", T.p6), ("p7", T.p7))[h]
        for q in range(16):
            mm(["zb", "win"], key, ps[:, 0:64], T.zb[:, 16 - q:144 - q], T.win[:, 1024 * h + q:1024 * h + 1024:16], q == 0, q == 15)
        op("v", "copy", [key], ["perm%d" % h], T.plist[:, 64 * h:64 * h + 64], ps[:, 0:64])

    if not isR:
        qn = senders.index(core)
        others = [c for c in senders if c != core]
        pass_eng = [eng_all[2 * CW + i::3] for i in range(3)]
        vset("xpad", T.xs[:, TC:], 0.0)
        inverse_numbers()
        offset_constants(dest)
        inverse_window()
        for i in range(4):
            arrive("xq%d" % i, xw if i == qn else len(pass_eng[0]), ["x%d" % i])
        arrive("cown", len(chip_eng), ["cdown"])
        arrive("soar", len(eng_all), ["so"])
        fused(["x%d" % qn], [([c], xq[qn], xq[qn], es, "xq%d" % qn) for c, es in zip(others, pass_eng)])
        fused(["cdown"], cnt_trs)
        load_counts()
        scatter()
        inverse(0)
        sort_x("v", 0, 512)
        sort_x("s", 512, 1024)
        inverse(1)
        sort_x("s", 1024, 1536)
        places()
        sort_x("v", 1536, TC)
        starts()
        for call in calls_of(mine, eng_off):
            for j, m, n in call:
                gather("v" if j % 2 == 0 else "s", T.msg[:, CAP * j:CAP * j + CAP], "m%d" % j, j)
            fused(["m%d" % j for j, m, n in call],
                  [([mine[j]], T.msg[:, CAP * j:CAP * j + CAP], T.rcv[:, CAP * SLOT[rk]:CAP * SLOT[rk] + CAP], engines(m), "data") for j, m, n in call])
        finish()
        return

    dma("s", "dkt0", [], ["kt0"], T.kt[0:8, :], T.key[:, 0:64])
    dma("y", "dkt1", [], ["kt1"], T.kt[8:16, :], T.key[:, 64:128])
    dma("y", "dx0", [], XQ[0:2], T.xb[:, 0:1024], T.x[:, 0:1024])
    dma("s", "dx1", [], XQ[2:4], T.xb[:, 1024:2048], T.x[:, 1024:2048])
    iota(T.i65[:], "i65", [[1, 66]], 0, 0)
    for h in (0, 1):
        fused([XQ[2 * h]], [([senders[q]], xq[q], xq[q], eng_all[q % 2::2], "xq%d" % q) for q in (2 * h, 2 * h + 1)])
    vset("hs8", T.hs8[:, 0:64], 0.0)
    vset("hs8", T.hs8[:, 64:128], 8.0)
    op("v", "ts", ["pint"], ["pint1"], T.pint[:, 1:2], T.pint[:, 0:1], 63, None, A.bitwise_and)
    op("v", "copy", ["pint1"], ["kcol"], T.kcol[:], T.pint[:, 1:2])
    for a in range(8):
        op("v", "ts", ["hs8", "kcol"], ["sel"], T.sel[:, 128 * a:128 * a + 128], T.hs8[:], float(a), T.kcol[0:16, :], A.add, A.is_equal, acc=True)
    for i, v in enumerate((A.is_lt, A.is_ge)):
        op("v", "ts", ["pint"], ["hmh"], T.hmh[:, i:i + 1], T.pint[:, 0:1], 64.0, None, v, acc=True)
    op("v", "copy", ["kt0", "kt1"], ["ktb"], T.ktb[:], T.kt[:])
    op("v", "ts", ["i65", "kcol"], ["w1"], T.w1[:], T.i65[:], T.kcol[:], None, A.is_gt)
    op("v", "ts", ["i65", "kcol"], ["w2"], T.w2[0:64, :], T.i65[0:64, 0:64], T.kcol[0:64, :], None, A.is_ge, acc=True)
    op("v", "ts", ["i65", "kcol"], ["w2"], T.w2[64:128, :], T.i65[64:128, 0:64], T.kcol[64:128, :], None, A.is_gt, acc=True)
    for a in range(8):
        kq = T["p%d" % a]
        mm(["sel", "ktb"], "p%d" % a, kq[:, 0:128], T.sel[:, 128 * a:128 * a + 128], T.ktb[:])
        for q in range(2):
            op("v", "ts", ["p%d" % a, "kcol"], ["ot"], T.ot[:, 2 * a + q::16], kq[:, 64 * q:64 * q + 64], T.kcol[:], None, A.is_equal, acc=True)
    op("v", "scan", ["ot"], ["cp"], T.cp[:], T.ot[:], T.ot[:], 0.0, A.add, A.max)
    mm(["w1", "cp"], "p4", T.p4[0:2, 0:64], T.cp[:, 1022:1024], T.w1[:, 1:65])
    mm(["w1", "cp"], "p4", T.p4[0:64, 64:65], T.w1[:, 0:64], T.cp[:, 1023:1024])
    mm(["w2", "cp"], "p4", T.p4[64:128, 64:65], T.w2[:], T.cp[:, 1023:1024])

    def masked(i, a, c):
        op("v", "scan", ["ot", "cp"], ["pr%d" % i], T.pr[:, a:c], T.cp[:, a:c], T.ot[:, a:c], 0.0, A.max, A.mult)

    masked(0, 0, 256)
    op("v", "copy", ["p4"], ["cst"], T.cst[:], T.p4[0:2, 0:64])
    op("v", "ts", ["hmh", "p4"], ["ls"], T.ls[:], T.hmh[:], T.p4[:, 64:65], None, A.mult)
    masked(1, 256, 1024)
    dma("y", "dcs", ["cst"], ["cdown"], T.cd[rk], T.cst[:])
    for b in range(8):
        sl = slice(128 * b, 128 * b + 128)
        mm(["ot", "ls"], "p5", T.p5[:, 2 * b:2 * b + 2], T.ot[:, sl], T.ls[:], True, False)
        mm(["pr%d" % min(b // 2, 1), "hmh"], "p5", T.p5[:, 2 * b:2 * b + 2], T.pr[:, sl], T.hmh[:], False, True)
    op("v", "ts", ["p5"], ["so"], T.so[:], T.p5[:, 0:16], -1.0, None, A.add)
    fused(["so"], [(senders, T.so[:], T.so[:], eng_all, "soar")])
    fused(["cdown"], [(senders, T.cd[rk], T.cd[rk], chip_eng, "cown")] + cnt_trs)
    vset("xpad", T.xs[:, TC:], 0.0)
    inverse_numbers()
    inverse_window()
    scatter()
    for h in (0, 1):
        inverse(h)
        sort_x("s", 1024 * h, 1024 * h + 1024)
    arrive("kc0", 4, ["oc"])
    arrive("kc1", 4, ["lc"])
    arrive("kc2", 4, ["lc2"])
    load_counts()
    places()
    starts()
    gather("s", T.rcv[:, CAP * SLOT[rk]:CAP * SLOT[rk] + CAP], "own", 0)
    lc = T.lc
    mm(["cb", "lc"], "p2", T.p2[0:64, 0:10], upto, lc[0:33, 0:10], True, False)
    mm(["cb", "lc"], "p2", T.p2[0:64, 0:10], below, lc[0:16, 20:30], False, False)
    mm(["cb", "lc"], "p2", T.p2[0:64, 0:10], below2, lc[0:16, 40:50], False, True)
    mm(["cb", "lc"], "p2", T.p2[64:128, 0:10], upto, lc[0:33, 10:20], True, False)
    mm(["cb", "lc"], "p2", T.p2[64:128, 0:10], below, lc[0:16, 30:40], False, True)
    op("v", "ts", ["p2"], ["sc"], T.sc[:], T.p2[:, 0:10], 0.0, float(TC), A.max, A.min)
    op("v", "ts", ["p2"], ["sci"], T.sci[:, 0:8], T.p2[:, 1:9], 0.0, float(TC), A.max, A.min)
    op("v", "ts", ["sci"], ["scm"], T.sci[:, 8:16], T.sci[:, 0:8], 2 * TC - 16, None, A.bitwise_and)
    op("v", "copy", ["scm"], ["hif"], T.hif[:], T.sci[:, 8:16])
    mm(["lc"], "p3", T.p3[:, 0:8], lc[0:33, LHS + 8:LHS + 136], lc[0:33, LHS:LHS + 8], True, False)
    mm(["lc", "sc"], "p3", T.p3[:, 0:8], lc[:, LTR:LTR + 128], T.sc[:, 2:10], False, False)
    mm(["lc", "sc"], "p3", T.p3[:, 0:8], lc[:, LTR + 128:LTR + 256], T.sc[:, 0:8], False, False)
    mm(["lc", "sc"], "p3", T.p3[:, 0:8], lc[:, LTR + 256:LTR + 384], T.sc[:, 1:9], False, True)
    mm(["oc", "lc2"], "p4", T.p4[:, 0:128], T.oc[64:128, OLQ:OLQ + 128], lc[64:128, LIP:LIP + 128], True, False)
    iq, ic = lc[:, LIQ:LIQ + 128], lc[:, LIC:LIC + 129]
    for i in range(8):
        a0, z0 = 256 * i, 136 * i
        na, ya, zi = T.aa[:, a0:a0 + 128], T.aa[:, a0 + 128:a0 + 256], T.zz[:, z0:z0 + 129]
        hi, pl, st = T.hif[:, i:i + 1], T.p2[:, 1 + i:2 + i], T.p3[:, i:i + 1]
        op("v", "ts", ["lc2", "hif", "p2"], ["na%d" % i], na, iq, hi, pl, A.add, A.is_lt)
        op("v", "ts", ["lc2", "hif", "p2"], ["ya%d" % i], ya, iq, hi, pl, A.add, A.is_ge)
        op("v", "ts", ["lc2", "hif", "p3"], ["zz%d" % i], zi, ic, hi, st, A.is_gt, A.mult)
        mm(["na%d" % i, "zz%d" % i], "p4", T.p4[:, 0:128], na, T.zz[:, z0:z0 + 128], False, False)
        mm(["ya%d" % i, "zz%d" % i], "p4", T.p4[:, 0:128], ya, T.zz[:, z0 + 1:z0 + 129], False, i == 7)
    op("v", "copy", ["p4"], ["yoff"], T.yoff[:], T.p4[:, 0:128])
    n_in = 0
    for c2 in P["msgs"]:
        if topo.chip(c2) != ch:
            for call in calls_of(P["msgs"][c2], engines(topo.mask(c2, R))):
                n_in += sum(n for j, m, n in call if P["msgs"][c2][j] == R)
    arrive("data", n_in, ["rcv"])
    yr = ["rcv", "own", "yoff"]
    for h in range(3):
        a, c = YPART[h], YPART[h + 1]
        b = (a + c) // 2
        op("v", "copy", yr, ["yl%d" % h], T.yb[:, a:b], T.rcv[:].indirect(T.yoff[:, a // 16:b // 16]))
        op("s", "act", yr, ["yr%d" % h], T.yb[:, b:c], T.rcv[:].indirect(T.yoff[:, b // 16:c // 16]), F.Copy)
        dma("y", "dy%d" % h, ["yl%d" % h, "yr%d" % h], ["yo%d" % h], T.y[:, a:c], T.yb[:, a:c])
    finish()
